import numpy as np, ml_dtypes
CORES = [9,25,41,57]
N = 4
BF = ml_dtypes.bfloat16
W, C, K, VISITS = 4096, 1024, 256, 5
LEV = np.arange(16).reshape(1, 1, 16, 1)
HC = 39 + 14 * LEV
UC = 5 + 10 * LEV
SIZES = np.array([1, 1, 2, 2, 3, 4, 6, 8, 16, 32, 64, 128, 256, 512, W, W]).reshape(1, 1, 16, 1)
def take(a, i):
    return np.take_along_axis(a, i, a.ndim - 1)
def cell(z):
    return (255 + np.add.reduce(HC * z, axis=2)) & (C - 1)
def first(keys):
    return np.unique(keys, return_index=True)[1]
def parts(rng, amp=12):
    pool = np.argsort(rng.random((8, 16, W)), axis=-1); pl = np.broadcast_to(pool[None], (N, 8, 16, W))
    fo = np.where(rng.random((N, 8, W)) < 0.6, np.arange(W), rng.integers(0, W, (N, 8, W)))
    la = take(pl, (rng.random((N, 8, 16, K)) * SIZES).astype(np.int64)); bk = take(pl, (rng.random((N, 8, 16, C)) * SIZES).astype(np.int64))
    cen = rng.integers(40, 216, (1, 8, 16, 1))
    far = rng.random((N, 8, 1, W)) < 0.06
    for q in range(N):
        for g in range(8):
            far[q, g, 0, fo[q, g, pool[g, :4, :2].reshape(-1)]] = False
    x = np.where(far, rng.integers(0, 256, (N, 8, 16, W)), cen + rng.integers(-amp, amp + 1, (N, 8, 16, W)))
    z = np.where(rng.random((N, 8, 1, K)) < 0.04, rng.integers(0, 256, (N, 8, 16, K)), cen + rng.integers(-amp, amp + 1, (N, 8, 16, K)))
    t = 235 - 4 * LEV + rng.integers(0, 4, (N, 8, 16, 1))
    c = cell(z); same = rng.random((N, 8, K)) < 0.15
    for q in range(N):
        for g in range(8):
            j = np.flatnonzero(same[q, g]); j = j[first(c[q, g, j])]
            bk[q, g][:, c[q, g, j]] = la[q, g][:, j]
    return x, fo, bk, la, z, t
def pack(x, fo, bk, la, z, t):
    return {"x": np.ascontiguousarray(x.reshape(N, 128, W)).astype(np.float32).astype(BF), "fw": np.ascontiguousarray(fo).astype(np.int32),
            "bk": np.ascontiguousarray(bk.reshape(N, 128, C)).astype(np.int32), "la": np.ascontiguousarray(la.reshape(N, 128, K)).astype(np.int32),
            "zz": np.ascontiguousarray(z.reshape(N, 128, K)).astype(np.float32).astype(BF), "th": np.ascontiguousarray(t.reshape(N, 128, 1)).astype(np.int32)}
def setup_inputs(rng):
    return pack(*parts(rng))
def setup_inputs_spread(rng):
    x = np.minimum((np.exp2(8 * rng.random((N, 8, 1, W))) * rng.random((N, 8, 16, W))).astype(np.int64), 255)
    z = np.minimum((np.exp2(8 * rng.random((N, 8, 1, K))) * rng.random((N, 8, 16, K))).astype(np.int64), 255)
    t = -np.sort(-np.minimum(np.exp2(12 * rng.random((N, 8, 16, 1))).astype(np.int64), 4080), axis=2)
    fo = rng.integers(0, W, (N, 8, W)); la = (W * rng.random((N, 8, 16, K)) ** 3).astype(np.int64); bk = (W * rng.random((N, 8, 16, C)) ** 3).astype(np.int64)
    return pack(x, fo, np.minimum(bk, W - 1), np.minimum(la, W - 1), z, t)
def setup_inputs_ends(rng):
    def both(n):
        k = rng.integers(0, 3, (N, 8, 1, n)); return np.where(k == 0, 0, np.where(k == 1, 255, 255 * rng.integers(0, 2, (N, 8, 16, n))))
    x, z = both(W), both(K)
    fo = (W - 1) * rng.integers(0, 2, (N, 8, W)); bk = (W - 1) * rng.integers(0, 2, (N, 8, 16, C)); la = (W - 1) * rng.integers(0, 2, (N, 8, 16, K))
    t = 4080 * (rng.random((N, 8, 16, 1)) < rng.choice(np.array([0.5, 0.8, 0.95]), (N, 8, 1, 1))).astype(np.int64)
    t[N - 1, 7] = 4080; t[:, 6] = 4080; t[:, 6, 15] = 0
    near = (255 * (16 - np.arange(16) // 2) - 1 + np.arange(16) % 2).reshape(16, 1)
    for g, o in ((3, 1), (5, -1)):
        z[:, g] = 255 * (np.argsort(rng.random((N, 16, K)), axis=1) < np.argsort(rng.random((N, 1, K)), axis=-1) % 17)
        t[:, g] = near[::o]
    x[:, 1::2, :, 0] = 0; x[:, 1::2, :, W - 1] = 255; fo[:, 1::2, 0] = 0; fo[:, 1::2, W - 1] = W - 1
    z[..., K - 1] = 0; la[..., K - 1] = W - 1; z[..., K - 2] = 255; la[..., K - 2] = 0
    bk[:, 1::2, :, 255] = 0; bk[:, 1::2, :, C - 1] = W - 1
    return pack(x, fo, bk, la, z, t)
def setup_inputs_corners(rng):
    x, fo, bk, la, z, t = parts(rng); a = np.arange(W)
    pat = [a, 0 * a, 0 * a + W - 1, np.maximum(a - 1, 0), W - 1 - a, (a + 1) % W, a ^ 1]
    kind = rng.integers(0, 4, (N, 8)); kind[0] = (1, 0, 2, 3, 1, 3, 0, 1)
    r = rng.random((N, 8, 1, K)); la = np.where(r < 0.1, 0, np.where(r < 0.2, W - 1, la))
    z[..., K - 1] = z[..., 0]; c = cell(z)
    for q in range(N):
        for g in range(8):
            i = (g + q) % 8
            if i < 7: fo[q, g] = pat[i]
            if kind[q, g] == 1: t[q, g] = 4080
            if kind[q, g] == 2: t[q, g] = 0
            if kind[q, g] == 3: t[q, g] = np.where(LEV[0, 0] < rng.integers(1, 16), 4080, 0)
            for j in rng.permutation(K)[:8]:
                bk[q, g][:, c[q, g, j]] = la[q, g][:, j]; bk[q, g, 15, c[q, g, j]] = rng.integers(0, W)
    return pack(x, fo, bk, la, z, t)
def setup_inputs_crowd(rng):
    x, fo, bk, la, z, t = parts(rng)
    for q in range(N):
        for g in range(8):
            k = g % 4; j = K - 1 if q == 0 else int(rng.integers(0, K))
            if k != 3: z[q, g] = z[q, g][:, :1].copy(); la[q, g] = la[q, g][:, :1].copy()
            if k == 2: t[q, g] = 0
            else: fo[q, g] = np.arange(W); la[q, g, 0] = W - 1; t[q, g, 0] = 4080
            c = (255 + np.add.reduce(HC[0, 0] * z[q, g], axis=0)) & (C - 1)
            if k in (0, 1): bk[q, g][:, c[0]] = la[q, g][:, 0]; bk[q, g, 0, c[0]] = rng.integers(0, W - 1)
            if k == 3: bk[q, g, 0] = rng.integers(0, W - 1, C)
            if k == 1 or (k == 3 and q % 2 == 1): la[q, g][:, j] = bk[q, g][:, c[j]]
    return pack(x, fo, bk, la, z, t)
def setup_inputs_ties(rng):
    x, fo, bk, la, z, t = parts(rng, 1)
    t = -np.sort(-rng.integers(14, 25, (N, 8, 16, 1)), axis=2)
    for g in (2, 6):
        mid = rng.integers(40, 216, (16, 1)); fo[:, g] = np.arange(W)
        x[:, g] = mid + rng.integers(-1, 2, (N, 16, W)); z[:, g] = mid + rng.integers(-1, 2, (N, 16, K))
    t[:, 2] = 22 - LEV[0, 0] // 2
    for q in range(N):
        a = rng.integers(0, W - 1, (16, 1)); la[q, 2] = a; bk[q, 2] = a
        x[q, 2, :, W - 1] = x[q, 2, :, int(a[0, 0])]
        j = rng.permutation(K)[:1 + q % 3]; la[q, 2, 0, j] = W - 1; z[q, 2][:, j] = x[q, 2, :, W - 1:]
    la[:, 6] = rng.integers(0, W, (N, 16, K)); bk[:, 6] = rng.integers(0, W, (N, 16, C)); t[:, 6] = 9
    return pack(x, fo, bk, la, z, t)
def check_inputs(d):
    bad = []
    for k, hi in (("x", 255), ("fw", W - 1), ("bk", W - 1), ("la", W - 1), ("zz", 255), ("th", 4080)):
        v = np.asarray(d[k]).astype(np.float64)
        if not (np.min(v) >= 0 and np.max(v) <= hi): bad.append("range of " + k)
        elif np.any(v != np.floor(v)): bad.append("whole numbers of " + k)
    return bad
def reference(x, fw, bk, la, zz, th):
    X = x.astype(np.float32).astype(np.int32).reshape(N, 8, 16, W); Z = zz.astype(np.float32).astype(np.int32).reshape(N, 8, 16, K)
    F = fw.astype(np.int64).reshape(N, 8, W); B = bk.astype(np.int64).reshape(N, 8, 16, C); L = la.astype(np.int64).reshape(N, 8, 16, K)
    T = th.astype(np.int64).reshape(N, 8, 16, 1); A = np.zeros((N, 8, 1, 1), np.int64)
    for v in range(VISITS):
        if v > 0:
            s = 1 + (v - 1) % (N - 1); L = np.roll(L, s, axis=0); Z = np.roll(Z, s, axis=0)
        L = take(F, L.reshape(N, 8, 16 * K)).reshape(N, 8, 16, K)
        c = cell(Z)
        G = take(F, take(B, c[:, :, None, :]).reshape(N, 8, 16 * K)).reshape(N, 8, 16, K)
        d = np.add.reduce(np.abs(take(X, L.reshape(N, 8, 1, 16 * K)).reshape(N, 8, 16, 16, K) - Z[:, :, :, None, :]), axis=2)
        e = np.add.reduce(np.abs(take(X, G.reshape(N, 8, 1, 16 * K)).reshape(N, 8, 16, 16, K) - Z[:, :, :, None, :]), axis=2)
        fail = d > T + (A & 15); ks = np.where(np.any(fail, axis=2), np.argmax(fail, axis=2), 16)
        good = (G != L) & (e <= T); m = np.where(np.any(good, axis=2), np.argmax(good, axis=2), 16)
        merge = m < ks
        u = ((255 + np.add.reduce(UC * Z, axis=2)) & 1023)[:, :, None, :]
        new = np.where(LEV >= ks[:, :, None, :], (((L * u) >> 5) + L + 613 * LEV) & (W - 1), L)
        w = np.take_along_axis(new, np.minimum(ks, 15)[:, :, None, :], 2)
        val = np.where(ks[:, :, None, :] < 16, Z, (take(X, w) + Z) >> 1)
        mm = np.minimum(m, 15)[:, :, None, :]; gm = np.take_along_axis(G, mm, 2); lm = np.take_along_axis(L, mm, 2)
        hi = np.maximum(gm, lm)[:, :, 0]; lo = np.minimum(gm, lm)[:, :, 0]
        Z = np.where(m[:, :, None, :] < 16, (Z + take(X, gm)) >> 1, Z)
        for q in range(N):
            for g in range(8):
                j = first(w[q, g, 0]); X[q, g][:, w[q, g, 0, j]] = val[q, g][:, j]
                j = first(c[q, g]); B[q, g][:, c[q, g, j]] = new[q, g][:, j]
                j = np.flatnonzero(merge[q, g]); j = j[first(hi[q, g, j])]; F[q, g, hi[q, g, j]] = lo[q, g, j]
        A = np.add.reduce(merge.astype(np.int64), axis=2)[:, :, None, None]
        L = new
    return {"yx": X.reshape(N, 128, W).astype(np.float32).astype(BF), "yf": F.astype(np.float32), "yb": B.reshape(N, 128, C).astype(np.float32),
            "yl": L.reshape(N, 128, K).astype(np.float32), "yz": Z.reshape(N, 128, K).astype(np.float32).astype(BF)}

@@ -1,0 +1,598 @@
+from concourse.mybir import AluOpType as A, ActivationFunctionType as AF
+
+VIS, W, C, K, LV = 5, 4096, 1024, 256, 16
+PAD = 16
+NCH = 4
+CL = K // NCH
+CE = CL * LV
+WAKE, CYC, PEC, GAT, SCA, SLACK = 100.0, 1.0, 0.85, 1.56, 3.8, 60.0
+BASE = ("fg0 fg1 fg2 fg3 zb sc eb xl0 ul0 xl1 ul1 fh0 xl2 ul2 ob fh1 xl3 ul3 fh2 fh3 flf xg0 da0 da1 ug0 xg1 ug1 xg2 sd0 da2 ug2 "
+        "xg3 sd1 sd2 da3 sd3 df nn ea0 ug3 nw ea1 ea2 ea3 wv wm se0 se1 hv we ")
+ORDER = BASE + "sl bs vv se2 se3 eg h1 hk l1 zi h2 wl lm zz h3 wo xs aa l2 h4 fs"
+ORDER_LAST = BASE + "sl wl vv wo xs se2 se3 eg h1 hk l1 ff0 zi h2 ff1 lm zz h3 ff2 ff3 bs h4 fs"
+
+SCRATCH, LOC = {}, {}
+DT2 = ("bfloat16", "float16", "uint16")
+for _b, _d, _l in (
+        ("", "bfloat16", "X 4112 Fw 4112 FG 4096 FH 4096 D 4096 E 4096 DA 4096 EA 4096 z16 4096 zsp 4096 zm 4096 fh 256 fl 256 eq 256 "
+         "fs 256 gs 256 fg 256 mg 256 Emb 256 Emw 256 Emh 256 val 256 hm 256 lod 256"),
+        ("kb", "bfloat16", "SK 2048 MK 2048 cS 128 cSr 128 cSn 128 cSb 128 cSbn 128 cS1 128 cS4 128 cS4n 128 cSq 128 cI 128 cI8 128 C1 128 "
+         "C2 128 C2f 128 C3 128 C4 128 c01 128 cZ 128 MSK 256 dd 32 J16 16 ones 256"),
+        ("", "float32", "Ff 4112 Aac 1 fc 256 FLc 256 FLf 256 r1 256 lof 256 ybo 1024 ylo 256"),
+        ("kf", "float32", "cSf 128 mask 256 rq 128 gq 128 code 128 tr 128 idn 128 tmp 128 tmp2 128 tmp3 128 tmp4 128 tmp5 128 rq2 256 s16 16 "
+         "s8 16 j16 16 rp 1 gp 1 m0 1 m1 1 m15 1 zc 1 zc2 1 zc3 1 c613 1 bY 1 bG 1 bM 1 Tn 1 Tp 1 thr 1"),
+        ("", "int32", "Bt 1040 tI 1 f0 256 la0 256 i1 256 i2 256 r2 256 sn 256 new 256 zh 256 hd 256"),
+        ("ki", "int32", "pi 1 pi2 1 pi3 1 a1 1 a2 1"),
+        ("", "float16", "bu 256 nC 256 Vw 256 Vh 256 Vl 256 WTb 256 WTw 256 WTh 256"),
+        ("", "uint16", "bl 16 Bb 256 FLu 256 Gu 256 ofb 32 ofw 32 ofh 32 idx 16")):
+    _l, _c = _l.split(), 0
+    for _i in range(0, len(_l), 2):
+        _n, _w = _l[_i], int(_l[_i + 1])
+        if _b:
+            LOC[_n] = (_b, _c, _w)
+            _c += (_w + 15) // 16 * 16
+            SCRATCH[_b] = ("sbuf", [128, _c], _d)
+        else:
+            SCRATCH[_n] = ("sbuf", [128, _w], _d)
+for _v in range(VIS + 1):
+    if _v < VIS:
+        SCRATCH["L%d" % _v] = ("sbuf", [128, K], "uint16")
+        SCRATCH["z%d" % _v] = ("sbuf", [128, K], "bfloat16")
+    if _v > 0:
+        SCRATCH["zs%d" % _v] = ("sbuf", [128, K], "bfloat16")
+    if 0 < _v < VIS:
+        SCRATCH["Ls%d" % _v] = ("sbuf", [128, K], "uint16")
+PSUM = {"pF": 1024, "pd": 512, "pe": 512, "pC": 512, "pS": 512, "pH": 512, "pX": 512}
+for _n in PSUM:
+    SCRATCH[_n] = ("psum", [128, PSUM[_n]], "float32")
+NDMA = 16
+SEMAPHORES = ["q_v", "q_s", "q_t", "q_g"] + ["d%d" % i for i in range(NDMA)]
+for _v in range(1, VIS):
+    SEMAPHORES += ["aL%d" % _v, "aZ%d" % _v, "lL%d" % _v, "lZ%d" % _v]
+
+
+def make(g, T):
+    queues = {"v": g.vector, "s": g.scalar, "t": g.tensor, "g": g, "y": g.sync}
+    ops, hw, hr, bank, marks = [], {}, {}, {}, {}
+    nd = [0]
+
+    def ap(o):
+        if o[0] == "@":
+            return ap(o[1]).indirect(ap(o[2]))
+        b, a = (LOC[o[0]][0], LOC[o[0]][1]) if o[0] in LOC else (o[0], 0)
+        if len(o) == 4 and o[3] != 1:
+            return T[b][:, a + o[1]:a + o[2]:o[3]]
+        return T[b][:, a + o[1]:a + o[2]]
+
+    def regs(o):
+        if o is None or isinstance(o, (int, float)):
+            return []
+        if o[0] == "@":
+            return regs(o[1]) + regs(o[2])
+        return [o]
+
+    def val(o):
+        return o if o is None or isinstance(o, (int, float)) else ap(o)
+
+    def rec(q, reads, writes, call, cost, tail=0.0, tok=None, own=True, extra=(), beside=False):
+        i = len(ops)
+        deps = {}
+
+        def dep(j, w):
+            deps[j] = deps.get(j, False) or w
+        for o, w in [(r, False) for r in reads] + [(r, True) for r in writes]:
+            if w and beside:
+                continue
+            for h in hw.get(o[0], []):
+                if h[0] < o[2] and o[1] < h[1]:
+                    dep(h[2], not (own and ops[h[2]][0] == q and w and q == "t"))
+            if w:
+                for h in hr.get(o[0], []):
+                    if h[0] < o[2] and o[1] < h[1]:
+                        dep(h[2], not (own and ops[h[2]][0] == q))
+        for o in reads + writes:
+            if o[0] in PSUM:
+                for b in range(o[1] // 512, (o[2] - 1) // 512 + 1):
+                    k = bank.setdefault((o[0], b), {})
+                    for q2 in k:
+                        if k[q2] != i:
+                            dep(k[q2], q2 != q)
+                    k[q] = i
+        for j in extra:
+            dep(j, True)
+        ops.append((q, call, deps, cost, tail, tok))
+        for o in reads:
+            hr.setdefault(o[0], []).append((o[1], o[2], i))
+        for o in writes:
+            if (len(o) < 4 or o[3] == 1) and not beside:
+                for h in (hw, hr):
+                    h[o[0]] = [e for e in h.get(o[0], []) if not (o[1] <= e[0] and e[1] <= o[2])]
+            hw.setdefault(o[0], []).append((o[1], o[2], i))
+        return i
+
+    def num(o):
+        if o[0] == "@":
+            return LV * num(o[2])
+        return -(-(o[2] - o[1]) // (o[3] if len(o) > 3 else 1))
+
+    def two(*l):
+        for o in l:
+            o = o[1] if o[0] == "@" else o
+            if SCRATCH[LOC[o[0]][0] if o[0] in LOC else o[0]][2] not in DT2:
+                return 1.0
+        return 0.5
+
+    def vec(out, ins, call, rate):
+        n = num(out)
+        cost = max(64.0, rate * n) * CYC
+        for o in ins:
+            if not isinstance(o, (int, float)) and o[0] == "@":
+                cost = 50.0 + GAT * n * CYC
+        if out[0] == "@":
+            cost = 50.0 + SCA * n * CYC
+        reads, writes = sum([regs(o) for o in ins], []), regs(out)
+        if out[0] == "@":
+            reads, writes = reads + regs(out[2]), regs(out[1])
+        rec("v", reads, writes, call, cost)
+
+    def cp(out, in_):
+        vec(out, [in_], lambda e: e.tensor_copy(ap(out), ap(in_)), two(out, in_))
+
+    def ms(out, c):
+        vec(out, [], lambda e: e.memset(ap(out), c), two(out))
+
+    def tt(out, a, b, op):
+        vec(out, [a, b], lambda e: e.tensor_tensor(ap(out), ap(a), ap(b), op), 1.0 if a[0] in PSUM or b[0] in PSUM else 2.0)
+
+    def ts(out, a, s1, op0, s2=None, op1=None):
+        ins = [o for o in (a, s1, s2) if o is not None]
+        if op1 is None:
+            vec(out, ins, lambda e: e.tensor_scalar(ap(out), ap(a), val(s1), None, op0), two(out, a))
+        else:
+            vec(out, ins, lambda e: e.tensor_scalar(ap(out), ap(a), val(s1), val(s2), op0, op1), two(out, a))
+
+    def scan(out, a, b, op0, op1):
+        vec(out, [a, b], lambda e: e.tensor_tensor_scan(ap(out), ap(a), ap(b), 0.0, op0, op1), two(out, a, b))
+
+    def act(out, in_, func, bias=0.0, scale=1.0, acc=None):
+        kw = {}
+        if acc is not None:
+            kw["accum_out"] = ap(acc)
+        if not (isinstance(bias, float) and bias == 0.0):
+            kw["bias"] = val(bias)
+        if not (isinstance(scale, float) and scale == 1.0):
+            kw["scale"] = val(scale)
+        n = num(out)
+        cost = 65.0 + GAT * n * CYC if in_[0] == "@" else max(64.0, n) * CYC
+        rec("s", regs(in_) + regs(bias) + regs(scale), regs(out) + regs(acc), lambda e: e.activation(ap(out), ap(in_), func, **kw), cost)
+
+    def mm(out, lhsT, rhs, start=True, stop=True):
+        rec("t", regs(lhsT) + regs(rhs), regs(out), lambda e: e.matmul(ap(out), ap(lhsT), ap(rhs), start, stop), max(64.0, num(out)) * PEC)
+
+    def iota(out, pattern, mult):
+        rec("g", [], regs(out), lambda e: e.iota(ap(out), pattern, 0, mult, allow_small_or_imprecise_dtypes=True), 130.0 + 2 * num(out))
+
+    def pick(out, in_, pattern, base):
+        rec("g", regs(in_), regs(out), lambda e: e.affine_select(ap(out), ap(in_), pattern, A.is_equal, 0.0, base, 0), 170.0 + 2 * num(out))
+
+    def dma(q, out, in_, reads, writes, beside=False, us=2.5):
+        s = "d%d" % nd[0]
+        nd[0] += 1
+        rec(q, reads, writes, lambda e: e.dma_start(out, in_), 70.0, 1000.0 * us, (s, 16), False, (), beside)
+
+    def arrive(o, s, v, mark):
+        rec(None, [], [o], None, 0.0, 0.0, (s, v), False, (marks[mark],))
+
+    def send(o, out, topo, core, dst, rs, ls, mark):
+        rid, pid = topo.addr(dst)[0:2]
+        marks[mark] = rec("g", regs(o), [], lambda e: e.remote_dma(ap(out), ap(o), T.sem[rs], T.sem[ls], pid, rid, topo.mask(core, dst)),
+                          700.0, 3000.0, (ls, len(topo.engines(core, dst))), False)
+
+    def issue():
+        n = len(ops)
+        succ, left = [[] for _ in ops], [len(op[2]) for op in ops]
+        for i, op in enumerate(ops):
+            for j in op[2]:
+                succ[j].append(i)
+        prio = [0.0] * n
+        for i in range(n - 1, -1, -1):
+            prio[i] = ops[i][3] + ops[i][4] + max([prio[j] + (WAKE if ops[j][2][i] else 0.0) for j in succ[i]] or [0.0])
+        free = {q: 0.0 for q in queues}
+        done, start = [0.0] * n, [0.0] * n
+        ready = {q: [] for q in queues}
+        seq = []
+
+        def put(i):
+            t = max([done[j] if ops[i][2][j] else start[j] for j in ops[i][2]] or [-1.0])
+            if ops[i][0] is None:
+                finish(i, t)
+            else:
+                ready[ops[i][0]].append((t, i))
+
+        def finish(i, t):
+            start[i], done[i] = t, t + ops[i][3] + ops[i][4]
+            seq.append(i)
+            for j in succ[i]:
+                left[j] -= 1
+                if left[j] == 0:
+                    put(j)
+        for i in range(n):
+            if not ops[i][2]:
+                put(i)
+        while len(seq) < n:
+            best = None
+            for q in queues:
+                if not ready[q]:
+                    continue
+                c = [((free[q] if t < free[q] else t + WAKE), i) for t, i in ready[q]]
+                m = min(c)[0]
+                s, i = max([(prio[i], s, i) for s, i in c if s <= m + SLACK])[1:]
+                if best is None or s < best[0]:
+                    best = (s, q, i)
+            s, q, i = best
+            ready[q] = [e for e in ready[q] if e[1] != i]
+            free[q] = s + ops[i][3]
+            finish(i, s)
+        clk, snap, final = {q: {} for q in queues}, {}, {}
+        cnt, token = {"v": 0, "s": 0, "t": 0, "g": 0}, {}
+
+        def wait(q, tok):
+            s, v = tok
+            if clk[q].get(s, 0) >= v:
+                return
+            queues[q].wait_ge(T.sem[s], v)
+            for a in snap[tok]:
+                if clk[q].get(a, 0) < snap[tok][a]:
+                    clk[q][a] = snap[tok][a]
+            clk[q][s] = v
+        for i in seq:
+            q, call, deps, cost, tail, tok = ops[i]
+            need = {}
+            for j in deps:
+                if deps[j] and q is not None:
+                    need[token[j][0]] = max(need.get(token[j][0], 0), token[j][1])
+            for s in need:
+                wait(q, (s, need[s]))
+            if q is None:
+                snap[tok] = {}
+            else:
+                ins = call(queues[q])
+                if tok is None:
+                    cnt[q] += 1
+                    tok = ("q_" + q, cnt[q])
+                    ins.then_inc(T.sem[tok[0]], 1)
+                elif tok[0][0] == "d":
+                    ins.then_inc(T.sem[tok[0]], 16)
+                snap[tok] = dict(clk[q])
+            token[i] = tok
+            final[tok[0]] = max(final.get(tok[0], 0), tok[1])
+        for s in final:
+            wait("g", (s, final[s]))
+    return cp, ms, tt, ts, scan, act, mm, iota, pick, dma, arrive, send, issue
+
+
+def rank_program(g, core, T, topo):
+    rank = T.rank_of(core)
+    if rank is None:
+        return
+    cp, ms, tt, ts, scan, act, mm, iota, pick, dma, arrive, send, issue = make(g, T)
+    ranks = len(T.cores)
+
+    def f(name, w=None, a=0):
+        full = LOC[name][2] if name in LOC else SCRATCH[name][1][1]
+        return (name, a, full if w is None else a + w)
+
+    def sk(k, name="SK"):
+        return (name, 128 * k, 128 * k + 128)
+
+    dma("y", T.f0[:, :], T.fw[:, :], [], [f("f0")])
+    dma("y", T.la0[:, :], T.la[:, :], [], [f("la0")])
+    dma("y", T.z0[:, :], T.zz[:, :], [], [f("z0")])
+    dma("y", T.tI[:, :], T.th[:, :], [], [f("tI")])
+    iota(f("pi"), [[0, 1]], 1)
+    iota(f("gq"), [[1, 8], [0, 16]], 0)
+    iota(f("rq2"), [[0, 16], [1, 16]], 0)
+    iota(f("rq"), [[0, 8], [1, 16]], 0)
+    iota(f("s16"), [[1, 16]], 0)
+    iota(f("j16"), [[256, 16]], 0)
+    ts(f("pi2"), f("pi"), 15, A.bitwise_and)
+    ts(f("pi3"), f("pi"), 4, A.arith_shift_right)
+    cp(f("rp"), f("pi2"))
+    cp(f("gp"), f("pi3"))
+    ts(f("cSf"), f("gq"), f("gp"), A.is_equal)
+    cp(f("cS"), f("cSf"))
+    for k in range(LV):
+        pick(sk(k), f("cS"), [[0, 8], [1, 16]], -k)
+    ms(f("Fw"), 0.0)
+    for k in range(16):
+        act(f("zm", 256, 256 * k), f("rq2"), AF.Identity, 1.0, 0.0)
+    for k in range(8):
+        act(f("zsp", 256, 256 * k), f("rq2"), AF.Identity, 0.0, 0.0)
+    ts(f("fc"), f("f0"), -2048.0, A.add)
+    cp(f("fh"), f("fc"))
+    dma("y", T.Fw[0:128:16, PAD:PAD + W], T.fh[:, :], [f("fh")], [f("Fw")])
+    tt(f("fl"), f("fc"), f("fh"), A.subtract)
+    dma("y", T.Fw[1:128:16, PAD:PAD + W], T.fl[:, :], [f("fl")], [f("Fw")], True)
+    dma("y", T.Bt[:, PAD:PAD + C], T.bk[:, :], [], [f("Bt", C, PAD)], False, 4.0)
+    dma("y", T.X[:, PAD:PAD + W], T.x[:, :], [], [f("X", W, PAD)], False, 7.0)
+    cp(f("L0"), f("la0"))
+    ms(f("zsp", 2048, 2048), 0.0)
+    ms(("zm", 0, W, LV), 0.0)
+    ts(f("tmp"), f("gq"), f("gp"), A.not_equal, 100.0, A.mult)
+    tt(f("code"), f("tmp"), f("rq"), A.add)
+    ts(f("m0"), f("rp"), 0.0, A.is_equal)
+    ts(f("zc"), f("rp"), 10.0, A.mult, 5.0, A.add)
+    ts(f("zc2"), f("rp"), 4.0, A.mult, 34.0, A.add)
+    ts(f("tmp4"), f("code"), 0.0, A.is_equal, f("zc2"), A.mult)
+    ts(f("tmp2"), f("cSf"), f("zc"), A.mult)
+    tt(f("cZ"), f("tmp4"), f("tmp2"), A.add)
+    ts(f("cSb"), f("cSf"), f("m0"), A.mult)
+    ts(f("mask"), f("rq2"), f("rp"), A.is_equal)
+    ts(f("dd", 16), f("s16"), f("gp"), A.is_equal)
+    ts(f("s8"), f("s16"), -8.0, A.add)
+    ts(f("dd", 16, 16), f("s8"), f("gp"), A.is_equal)
+    ts(f("cSbn"), f("cSb"), -1.0, A.mult)
+    ts(f("m1"), f("rp"), 1.0, A.is_equal, 0.03125, A.mult)
+    ts(f("cS1"), f("cSf"), f("m1"), A.mult)
+    ts(f("MSK"), f("rq2"), f("rp"), A.is_le, 16384.0, A.mult)
+    ts(f("idn"), f("code"), f("rp"), A.is_equal)
+    cp(f("cI"), f("idn"))
+
+    def late_constants():
+        ts(f("cSr"), f("cSf"), f("rp"), A.mult)
+        for k in range(LV):
+            pick(sk(k, "MK"), f("cSr"), [[0, 8], [1, 16]], -k)
+        ts(f("cI8"), f("idn"), 8192.0, A.mult)
+        ts(f("cSn"), f("cSf"), -1.0, A.mult)
+        ts(f("cS4"), f("cSf"), 4096.0, A.mult)
+        ts(f("cS4n"), f("cSf"), -4096.0, A.mult)
+        ts(f("cSq"), f("cSf"), -256.0, A.mult)
+        ts(f("C4"), f("cSf"), -0.5, A.mult)
+        ts(f("tmp3"), f("rq"), f("rp"), A.is_ge)
+        tt(f("tr"), f("tmp3"), f("cSf"), A.mult)
+        ts(f("C1"), f("tr"), 131072.0, A.mult)
+        ts(f("C3"), f("tr"), -0.5, A.mult)
+        ts(f("tmp2"), f("idn"), 1.5, A.mult)
+        tt(f("tmp"), f("tmp2"), f("tr"), A.subtract)
+        cp(f("C2"), f("tmp"))
+        ts(f("m15"), f("rp"), 15.0, A.is_equal, 0.5, A.mult)
+        ts(f("tmp5"), f("code"), 15.0, A.is_equal, f("m15"), A.mult)
+        tt(f("C2f"), f("tmp"), f("tmp5"), A.subtract)
+        ts(f("c01"), f("code"), 1.0, A.is_le)
+        ms(f("ones"), 1.0)
+        ts(f("zc3"), f("rp"), 16.0, A.mult)
+        ts(f("J16"), f("j16"), f("zc3"), A.add)
+        ts(f("c613"), f("rp"), 613.0, A.mult, -15.5 / 32, A.add)
+        ts(f("bG"), f("rp"), -1.0, A.mult, 0.5, A.add)
+        tt(f("bY"), f("bG"), f("m15"), A.add)
+        ts(f("bM"), f("rp"), -1.5, A.mult)
+        ts(f("Tn"), f("tI"), -1.0, A.mult, -0.5, A.add)
+        ts(f("Tp"), f("tI"), 0.5, A.add)
+        cp(f("thr"), f("Tn"))
+
+    def keys_t(prods, pb, null=False):
+        for h in range(2):
+            if null:
+                mm(f(pb, 128, 128 * h), f("ones", 128), f("cSq"), True, False)
+            for i, (rows, sel, nsel) in enumerate(prods):
+                mm(f(pb, 128, 128 * h), f(rows, 128, 128 * h), f(sel), i == 0 and not null, i == len(prods) - 1)
+
+    def diff(prods, wt, pb):
+        mm(f(pb, 256, 256), f("cI"), f("MSK"), True, False)
+        for rows, sel, nsel in prods:
+            mm(f(pb, 256, 256), f(nsel), f(rows), False, False)
+        for h in range(2):
+            mm(f(pb, 128, 256 + 128 * h), f(wt, 128, 128 * h), f("cS"), False, h == 1)
+
+    def mylist(wt, pb, a, stop):
+        for h in range(2):
+            mm(f(pb, 16, a), f(wt, 128, 128 * h), f("dd", 16, 16 * h), h == 0, stop and h == 1)
+
+    def lost(em, pb):
+        for r in range(16):
+            mm(f(pb, 16), sk(r), (em, r, K, 16), False, r == 15)
+
+    def eqs(em, pb, null=0.0):
+        ts(f(em), f(pb, 256, 256), null, A.is_equal, -8192.0, A.mult)
+
+    def offs(of, pb, c):
+        ts((of, 0, 31, 2), f(pb, 16), c, A.add, f("rp"), A.max)
+
+    def scatter(tab, of, data):
+        for s in range(15, -1, -1):
+            cp(("@", f(tab), (of, 2 * s, 2 * s + 1)), f(data, 16, 16 * s))
+
+    FW, XW = f("Fw", W, PAD), f("X", W, PAD)
+    pb = [("bu", "cSb", "cSbn")]
+    pw = [("Vw", "cS", "cSn")]
+    ph = [("Vh", "cS", "cSn"), ("mg", "cS4", "cS4n")]
+
+    def pf(c):
+        return 512 * (c % 2) + CL * (c // 2)
+
+    def turn(out, src, c, stop=True):
+        for k in range(LV):
+            mm(out, sk(k), (src, CE * c + k, CE * (c + 1), LV), k == 0, stop and k == LV - 1)
+
+    def step(s, v, L, z, last, dst):
+        c = int(s[2]) if len(s) == 3 and s[2] in "0123" else 0
+        zs, nx = "zs%d" % (v + 1), "%d" % (v + 1)
+        lanes, ents = CL * c, f("z16", CE, CE * c)
+        k = s[:2]
+        if k == "fg":
+            act(f("FG", CE, CE * c), ("@", FW, f(L, CL, lanes)), AF.Copy)
+        elif k == "fh":
+            act(f("FH", CE, CE * c), ("@", FW, f("Bb", CL, lanes)), AF.Copy)
+        elif k == "zb":
+            mm(f("pX", 256), f("cZ"), f(z))
+            ts(f("i1"), f("pX", 256), 255.0, A.add)
+            ts(f("i2"), f("i1"), 1023, A.bitwise_and)
+            cp(f("bu"), f("i2"))
+            keys_t(pb, "pC")
+            cp(("zsp", 0, W, LV), f(z))
+            tt(f("WTb"), f("pC", 256), f("mask"), A.mult)
+            mylist("WTb", "pC", 16, True)
+            cp(f("bl"), f("pC", 16, 16))
+            cp(f("Bb"), ("@", f("Bt", C, PAD), f("bl")))
+            diff(pb, "WTb", "pC")
+            mm(f("pX", 256, 256), f("cS1"), f("bu"))
+        elif k == "sc":
+            for c in range(NCH):
+                scan(f("z16", CE, CE * c), f("zm", CE, CE * c), f("zsp", CE, CE * c), A.mult, A.add)
+        elif k == "eb":
+            eqs("Emb", "pC")
+        elif k == "ob":
+            mylist("WTb", "pC", 0, False)
+            lost("Emb", "pC")
+            offs("ofb", "pC", float(PAD))
+        elif s == "flf":
+            act(f("FLf"), f("FLc"), AF.Identity, 2048.0)
+            if v == 0:
+                late_constants()
+        elif k == "xl":
+            turn(f("pF", CL, pf(c)), "FG", c)
+        elif k == "ul":
+            ts(f("FLu", CL, lanes), f("pF", CL, pf(c)), 2048.0, A.add)
+            cp(f("FLc", CL, lanes), f("pF", CL, pf(c)))
+            tt(f("D", CE, CE * c), ("@", XW, f("FLu", CL, lanes)), ents, A.subtract)
+        elif k == "xg":
+            turn(f("pF", CL, pf(NCH + c)), "FH", c)
+        elif k == "ug":
+            p = f("pF", CL, pf(NCH + c))
+            ts(f("Gu", CL, lanes), p, 2048.0, A.add)
+            tt(f("eq", CL, lanes), p, f("FLc", CL, lanes), A.is_equal)
+            tt(f("pH", CL, lanes), p, f("FLc", CL, lanes), A.max)
+            tt(f("pH", CL, 256 + lanes), p, f("FLc", CL, lanes), A.min)
+            tt(f("E", CE, CE * c), ("@", XW, f("Gu", CL, lanes)), ents, A.subtract)
+        elif k == "da":
+            act(f("DA", CE, CE * c), f("D", CE, CE * c), AF.Abs)
+        elif k == "sd":
+            turn(f("pd", CL, lanes), "DA", c)
+        elif k == "ea":
+            act(f("EA", CE, CE * c), f("E", CE, CE * c), AF.Abs)
+        elif k == "se":
+            turn(f("pe", CL, lanes), "EA", c, False)
+            mm(f("pe", CL, lanes), f("cI8"), f("eq", CL, lanes), False, True)
+        elif k == "df":
+            act(f("fs"), f("pd", 256), AF.Sign, f("thr"))
+            mm(f("pC", 256), f("C1"), f("ones"), True, False)
+            mm(f("pC", 256), f("C1"), f("fs"), False, True)
+            mm(f("pd", 256, 256), f("C2f"), f("fs"))
+            act(f("pd", 256), f("pd", 256, 256), AF.Relu, f("bY"))
+        elif k == "nn":
+            mm(f("pd", 256, 256), f("C4"), f("fs"))
+            act(f("pd", 256, 256), f("pd", 256, 256), AF.Relu, -7.0)
+        elif k == "nw":
+            tt(f("r1"), f("pX", 256, 256), f("FLf"), A.mult)
+            ts(f("r2"), f("r1"), f("c613"), A.add)
+            tt(f("pC", 256, 256), f("pC", 256), f("r2"), A.min)
+            tt(f("sn"), f("pC", 256, 256), f("FLf"), A.add)
+            ts(f("new"), f("sn"), 4095, A.bitwise_and)
+        elif k == "sl":
+            if last:
+                cp(f("ylo"), f("new"))
+                dma("y", T.yl[:, :], T.ylo[:, :], [f("ylo")], [])
+            else:
+                cp(f("Ls" + nx), f("new"))
+                send(f("Ls" + nx), f("L" + nx), topo, core, dst, "aL" + nx, "lL" + nx, "L" + nx)
+        elif k == "wv":
+            ts(f("nC"), f("new"), -2048.0, A.add)
+            tt(f("Vw"), f("pd", 256), f("nC"), A.mult)
+        elif k == "wm":
+            keys_t(pw, "pX")
+            tt(f("WTw"), f("pX", 256), f("mask"), A.mult)
+            diff(pw, "WTw", "pX")
+            mylist("WTw", "pX", 0, False)
+        elif k == "we":
+            eqs("Emw", "pX")
+        elif k == "wl":
+            lost("Emw", "pX")
+        elif k == "wo":
+            offs("ofw", "pX", float(2048 + PAD))
+        elif k == "eg":
+            act(f("gs"), f("pe", 256), AF.Sign, f("Tp"), -1.0)
+            mm(f("pS", 256, 256), f("C3"), f("fs"), True, False)
+            mm(f("pS", 256, 256), f("C2"), f("gs"), False, True)
+            act(f("mg"), f("pS", 256, 256), AF.Relu, f("bM"), 1.0, f("Aac"))
+            mm(f("pS", 256), f("C2"), f("gs"))
+            act(f("fg"), f("pS", 256), AF.Relu, f("bG"))
+        elif k == "h1":
+            tt(f("Vh"), f("pH", 256), f("mg"), A.mult)
+        elif k == "hk":
+            keys_t(ph, "pC", True)
+        elif k == "zi":
+            mm(f("pF", 16, 256), f("cI"), f("J16"), True, False)
+            for r in range(16):
+                mm(f("pF", 16, 256), sk(r, "MK"), ("fg", r, K, 16), False, r == 15)
+            mm(f("pF", 256), f("cS"), f("fg"))
+        elif k == "zz":
+            cp(f("idx"), f("pF", 16, 256))
+            ts(f("zh"), ("@", f("E"), f("idx")), 0.5, A.mult, -0.25, A.add)
+            tt(f("pF", 256, 256), f("pF", 256), f("zh"), A.mult)
+            tt(f(zs), f("pF", 256, 256), f(z), A.add)
+            if last:
+                dma("y", T.yz[:, :], T[zs][:, :], [f(zs)], [])
+            else:
+                send(f(zs), f("z" + nx), topo, core, dst, "aZ" + nx, "lZ" + nx, "Z" + nx)
+        elif k == "h2":
+            tt(f("WTh"), f("pC", 256), f("mask"), A.mult)
+            diff(ph, "WTh", "pC")
+            mylist("WTh", "pC", 0, False)
+        elif k == "h3":
+            eqs("Emh", "pC", -4096.0)
+            lost("Emh", "pC")
+        elif k == "h4":
+            offs("ofh", "pC", float(PAD + 2048))
+        elif k == "l1":
+            tt(f("Vl"), f("pH", 256, 256), f("mg"), A.mult)
+        elif k == "lm":
+            mm(f("pF", 256, 768), f("c01"), f("Vl"))
+            if last:
+                ts(f("lof"), f("pF", 256, 768), 2048.0, A.add)
+            else:
+                act(f("hm"), f("pF", 256, 768), AF.Identity, 0.0, f("m0"))
+        elif k == "l2":
+            tt(f("lod"), f("pF", 256, 768), f("hm"), A.subtract)
+        elif k == "ff":
+            for b in (2 * c, 2 * c + 1):
+                bank = ("pd", "pX")[b % 2]
+                mm(f(bank), f("cS"), f("Fw", 512, PAD + 512 * b))
+                act(f("Ff", 512, PAD + 512 * b), f(bank), AF.Identity, 2048.0)
+        elif k == "fs":
+            if last:
+                scatter("Ff", "ofh", "lof")
+                dma("y", T.yf[:, :], T.Ff[0:128:16, PAD:PAD + W], [f("Ff")], [])
+            else:
+                scatter("Fw", "ofh", "lod")
+        elif k == "bs":
+            scatter("Bt", "ofb", "new")
+            if last:
+                cp(f("ybo"), f("Bt", C, PAD))
+                dma("y", T.yb[:, :], T.ybo[:, :], [f("ybo")], [], False, 4.5)
+        elif k == "hv":
+            ts(f("hd"), ("D", 15, W, LV), 0.5, A.mult, -0.25, A.add)
+        elif k == "vv":
+            tt(f("pd", 256, 256), f("pd", 256, 256), f("hd"), A.mult)
+            tt(f("val"), f("pd", 256, 256), f(z), A.add)
+        elif k == "xs":
+            scatter("X", "ofw", "val")
+            if last:
+                dma("s", T.yx[:, :], T.X[:, PAD:PAD + W], [f("X", W, PAD)], [], False, 7.0)
+        elif k == "aa":
+            mm(f("pS", 1, 256), f("cSf"), f("Aac"))
+            cp(f("a1"), f("pS", 1, 256))
+            ts(f("a2"), f("a1"), 15, A.bitwise_and)
+            tt(f("thr"), f("Tn"), f("a2"), A.subtract)
+
+    for v in range(VIS):
+        L, z = "L%d" % v, "z%d" % v
+        last = v == VIS - 1
+        dst = T.cores[(rank + 1 + v % (ranks - 1)) % ranks]
+        if v > 0:
+            src = T.cores[(rank - 1 - (v - 1) % (ranks - 1)) % ranks]
+            n = len(topo.engines(src, core))
+            arrive(f(L), "aL%d" % v, n, "L%d" % v)
+            arrive(f(z), "aZ%d" % v, n, "Z%d" % v)
+        for s in (ORDER_LAST if last else ORDER).split():
+            step(s, v, L, z, last, dst)
+    issue()

@@ -1,30 +1,49 @@
 from concourse.mybir import AluOpType as A, ActivationFunctionType as AF
 
 VIS, W, C, K, LV = 5, 4096, 1024, 256, 16
-PAD = 16
+PAD = 32
 NCH = 4
 CL = K // NCH
 CE = CL * LV
-WAKE, CYC, PEC, GAT, SCA, SLACK = 100.0, 1.0, 0.85, 1.56, 3.8, 60.0
-BASE = ("fg0 fg1 fg2 fg3 zb sc eb xl0 ul0 xl1 ul1 fh0 xl2 ul2 ob fh1 xl3 ul3 fh2 fh3 flf xg0 da0 da1 ug0 xg1 ug1 xg2 sd0 da2 ug2 "
-        "xg3 sd1 sd2 da3 sd3 df nn ea0 ug3 nw ea1 ea2 ea3 wv wm se0 se1 hv we ")
-ORDER = BASE + "sl bs vv se2 se3 eg h1 hk l1 zi h2 wl lm zz h3 wo xs aa l2 h4 fs"
-ORDER_LAST = BASE + "sl wl vv wo xs se2 se3 eg h1 hk l1 ff0 zi h2 ff1 lm zz h3 ff2 ff3 bs h4 fs"
+ES = CE + 16
+PARTS = ((128, 128), (0, 128))
+NULL, BIG, ROUND, LIFT = -4096.0, 8192.0, 12582912.0, 64.0
+BLOCK = {"X": 16, "F": 32}
+WAKE, CYC, PEC, GAT, SCA, SEND, FLY, ROUNDS = 160.0, 0.9, 0.5, 1.56, 3.8, 1200.0, 4500.0, 3
+ENG = {"fg": "ssss", "fh": "ssss", "da": "ssss", "ea": "vsss", "zz": ("v", "gv"), "y2": "ss", "eg": "s", "bs": "s"}
+ORDER = ("fg3 fg2 ce1 zz1 xl3 xl2 fh3 fh2 fl1 yy1 xg3 xg2 hl1 ce0 zz0 cb fg1 fg0 xl1 xl0 fl0 yy0 fh1 fh0 da3 da2 fs1 nw1 cw1 vq1 ea3 ea2 "
+         "gs0 zp0 mg0 xg1 xg0 hl0 da1 da0 fs0 nw0 cw0 vq0 ea1 ea0 gs1 mg1 zp1 bs1 bs0 xs1 xs0 ")
+ORDER_NEXT, ORDER_LAST = ORDER + "aa", "cp " + ORDER
+RANK_NEXT = ("ea2 zp0 fs0 zp1 fg3 ea0 mg0 nw1 hl1 xl2 nw0 fl1 da2 xg2 ea3 xl3 ea1 gs0 gs1 aa hl0 da3 xg0 zz0 ce0 +zz1 k4 xg3 yy0 fs1 fh3 cw1 fh1 "
+             "mg1 fg2 xg1 yy1 fg1 fl0 +ce1 bs0 cw0 xs1 in xs0 xl0 fh2 da1 k2 fg0 vq1 xl1 k1 cb fh0 vq0 k3 da0 bs1")
+RANK_LAST = ("zp0 ea2 gs1 gs0 cp fs0 ea3 cw0 xg2 fg3 zp1 zz1 fl1 fl0 fh2 hl1 fg0 fh1 mg1 fg2 fh3 zz0 fs1 ea1 yy0 xg3 da1 hl0 yy1 ce0 ce1 ea0 xs1 "
+             "nw0 cw1 xl3 xg0 nw1 vq1 xl0 bs1 xg1 cb fh0 vq0 da3 xl2 da2 da0 xs0 xl1 bs0 mg0 fg1")
+FIRST, SLACK, CHAIN = {}, 0.0, 1e-6
+for _v in range(VIS):
+    for _i, _s in enumerate((RANK_LAST if _v == VIS - 1 else RANK_NEXT).split()):
+        if _s[0] == "+":
+            FIRST[(_v + 1, _s[1:])] = 1000 * _v + _i
+            FIRST[(0, _s[1:])] = _i - 100
+        else:
+            FIRST.setdefault((_v, _s), 1000 * _v + _i)
+FIRST[(0, "in")] = -200
 
+DBG = {"rw": [], "tag": None}
 SCRATCH, LOC = {}, {}
 DT2 = ("bfloat16", "float16", "uint16")
 for _b, _d, _l in (
-        ("", "bfloat16", "X 4112 Fw 4112 FG 4096 FH 4096 D 4096 E 4096 DA 4096 EA 4096 z16 4096 zsp 4096 zm 4096 fh 256 fl 256 eq 256 "
-         "fs 256 gs 256 fg 256 mg 256 Emb 256 Emw 256 Emh 256 val 256 hm 256 lod 256"),
-        ("kb", "bfloat16", "SK 2048 MK 2048 cS 128 cSr 128 cSn 128 cSb 128 cSbn 128 cS1 128 cS4 128 cS4n 128 cSq 128 cI 128 cI8 128 C1 128 "
-         "C2 128 C2f 128 C3 128 C4 128 c01 128 cZ 128 MSK 256 dd 32 J16 16 ones 256"),
-        ("", "float32", "Ff 4112 Aac 1 fc 256 FLc 256 FLf 256 r1 256 lof 256 ybo 1024 ylo 256"),
-        ("kf", "float32", "cSf 128 mask 256 rq 128 gq 128 code 128 tr 128 idn 128 tmp 128 tmp2 128 tmp3 128 tmp4 128 tmp5 128 rq2 256 s16 16 "
-         "s8 16 j16 16 rp 1 gp 1 m0 1 m1 1 m15 1 zc 1 zc2 1 zc3 1 c613 1 bY 1 bG 1 bM 1 Tn 1 Tp 1 thr 1"),
-        ("", "int32", "Bt 1040 tI 1 f0 256 la0 256 i1 256 i2 256 r2 256 sn 256 new 256 zh 256 hd 256"),
-        ("ki", "int32", "pi 1 pi2 1 pi3 1 a1 1 a2 1"),
-        ("", "float16", "bu 256 nC 256 Vw 256 Vh 256 Vl 256 WTb 256 WTw 256 WTh 256"),
-        ("", "uint16", "bl 16 Bb 256 FLu 256 Gu 256 ofb 32 ofw 32 ofh 32 idx 16")):
+        ("", "bfloat16", "X 4128 X2 4128 Fw 4128 FG 4096 FH 4096 D 4096 E 4160 DA 4096 EA 4096 z16 4096 fh 256 fl 256 nq 256 "
+         "fs 256 gs 256 npb 256 sgb 256 eqF 256 eqX 256 sgc 384 hm 256 lod 256 Eg 256"),
+        ("kb", "bfloat16", "SK 2048 SKc 2048 SKu 2048 SEL 2048 DF 2048 LOST 2048 code 128 code2 128 cS 256 I 128 In 128 I32 128 Ih 128 "
+         "Iq 128 I8 128 tr 128 C1 128 Cc 128 C2B 128 C3B 128 C3 128 C2f 128 cV 128 cQ 128 c256 128 HM 128 c75 256 "
+         "mT16 128 mR16 128 bk16 128 dd16 16 mT32 256 mR32 256 bk32 128 dd32 16 t1 128 t2 128 J 16 ones 256"),
+        ("", "float32", "Ff 4128 Bt 1056 fc 256 FLf 256 y1 256 y2 256 lof 256 ylo 256 newf 256 ybo 1024"),
+        ("kf", "float32", "q16 128 g16 128 q32 256 g32 128 tmp 128 s16 16 j16 16 oh 16 da 16 db 16 la 16 lb 16 rp 1 p16 1 r32 1 p32 1 wc 1 wu 1 wv 1 n15 1 "
+         "c613 1 bW0 1 bW 1 bH 1 wN 1 bN0 1 bN 1 bhm 1 blo 1 r16 1 rp1 1 Tn 1 Tp 1 thr 1"),
+        ("", "int32", "Bi 1024 tI 1 f0 256 la0 256 i1 32 i2 32 rr 256 new 256 vq 256 val 256"),
+        ("ki", "int32", "pi 1 pi2 1 pi3 1 pi4 1 pi5 1 a1 1 a2 1"),
+        ("", "float16", "bu 32 FLc 256 hiC 256 loC 256 nC 256 Vw 256 Vh 256 Vl 256 WTF 256 WTX 256"),
+        ("", "uint16", "bl 16 Bb 256 FLu 256 Gu 256 ofB 32 ofX 32 ofF 32 idx 16")):
     _l, _c = _l.split(), 0
     for _i in range(0, len(_l), 2):
         _n, _w = _l[_i], int(_l[_i + 1])
@@ -42,27 +61,34 @@ for _v in range(VIS + 1):
         SCRATCH["zs%d" % _v] = ("sbuf", [128, K], "bfloat16")
     if 0 < _v < VIS:
         SCRATCH["Ls%d" % _v] = ("sbuf", [128, K], "uint16")
-PSUM = {"pF": 1024, "pd": 512, "pe": 512, "pC": 512, "pS": 512, "pH": 512, "pX": 512}
+PSUM = ("a0", "b0", "c0", "d0", "a1p", "b1", "c1", "d1")
+PLACE = {"FL": (0, 0), "G": (0, 128), "difF": (0, 256),
+         "d": (1, 0), "M": (1, 0), "Pw": (1, 0), "keyX": (1, 0), "difX": (1, 128), "ub": (1, 256), "Q": (1, 256), "lstX": (1, 384),
+         "cu": (1, 392), "ix": (1, 408), "lstB": (1, 416),
+         "e": (2, 0), "np": (2, 0), "Pz": (2, 0), "dl": (2, 128), "Pl": (2, 128), "difB": (2, 256),
+         "Ph": (3, 0), "keyF": (3, 128), "lstF": (3, 384), "aa": (3, 400)}
 for _n in PSUM:
-    SCRATCH[_n] = ("psum", [128, PSUM[_n]], "float32")
-NDMA = 16
+    SCRATCH[_n] = ("psum", [128, 512], "float32")
+NDMA = 24
 SEMAPHORES = ["q_v", "q_s", "q_t", "q_g"] + ["d%d" % i for i in range(NDMA)]
 for _v in range(1, VIS):
-    SEMAPHORES += ["aL%d" % _v, "aZ%d" % _v, "lL%d" % _v, "lZ%d" % _v]
+    for _p in ("L0", "L1", "Z0", "Z1", "Z2"):
+        SEMAPHORES += ["a%s_%d" % (_p, _v), "l%s_%d" % (_p, _v)]
 
 
 def make(g, T):
     queues = {"v": g.vector, "s": g.scalar, "t": g.tensor, "g": g, "y": g.sync}
-    ops, hw, hr, bank, marks = [], {}, {}, {}, {}
-    nd = [0]
+    ops, hw, hr, bank, marks = [], {}, {}, [], {}
+    nd, fence = [0], {}
 
     def ap(o):
         if o[0] == "@":
             return ap(o[1]).indirect(ap(o[2]))
         b, a = (LOC[o[0]][0], LOC[o[0]][1]) if o[0] in LOC else (o[0], 0)
-        if len(o) == 4 and o[3] != 1:
-            return T[b][:, a + o[1]:a + o[2]:o[3]]
-        return T[b][:, a + o[1]:a + o[2]]
+        rows = slice(None) if o[4] == 128 else slice(0, o[4])
+        if o[3] != 1:
+            return T[b][rows, a + o[1]:a + o[2]:o[3]]
+        return T[b][rows, a + o[1]:a + o[2]]
 
     def regs(o):
         if o is None or isinstance(o, (int, float)):
@@ -74,6 +100,9 @@ def make(g, T):
     def val(o):
         return o if o is None or isinstance(o, (int, float)) else ap(o)
 
+    def meet(h, o):
+        return h[0] < o[2] and o[1] < h[1] and not (h[3] == o[3] and (h[0] - o[1]) % o[3])
+
     def rec(q, reads, writes, call, cost, tail=0.0, tok=None, own=True, extra=(), beside=False):
         i = len(ops)
         deps = {}
@@ -84,36 +113,30 @@ def make(g, T):
             if w and beside:
                 continue
             for h in hw.get(o[0], []):
-                if h[0] < o[2] and o[1] < h[1]:
+                if meet(h, o):
                     dep(h[2], not (own and ops[h[2]][0] == q and w and q == "t"))
             if w:
                 for h in hr.get(o[0], []):
-                    if h[0] < o[2] and o[1] < h[1]:
-                        dep(h[2], not (own and ops[h[2]][0] == q))
-        for o in reads + writes:
-            if o[0] in PSUM:
-                for b in range(o[1] // 512, (o[2] - 1) // 512 + 1):
-                    k = bank.setdefault((o[0], b), {})
-                    for q2 in k:
-                        if k[q2] != i:
-                            dep(k[q2], q2 != q)
-                    k[q] = i
-        for j in extra:
-            dep(j, True)
+                    if meet(h, o):
+                        dep(h[2], not (own and ops[h[2]][0] == q and ops[h[2]][5] is None))
+        bank.append(sorted(set(o[0] for o in reads + writes if o[0] in PSUM)))
+        for j, w in extra:
+            dep(j, w)
         ops.append((q, call, deps, cost, tail, tok))
+        DBG["rw"].append((DBG["tag"], reads, writes))
         for o in reads:
-            hr.setdefault(o[0], []).append((o[1], o[2], i))
+            hr.setdefault(o[0], []).append((o[1], o[2], i, o[3]))
         for o in writes:
-            if (len(o) < 4 or o[3] == 1) and not beside:
+            if o[3] == 1 and o[4] == 128 and not beside:
                 for h in (hw, hr):
                     h[o[0]] = [e for e in h.get(o[0], []) if not (o[1] <= e[0] and e[1] <= o[2])]
-            hw.setdefault(o[0], []).append((o[1], o[2], i))
+            hw.setdefault(o[0], []).append((o[1], o[2], i, o[3]))
         return i
 
     def num(o):
         if o[0] == "@":
             return LV * num(o[2])
-        return -(-(o[2] - o[1]) // (o[3] if len(o) > 3 else 1))
+        return -(-(o[2] - o[1]) // o[3])
 
     def two(*l):
         for o in l:
@@ -122,117 +145,192 @@ def make(g, T):
                 return 1.0
         return 0.5
 
-    def vec(out, ins, call, rate):
-        n = num(out)
+    def work(q, out, ins, call, rate):
+        n, fixed = num(out), 50.0 if q == "v" else 65.0
         cost = max(64.0, rate * n) * CYC
         for o in ins:
             if not isinstance(o, (int, float)) and o[0] == "@":
-                cost = 50.0 + GAT * n * CYC
+                cost = fixed + GAT * n * CYC
         if out[0] == "@":
-            cost = 50.0 + SCA * n * CYC
+            cost = fixed + SCA * n * CYC
         reads, writes = sum([regs(o) for o in ins], []), regs(out)
         if out[0] == "@":
             reads, writes = reads + regs(out[2]), regs(out[1])
-        rec("v", reads, writes, call, cost)
+        rec(q, reads, writes, call, cost)
 
     def cp(out, in_):
-        vec(out, [in_], lambda e: e.tensor_copy(ap(out), ap(in_)), two(out, in_))
+        work("v", out, [in_], lambda e: e.tensor_copy(ap(out), ap(in_)), two(out, in_))
 
     def ms(out, c):
-        vec(out, [], lambda e: e.memset(ap(out), c), two(out))
+        work("v", out, [], lambda e: e.memset(ap(out), c), two(out))
 
     def tt(out, a, b, op):
-        vec(out, [a, b], lambda e: e.tensor_tensor(ap(out), ap(a), ap(b), op), 1.0 if a[0] in PSUM or b[0] in PSUM else 2.0)
+        work("v", out, [a, b], lambda e: e.tensor_tensor(ap(out), ap(a), ap(b), op), 1.0 if a[0] in PSUM or b[0] in PSUM else 2.0)
 
     def ts(out, a, s1, op0, s2=None, op1=None):
         ins = [o for o in (a, s1, s2) if o is not None]
         if op1 is None:
-            vec(out, ins, lambda e: e.tensor_scalar(ap(out), ap(a), val(s1), None, op0), two(out, a))
+            work("v", out, ins, lambda e: e.tensor_scalar(ap(out), ap(a), val(s1), None, op0), two(out, a))
         else:
-            vec(out, ins, lambda e: e.tensor_scalar(ap(out), ap(a), val(s1), val(s2), op0, op1), two(out, a))
+            work("v", out, ins, lambda e: e.tensor_scalar(ap(out), ap(a), val(s1), val(s2), op0, op1), two(out, a))
 
-    def scan(out, a, b, op0, op1):
-        vec(out, [a, b], lambda e: e.tensor_tensor_scan(ap(out), ap(a), ap(b), 0.0, op0, op1), two(out, a, b))
-
-    def act(out, in_, func, bias=0.0, scale=1.0, acc=None):
+    def act(out, in_, func, bias=0.0, scale=1.0):
         kw = {}
-        if acc is not None:
-            kw["accum_out"] = ap(acc)
         if not (isinstance(bias, float) and bias == 0.0):
             kw["bias"] = val(bias)
         if not (isinstance(scale, float) and scale == 1.0):
             kw["scale"] = val(scale)
-        n = num(out)
-        cost = 65.0 + GAT * n * CYC if in_[0] == "@" else max(64.0, n) * CYC
-        rec("s", regs(in_) + regs(bias) + regs(scale), regs(out) + regs(acc), lambda e: e.activation(ap(out), ap(in_), func, **kw), cost)
+        work("s", out, [in_, bias, scale], lambda e: e.activation(ap(out), ap(in_), func, **kw), 1.0)
 
-    def mm(out, lhsT, rhs, start=True, stop=True):
-        rec("t", regs(lhsT) + regs(rhs), regs(out), lambda e: e.matmul(ap(out), ap(lhsT), ap(rhs), start, stop), max(64.0, num(out)) * PEC)
+    def mms(l):
+        since = fence.setdefault(l[0][0][0], [])
+        opens = l[0][3] and not l[-1][4]
+        i = rec("t", [o for m in l for o in m[1:3]], [m[0] for m in l],
+                [lambda e, m=m: e.matmul(ap(m[0]), ap(m[1]), ap(m[2]), m[3], m[4]) for m in l], sum(max(64.0, num(m[0])) * PEC for m in l),
+                extra=[(j, False) for j in (since if opens else since[:1])])
+        if l[-1][4] and not l[0][3]:
+            del since[:]
+        since.append(i)
 
-    def iota(out, pattern, mult):
-        rec("g", [], regs(out), lambda e: e.iota(ap(out), pattern, 0, mult, allow_small_or_imprecise_dtypes=True), 130.0 + 2 * num(out))
+    def iota(out, pattern, mult, base=0):
+        rec("g", [], regs(out), lambda e: e.iota(ap(out), pattern, base, mult, allow_small_or_imprecise_dtypes=True), 130.0 + 2 * CYC * num(out))
 
-    def pick(out, in_, pattern, base):
-        rec("g", regs(in_), regs(out), lambda e: e.affine_select(ap(out), ap(in_), pattern, A.is_equal, 0.0, base, 0), 170.0 + 2 * num(out))
+    def keep(out, in_):
+        rec("g", regs(in_), regs(out), lambda e: e.affine_select(ap(out), ap(in_), [[0, num(out)]], A.is_equal, 0.0, 0, 0), 170.0 + 2 * CYC * num(out))
 
-    def dma(q, out, in_, reads, writes, beside=False, us=2.5):
+    def dma(q, out, in_, reads, writes, beside=False, us=2.5, add=False, after=()):
         s = "d%d" % nd[0]
         nd[0] += 1
-        rec(q, reads, writes, lambda e: e.dma_start(out, in_), 70.0, 1000.0 * us, (s, 16), False, (), beside)
+        kw = {"accum_op": A.add} if add else {}
+        return rec(q, reads, writes, lambda e: e.dma_start(out, in_, **kw), 70.0, 1000.0 * us, (s, 16), False, [(j, False) for j in after], beside)
 
-    def arrive(o, s, v, mark):
-        rec(None, [], [o], None, 0.0, 0.0, (s, v), False, (marks[mark],))
+    def arrive(o, mark, v):
+        rec(None, [], [o], None, 0.0, 0.0, ("a" + mark, v), False, [(marks[mark], True)])
 
-    def send(o, out, topo, core, dst, rs, ls, mark):
+    def send(o, out, topo, core, dst, mark):
         rid, pid = topo.addr(dst)[0:2]
-        marks[mark] = rec("g", regs(o), [], lambda e: e.remote_dma(ap(out), ap(o), T.sem[rs], T.sem[ls], pid, rid, topo.mask(core, dst)),
-                          700.0, 3000.0, (ls, len(topo.engines(core, dst))), False)
+        marks[mark] = rec("g", regs(o), [], lambda e: e.remote_dma(ap(out), ap(o), T.sem["a" + mark], T.sem["l" + mark], pid, rid, topo.mask(core, dst)),
+                          SEND, FLY, ("l" + mark, len(topo.engines(core, dst))), False)
 
     def issue():
         n = len(ops)
-        succ, left = [[] for _ in ops], [len(op[2]) for op in ops]
+        cost, tail = [op[3] for op in ops], [op[4] for op in ops]
+        fwd, bwd = [[] for _ in ops], [[] for _ in ops]
         for i, op in enumerate(ops):
             for j in op[2]:
-                succ[j].append(i)
-        prio = [0.0] * n
-        for i in range(n - 1, -1, -1):
-            prio[i] = ops[i][3] + ops[i][4] + max([prio[j] + (WAKE if ops[j][2][i] else 0.0) for j in succ[i]] or [0.0])
-        free = {q: 0.0 for q in queues}
-        done, start = [0.0] * n, [0.0] * n
-        ready = {q: [] for q in queues}
-        seq = []
+                lag = cost[j] + ((tail[j] + (WAKE if op[0] else 0.0)) if op[2][j] else 0.0)
+                fwd[i].append((j, lag))
+                bwd[j].append((i, lag + cost[i] - cost[j]))
 
-        def put(i):
-            t = max([done[j] if ops[i][2][j] else start[j] for j in ops[i][2]] or [-1.0])
-            if ops[i][0] is None:
-                finish(i, t)
-            else:
-                ready[ops[i][0]].append((t, i))
+        def place(order, first, least):
+            at, busy = [0.0] * n, {q: [] for q in list(queues) + list(PSUM)}
+            for i in order:
+                t, q, c = max([at[j] + lag for j, lag in first[i]] + [least[i]]), ops[i][0], cost[i]
+                if q:
+                    t0 = -1.0
+                    while t0 < t:
+                        t0 = t
+                        for r, gap in [(q, 0.0)] + [(b, WAKE) for b in bank[i]]:
+                            b = busy[r]
+                            k = len(b)
+                            while k and b[k - 1][1] + gap > t:
+                                k -= 1
+                            while k < len(b) and b[k][0] < t + c + gap:
+                                if b[k][2] != q or not gap:
+                                    t = max(t, b[k][1] + gap)
+                                k += 1
+                    for r in [q] + bank[i]:
+                        b = busy[r]
+                        k = len(b)
+                        while k and b[k - 1][0] > t:
+                            k -= 1
+                        b.insert(k, (t, t + c, q))
+                at[i] = t
+            return at
 
-        def finish(i, t):
-            start[i], done[i] = t, t + ops[i][3] + ops[i][4]
-            seq.append(i)
-            for j in succ[i]:
-                left[j] -= 1
-                if left[j] == 0:
-                    put(j)
-        for i in range(n):
-            if not ops[i][2]:
-                put(i)
-        while len(seq) < n:
+        def ranked(rank):
+            order, seen = [], [False] * n
+            for i in sorted(range(n), key=lambda i: (rank[i], i)):
+                todo = [i]
+                while todo:
+                    j = todo[-1]
+                    miss = [k for k, _ in fwd[j] if not seen[k]]
+                    if miss:
+                        todo.append(min(miss))
+                    else:
+                        todo.pop()
+                        if not seen[j]:
+                            seen[j] = True
+                            order.append(j)
+            return order
+
+        def listed(rank, slack):
+            at, left, ready = [0.0] * n, [len(x) for x in fwd], {q: [] for q in queues}
+            free, held, todo = {q: 0.0 for q in queues}, {b: {} for b in PSUM}, [i for i in range(n) if not fwd[i]]
+            while True:
+                while todo:
+                    i = todo.pop()
+                    at[i] = max([at[j] + lag for j, lag in fwd[i]] or [0.0])
+                    if ops[i][0]:
+                        ready[ops[i][0]].append(i)
+                        continue
+                    for j, _ in bwd[i]:
+                        left[j] -= 1
+                        if not left[j]:
+                            todo.append(j)
+                best = None
+                for q in queues:
+                    if ready[q]:
+                        c = [(max([at[i], free[q]] + [held[b][r] + WAKE for b in bank[i] for r in held[b] if r != q]), i) for i in ready[q]]
+                        m = min(c)[0]
+                        i = min([(rank[i], i) for s, i in c if s == m])[1]
+                        s, i = min([(rank[j], s, j) for s, j in c if s <= m + slack * cost[i]])[1:]
+                        if best is None or s < best[0]:
+                            best = (s, q, i)
+                if best is None:
+                    return at
+                s, q, i = best
+                ready[q].remove(i)
+                at[i], free[q] = s, s + cost[i]
+                for b in bank[i]:
+                    held[b][q] = s + cost[i]
+                for j, _ in bwd[i]:
+                    left[j] -= 1
+                    if not left[j]:
+                        todo.append(j)
+
+        def rounds(order, m):
             best = None
-            for q in queues:
-                if not ready[q]:
-                    continue
-                c = [((free[q] if t < free[q] else t + WAKE), i) for t, i in ready[q]]
-                m = min(c)[0]
-                s, i = max([(prio[i], s, i) for s, i in c if s <= m + SLACK])[1:]
-                if best is None or s < best[0]:
-                    best = (s, q, i)
-            s, q, i = best
-            ready[q] = [e for e in ready[q] if e[1] != i]
-            free[q] = s + ops[i][3]
-            finish(i, s)
+            for r in range(m):
+                at = place(order, fwd, [0.0] * n)
+                end = max(at[i] + cost[i] + tail[i] for i in range(n))
+                if best is None or end < best[0]:
+                    best = (end, at)
+                if r < m - 1:
+                    back = place(sorted(range(n), key=lambda i: (-at[i] - cost[i], -i)), bwd, tail)
+                    order = sorted(range(n), key=lambda i: (-back[i] - cost[i], i))
+            return best
+        if DBG.get("only"):
+            DBG.update(place=place, rounds=rounds, ranked=ranked, listed=listed, fwd=fwd, bwd=bwd, cost=cost, tail=tail, ops=ops, bank=bank)
+            return
+        back = [0.0] * n
+        for i in range(n - 1, -1, -1):
+            back[i] = cost[i] + max([back[j] + lag - cost[j] for j, lag in bwd[i]] + [tail[i]])
+        at = listed([FIRST.get(DBG["rw"][i - n][0], 0.0) - CHAIN * back[i] for i in range(n)], SLACK)
+        best = (max(at[i] + cost[i] + tail[i] for i in range(n)), at)
+        if ROUNDS:
+            best = min(best, rounds(sorted(range(n), key=lambda i: (at[i], i)), ROUNDS))
+        if DBG.get("at"):
+            best = (0, DBG["at"])
+        DBG["end"] = best[0]
+        seq = sorted(range(n), key=lambda i: (best[1][i], i))
+        holder = {b: {} for b in PSUM}
+        for i in seq:
+            for b in bank[i]:
+                for q in holder[b]:
+                    if q != ops[i][0]:
+                        ops[i][2][holder[b][q]] = True
+                holder[b][ops[i][0]] = i
         clk, snap, final = {q: {} for q in queues}, {}, {}
         cnt, token = {"v": 0, "s": 0, "t": 0, "g": 0}, {}
 
@@ -246,7 +344,7 @@ def make(g, T):
                     clk[q][a] = snap[tok][a]
             clk[q][s] = v
         for i in seq:
-            q, call, deps, cost, tail, tok = ops[i]
+            q, call, deps, _, _, tok = ops[i]
             need = {}
             for j in deps:
                 if deps[j] and q is not None:
@@ -256,343 +354,377 @@ def make(g, T):
             if q is None:
                 snap[tok] = {}
             else:
-                ins = call(queues[q])
-                if tok is None:
-                    cnt[q] += 1
-                    tok = ("q_" + q, cnt[q])
-                    ins.then_inc(T.sem[tok[0]], 1)
-                elif tok[0][0] == "d":
-                    ins.then_inc(T.sem[tok[0]], 16)
+                own = tok is None
+                for one in (call if isinstance(call, list) else [call]):
+                    ins = one(queues[q])
+                    if own:
+                        cnt[q] += 1
+                        tok = ("q_" + q, cnt[q])
+                        ins.then_inc(T.sem[tok[0]], 1)
+                    elif tok[0][0] == "d":
+                        ins.then_inc(T.sem[tok[0]], 16)
                 snap[tok] = dict(clk[q])
             token[i] = tok
             final[tok[0]] = max(final.get(tok[0], 0), tok[1])
         for s in final:
             wait("g", (s, final[s]))
-    return cp, ms, tt, ts, scan, act, mm, iota, pick, dma, arrive, send, issue
+    return cp, ms, tt, ts, act, mms, iota, keep, dma, arrive, send, issue
 
 
 def rank_program(g, core, T, topo):
     rank = T.rank_of(core)
     if rank is None:
         return
-    cp, ms, tt, ts, scan, act, mm, iota, pick, dma, arrive, send, issue = make(g, T)
+    cp, ms, tt, ts, act, mms, iota, keep, dma, arrive, send, issue = make(g, T)
     ranks = len(T.cores)
+    lift = LIFT if ENG["bs"] == "s" else 0.0
 
-    def f(name, w=None, a=0):
+    def f(name, w=None, a=0, rows=128):
         full = LOC[name][2] if name in LOC else SCRATCH[name][1][1]
-        return (name, a, full if w is None else a + w)
+        return (name, a, full if w is None else a + w, 1, rows)
+
+    def st(name, a, end, by=LV):
+        return (name, a, end, by, 128)
 
     def sk(k, name="SK"):
-        return (name, 128 * k, 128 * k + 128)
+        return f(name, 128, 128 * k)
 
+    def mm(out, lhsT, rhs, start=True, stop=True):
+        mms([(out, lhsT, rhs, start, stop)])
+
+    def line(out, a, b):
+        ts(out, f("rp"), float(a), A.mult, float(b), A.add)
+
+    DBG["tag"] = (0, "in")
     dma("y", T.f0[:, :], T.fw[:, :], [], [f("f0")])
-    dma("y", T.la0[:, :], T.la[:, :], [], [f("la0")])
-    dma("y", T.z0[:, :], T.zz[:, :], [], [f("z0")])
-    dma("y", T.tI[:, :], T.th[:, :], [], [f("tI")])
+    dma("s", T.la0[:, :], T.la[:, :], [], [f("la0")])
+    dma("s", T.z0[:, :], T.zz[:, :], [], [f("z0")])
+    dma("s", T.tI[:, :], T.th[:, :], [], [f("tI")])
+    dma("y", T.X[:, PAD:PAD + W // 2], T.x[:, :W // 2], [], [f("X", W // 2, PAD)], False, 4.5)
+    ms(f("Fw"), 0.0)
+    ts(f("fc"), f("f0"), -2048.0, A.add)
+    cp(f("fh"), f("fc"))
+    d = dma("y", T.Fw[0:128:16, PAD:PAD + W], T.fh[:, :], [f("fh")], [f("Fw")])
+    tt(f("fl"), f("fc"), f("fh"), A.subtract)
+    d = dma("y", T.Fw[1:128:16, PAD:PAD + W], T.fl[:, :], [f("fl")], [f("Fw")], True)
+    dma("y", T.X[:, PAD + W // 2:PAD + W], T.x[:, W // 2:], [], [f("X", W // 2, PAD + W // 2)], False, 4.5, False, [d])
+    dma("y", T.Bi[:, :], T.bk[:, :], [], [f("Bi")], False, 6.0, False, [d])
+    cp(f("L0"), f("la0"))
     iota(f("pi"), [[0, 1]], 1)
-    iota(f("gq"), [[1, 8], [0, 16]], 0)
-    iota(f("rq2"), [[0, 16], [1, 16]], 0)
-    iota(f("rq"), [[0, 8], [1, 16]], 0)
+    iota(f("g16"), [[1, 8], [0, 16]], 0)
+    iota(f("q16"), [[0, 8], [1, 16]], 0)
     iota(f("s16"), [[1, 16]], 0)
-    iota(f("j16"), [[256, 16]], 0)
+    iota(f("g32"), [[1, 4], [0, 32]], 0)
+    iota(f("q32"), [[16, 2], [0, 8], [1, 16]], 0)
+    for a, n in PARTS:
+        iota(f("j16", n // 16, a // 16), [[ES, n // CL], [256, CL // 16]], 0)
     ts(f("pi2"), f("pi"), 15, A.bitwise_and)
     ts(f("pi3"), f("pi"), 4, A.arith_shift_right)
     cp(f("rp"), f("pi2"))
-    cp(f("gp"), f("pi3"))
-    ts(f("cSf"), f("gq"), f("gp"), A.is_equal)
-    cp(f("cS"), f("cSf"))
+    cp(f("p16"), f("pi3"))
+    ts(f("tmp"), f("g16"), f("p16"), A.not_equal, -100.0, A.mult)
+    tt(f("code"), f("tmp"), f("q16"), A.add)
+    line(f("wc"), 14, 39)
+    line(f("wu"), 10, 5)
     for k in range(LV):
-        pick(sk(k), f("cS"), [[0, 8], [1, 16]], -k)
-    ms(f("Fw"), 0.0)
-    for k in range(16):
-        act(f("zm", 256, 256 * k), f("rq2"), AF.Identity, 1.0, 0.0)
-    for k in range(8):
-        act(f("zsp", 256, 256 * k), f("rq2"), AF.Identity, 0.0, 0.0)
-    ts(f("fc"), f("f0"), -2048.0, A.add)
-    cp(f("fh"), f("fc"))
-    dma("y", T.Fw[0:128:16, PAD:PAD + W], T.fh[:, :], [f("fh")], [f("Fw")])
-    tt(f("fl"), f("fc"), f("fh"), A.subtract)
-    dma("y", T.Fw[1:128:16, PAD:PAD + W], T.fl[:, :], [f("fl")], [f("Fw")], True)
-    dma("y", T.Bt[:, PAD:PAD + C], T.bk[:, :], [], [f("Bt", C, PAD)], False, 4.0)
-    dma("y", T.X[:, PAD:PAD + W], T.x[:, :], [], [f("X", W, PAD)], False, 7.0)
-    cp(f("L0"), f("la0"))
-    ms(f("zsp", 2048, 2048), 0.0)
-    ms(("zm", 0, W, LV), 0.0)
-    ts(f("tmp"), f("gq"), f("gp"), A.not_equal, 100.0, A.mult)
-    tt(f("code"), f("tmp"), f("rq"), A.add)
-    ts(f("m0"), f("rp"), 0.0, A.is_equal)
-    ts(f("zc"), f("rp"), 10.0, A.mult, 5.0, A.add)
-    ts(f("zc2"), f("rp"), 4.0, A.mult, 34.0, A.add)
-    ts(f("tmp4"), f("code"), 0.0, A.is_equal, f("zc2"), A.mult)
-    ts(f("tmp2"), f("cSf"), f("zc"), A.mult)
-    tt(f("cZ"), f("tmp4"), f("tmp2"), A.add)
-    ts(f("cSb"), f("cSf"), f("m0"), A.mult)
-    ts(f("mask"), f("rq2"), f("rp"), A.is_equal)
-    ts(f("dd", 16), f("s16"), f("gp"), A.is_equal)
-    ts(f("s8"), f("s16"), -8.0, A.add)
-    ts(f("dd", 16, 16), f("s8"), f("gp"), A.is_equal)
-    ts(f("cSbn"), f("cSb"), -1.0, A.mult)
-    ts(f("m1"), f("rp"), 1.0, A.is_equal, 0.03125, A.mult)
-    ts(f("cS1"), f("cSf"), f("m1"), A.mult)
-    ts(f("MSK"), f("rq2"), f("rp"), A.is_le, 16384.0, A.mult)
-    ts(f("idn"), f("code"), f("rp"), A.is_equal)
-    cp(f("cI"), f("idn"))
-
-    def late_constants():
-        ts(f("cSr"), f("cSf"), f("rp"), A.mult)
-        for k in range(LV):
-            pick(sk(k, "MK"), f("cSr"), [[0, 8], [1, 16]], -k)
-        ts(f("cI8"), f("idn"), 8192.0, A.mult)
-        ts(f("cSn"), f("cSf"), -1.0, A.mult)
-        ts(f("cS4"), f("cSf"), 4096.0, A.mult)
-        ts(f("cS4n"), f("cSf"), -4096.0, A.mult)
-        ts(f("cSq"), f("cSf"), -256.0, A.mult)
-        ts(f("C4"), f("cSf"), -0.5, A.mult)
-        ts(f("tmp3"), f("rq"), f("rp"), A.is_ge)
-        tt(f("tr"), f("tmp3"), f("cSf"), A.mult)
-        ts(f("C1"), f("tr"), 131072.0, A.mult)
-        ts(f("C3"), f("tr"), -0.5, A.mult)
-        ts(f("tmp2"), f("idn"), 1.5, A.mult)
-        tt(f("tmp"), f("tmp2"), f("tr"), A.subtract)
-        cp(f("C2"), f("tmp"))
-        ts(f("m15"), f("rp"), 15.0, A.is_equal, 0.5, A.mult)
-        ts(f("tmp5"), f("code"), 15.0, A.is_equal, f("m15"), A.mult)
-        tt(f("C2f"), f("tmp"), f("tmp5"), A.subtract)
-        ts(f("c01"), f("code"), 1.0, A.is_le)
-        ms(f("ones"), 1.0)
-        ts(f("zc3"), f("rp"), 16.0, A.mult)
-        ts(f("J16"), f("j16"), f("zc3"), A.add)
-        ts(f("c613"), f("rp"), 613.0, A.mult, -15.5 / 32, A.add)
-        ts(f("bG"), f("rp"), -1.0, A.mult, 0.5, A.add)
-        tt(f("bY"), f("bG"), f("m15"), A.add)
-        ts(f("bM"), f("rp"), -1.5, A.mult)
-        ts(f("Tn"), f("tI"), -1.0, A.mult, -0.5, A.add)
-        ts(f("Tp"), f("tI"), 0.5, A.add)
-        cp(f("thr"), f("Tn"))
-
-    def keys_t(prods, pb, null=False):
-        for h in range(2):
-            if null:
-                mm(f(pb, 128, 128 * h), f("ones", 128), f("cSq"), True, False)
-            for i, (rows, sel, nsel) in enumerate(prods):
-                mm(f(pb, 128, 128 * h), f(rows, 128, 128 * h), f(sel), i == 0 and not null, i == len(prods) - 1)
-
-    def diff(prods, wt, pb):
-        mm(f(pb, 256, 256), f("cI"), f("MSK"), True, False)
-        for rows, sel, nsel in prods:
-            mm(f(pb, 256, 256), f(nsel), f(rows), False, False)
-        for h in range(2):
-            mm(f(pb, 128, 256 + 128 * h), f(wt, 128, 128 * h), f("cS"), False, h == 1)
-
-    def mylist(wt, pb, a, stop):
-        for h in range(2):
-            mm(f(pb, 16, a), f(wt, 128, 128 * h), f("dd", 16, 16 * h), h == 0, stop and h == 1)
-
-    def lost(em, pb):
-        for r in range(16):
-            mm(f(pb, 16), sk(r), (em, r, K, 16), False, r == 15)
-
-    def eqs(em, pb, null=0.0):
-        ts(f(em), f(pb, 256, 256), null, A.is_equal, -8192.0, A.mult)
-
-    def offs(of, pb, c):
-        ts((of, 0, 31, 2), f(pb, 16), c, A.add, f("rp"), A.max)
-
-    def scatter(tab, of, data):
-        for s in range(15, -1, -1):
-            cp(("@", f(tab), (of, 2 * s, 2 * s + 1)), f(data, 16, 16 * s))
+        ts(sk(k), f("code"), float(k), A.is_equal)
+    act(f("SKc"), f("SK"), AF.Identity, 0.0, f("wc"))
+    ts(f("Bt", C, PAD), f("Bi"), lift, A.add)
+    DBG["tag"] = (0, "k1")
+    for k in range(LV):
+        ts(sk(k, "SKu"), f("code"), float(k), A.is_equal, f("wu"), A.mult)
+    for h in range(2):
+        ts(f("cS", 128, 128 * h), f("code"), 0.0, A.is_ge)
+    ts(f("I"), f("code"), f("rp"), A.is_equal)
+    ts(f("tr"), f("code"), f("rp"), A.is_ge)
+    ts(f("oh"), f("s16"), f("rp"), A.is_equal)
+    for k in range(LV):
+        ts(sk(k, "SEL"), f("cS", 128), f("oh", 1, k), A.mult)
+    DBG["tag"] = (0, "k2")
+    tt(f("code2"), f("cS", 128), f("I"), A.add)
+    ts(f("da"), f("s16"), f("rp"), A.not_equal, 1.0, A.add)
+    ts(f("db"), f("s16"), f("rp"), A.not_equal, -0.5, A.add)
+    ts(f("la"), f("s16"), f("rp"), A.max)
+    ts(f("lb"), f("s16"), f("rp"), A.not_equal, -BIG / 2, A.mult)
+    for k in range(LV):
+        ts(sk(k, "DF"), f("code2"), f("da", 1, k), A.is_equal, f("db", 1, k), A.mult)
+        ts(sk(k, "LOST"), f("code"), f("la", 1, k), A.is_equal, f("lb", 1, k), A.mult)
+    DBG["tag"] = (0, "k3")
+    for n, m, s in (("In", "I", -1), ("I32", "I", 32), ("Ih", "I", 0.5), ("Iq", "I", -BIG / 2), ("I8", "I", BIG),
+                    ("C1", "tr", 2 ** 22), ("C3B", "tr", -BIG / 2), ("C3", "tr", -0.5), ("cQ", "cS", -1 / 64), ("c256", "cS", -256),
+                    ("t1", "I", 2 ** 16)):
+        ts(f(n), f(m, 128), float(s), A.mult)
+    tt(f("Cc"), f("C1"), f("t1"), A.add)
+    ts(f("t2"), f("code"), f("rp"), A.is_gt, -BIG, A.mult)
+    tt(f("C2B"), f("t2"), f("Iq"), A.subtract)
+    ts(f("n15"), f("rp"), 15.0, A.not_equal)
+    ts(f("C2f"), f("C2B"), f("n15"), A.mult)
+    ts(f("wv"), f("oh", 1), 255.75, A.mult, -256.0, A.add)
+    ts(f("cV"), f("cS", 128), f("wv"), A.mult)
+    tt(f("HM"), sk(0), sk(1), A.subtract)
+    ms(f("c75"), -15 * NULL / BIG)
+    ms(f("ones"), 1.0)
+    ts(f("pi4"), f("pi"), 31, A.bitwise_and)
+    ts(f("pi5"), f("pi"), 5, A.arith_shift_right)
+    cp(f("r32"), f("pi4"))
+    cp(f("p32"), f("pi5"))
+    for b in sorted(set(BLOCK.values())):
+        r, s = f("rp" if b == 16 else "r32"), "%d" % b
+        ts(f("mT" + s), f("q" + s), r, A.is_le, -15 * NULL / BIG, A.add)
+        ts(f("mR" + s), f("q" + s), r, A.is_equal)
+        ts(f("bk" + s), f("g" + s), f("p" + s), A.is_equal, -1.0, A.mult)
+        ts(f("dd" + s), f("s16"), f("p" + s), A.is_equal)
+    line(f("rp1"), 1, 16)
+    line(f("r16"), 16, 0)
+    ts(f("J"), f("j16"), f("r16"), A.add)
+    line(f("c613"), 613 * 32, 0)
+    line(f("bW0"), -BIG, -BIG / 2)
+    ts(f("bW"), f("oh", 1, 15), BIG / 2, A.mult, f("bW0"), A.add)
+    line(f("bH"), -1.5 * BIG, -BIG)
+    ts(f("wN"), f("oh", 1, 15), BIG - 1, A.mult, 1.0, A.add)
+    line(f("bN0"), -0.5, 0.5)
+    ts(f("bN"), f("bN0"), f("wN"), A.mult)
+    ts(f("bhm"), f("oh", 1), -15 * NULL, A.mult)
+    ts(f("blo"), f("oh", 1, 1), -15 * NULL, A.mult)
+    ts(f("Tn"), f("tI"), -1.0, A.mult, -0.5, A.add)
+    ts(f("Tp"), f("tI"), 0.5 - BIG / 2, A.add)
+    cp(f("thr"), f("Tn"))
+    for c in range(NCH):
+        ms(f("E", 16, ES * c + CE), 0.0)
+    DBG["tag"] = (0, "k4")
+    iota(f("Ff"), [[0, PAD + W]], 0, 2048)
 
     FW, XW = f("Fw", W, PAD), f("X", W, PAD)
-    pb = [("bu", "cSb", "cSbn")]
-    pw = [("Vw", "cS", "cSn")]
-    ph = [("Vh", "cS", "cSn"), ("mg", "cS4", "cS4n")]
 
-    def pf(c):
-        return 512 * (c % 2) + CL * (c // 2)
+    def ent(name, c):
+        return f(name, CE, (ES if name == "E" else CE) * c)
 
-    def turn(out, src, c, stop=True):
-        for k in range(LV):
-            mm(out, sk(k), (src, CE * c + k, CE * (c + 1), LV), k == 0, stop and k == LV - 1)
+    def copy(e, out, in_):
+        if e == "s":
+            act(out, in_, AF.Copy)
+        elif e == "v":
+            cp(out, in_)
+        else:
+            keep(out, in_)
 
-    def step(s, v, L, z, last, dst):
-        c = int(s[2]) if len(s) == 3 and s[2] in "0123" else 0
-        zs, nx = "zs%d" % (v + 1), "%d" % (v + 1)
-        lanes, ents = CL * c, f("z16", CE, CE * c)
-        k = s[:2]
-        if k == "fg":
-            act(f("FG", CE, CE * c), ("@", FW, f(L, CL, lanes)), AF.Copy)
+    def turn(out, srcs, c, stop=True):
+        for i, src in enumerate(srcs):
+            a = ent(src, c)[1]
+            mms([(out, sk(k), st(src, a + k, a + CE), i == 0 and k == 0, stop and k == LV - 1 and i == len(srcs) - 1) for k in range(LV)])
+
+    def ps(name, lane, n, at=None, rows=128):
+        b, a = PLACE[name]
+        return f(PSUM[4 * (lane // 128) + b], n, a + (lane % 128 if at is None else at), rows)
+
+    def each(o, r, by=LV):
+        return (o[0], o[1] + r, o[2], by, o[4])
+
+    def sizes(e, src, dst, c):
+        if e == "s":
+            act(ent(dst, c), ent(src, c), AF.Abs)
+            return [dst]
+        ts(ent(dst, c), ent(src, c), 0.0, A.min, -2.0, A.mult)
+        return [src, dst]
+
+    def wrap(out, fam, src, a, n, start=True):
+        mms([(out, sk(r, fam), st(src, a + r, a + n), start and r == 0, r == LV - 1) for r in range(LV)])
+
+    def offs(tab, p, a, n, c):
+        if BLOCK.get(tab) == 32:
+            for h in range(2):
+                ts(st("of" + tab, a // 16 + h, (a + n) // 16, 2), st(p[0], p[1] + h, p[2], 2), c, A.add, f(("rp", "rp1")[h]), A.max)
+        else:
+            ts(st("of" + tab, a // 8, (a + n) // 8 - 1, 2), p, c, A.add, f("rp"), A.max)
+
+    def contest(tab, rows, a, n):
+        b = BLOCK[tab]
+        s, w, m = "%d" % b, 8 * b, b // 16
+        key, dif, lst = ps("key" + tab, a, w, 0, n), ps("dif" + tab, a, w, 0, n), ps("lst" + tab, a, n // 16, a % 128 // 16)
+        wt, eq = f("WT" + tab, w, 0, n), f("eq" + tab, w, 0, n)
+        mms([(key, f("I8", n), f("c75", w), True, False), (key, rows, f("cS", w), False, True)])
+        mms([(dif, f("I8", n), f("mT" + s), True, False), (dif, rows, f("cS", w), False, False)])
+        tt(wt, key, f("mR" + s, w, 0, n), A.mult)
+        mm(dif, f("bk" + s, n, 0, n), wt, False, True)
+        ts(eq, dif, 0.0, A.is_equal, -BIG, A.mult)
+        mms([(each(lst, h, m), f(x + tab, 128, 128 * h, n), f("dd" + s, n // b, 0, n), x == "WT", x == "eq")
+             for h in range(m) for x in ("WT", "eq")])
+        offs(tab, lst, a, n, float(2048 + PAD))
+
+    def scatter(tab, of, data, a, n, e="v"):
+        b = BLOCK.get(of, 16)
+        for s in range((a + n) // b - 1, a // b - 1, -1):
+            out = ("@", f(tab), f("of" + of, b // 16, 2 * s))
+            if e == "s":
+                act(out, f(data, b, b * s), AF.Silu)
+            else:
+                cp(out, f(data, b, b * s))
+
+    def step(s, v):
+        L, z, nx = "L%d" % v, "z%d" % v, "%d" % (v + 1)
+        last = v == VIS - 1
+        dst = T.cores[(rank + 1 + v % (ranks - 1)) % ranks]
+        k, c = s[:2], int(s[2:] or 0)
+        a = 128 * c
+
+        def ln(name, b=0):
+            return f(name, 128, a + b)
+
+        def pl(name):
+            return ps(name, a, 128)
+        if k == "cp":
+            dma("y", T.X2[:, PAD:PAD + W], T.X[:, PAD:PAD + W], [XW], [f("X2", W, PAD)], False, 7.0)
+            for d in range(2):
+                for a in (PAD, PAD + W // 2):
+                    dma("g", T.Ff[0:128:16, a:a + W // 2], T.Fw[d:128:16, a:a + W // 2], [f("Fw"), f("Ff", W // 2, a)], [f("Ff", W // 2, a)], False, 3.0, True)
+        elif k == "fg":
+            copy(ENG["fg"][c], ent("FG", c), ("@", FW, f(L, CL, CL * c)))
         elif k == "fh":
-            act(f("FH", CE, CE * c), ("@", FW, f("Bb", CL, lanes)), AF.Copy)
-        elif k == "zb":
-            mm(f("pX", 256), f("cZ"), f(z))
-            ts(f("i1"), f("pX", 256), 255.0, A.add)
-            ts(f("i2"), f("i1"), 1023, A.bitwise_and)
-            cp(f("bu"), f("i2"))
-            keys_t(pb, "pC")
-            cp(("zsp", 0, W, LV), f(z))
-            tt(f("WTb"), f("pC", 256), f("mask"), A.mult)
-            mylist("WTb", "pC", 16, True)
-            cp(f("bl"), f("pC", 16, 16))
-            cp(f("Bb"), ("@", f("Bt", C, PAD), f("bl")))
-            diff(pb, "WTb", "pC")
-            mm(f("pX", 256, 256), f("cS1"), f("bu"))
-        elif k == "sc":
-            for c in range(NCH):
-                scan(f("z16", CE, CE * c), f("zm", CE, CE * c), f("zsp", CE, CE * c), A.mult, A.add)
-        elif k == "eb":
-            eqs("Emb", "pC")
-        elif k == "ob":
-            mylist("WTb", "pC", 0, False)
-            lost("Emb", "pC")
-            offs("ofb", "pC", float(PAD))
-        elif s == "flf":
-            act(f("FLf"), f("FLc"), AF.Identity, 2048.0)
-            if v == 0:
-                late_constants()
-        elif k == "xl":
-            turn(f("pF", CL, pf(c)), "FG", c)
-        elif k == "ul":
-            ts(f("FLu", CL, lanes), f("pF", CL, pf(c)), 2048.0, A.add)
-            cp(f("FLc", CL, lanes), f("pF", CL, pf(c)))
-            tt(f("D", CE, CE * c), ("@", XW, f("FLu", CL, lanes)), ents, A.subtract)
-        elif k == "xg":
-            turn(f("pF", CL, pf(NCH + c)), "FH", c)
-        elif k == "ug":
-            p = f("pF", CL, pf(NCH + c))
-            ts(f("Gu", CL, lanes), p, 2048.0, A.add)
-            tt(f("eq", CL, lanes), p, f("FLc", CL, lanes), A.is_equal)
-            tt(f("pH", CL, lanes), p, f("FLc", CL, lanes), A.max)
-            tt(f("pH", CL, 256 + lanes), p, f("FLc", CL, lanes), A.min)
-            tt(f("E", CE, CE * c), ("@", XW, f("Gu", CL, lanes)), ents, A.subtract)
-        elif k == "da":
-            act(f("DA", CE, CE * c), f("D", CE, CE * c), AF.Abs)
-        elif k == "sd":
-            turn(f("pd", CL, lanes), "DA", c)
-        elif k == "ea":
-            act(f("EA", CE, CE * c), f("E", CE, CE * c), AF.Abs)
-        elif k == "se":
-            turn(f("pe", CL, lanes), "EA", c, False)
-            mm(f("pe", CL, lanes), f("cI8"), f("eq", CL, lanes), False, True)
-        elif k == "df":
-            act(f("fs"), f("pd", 256), AF.Sign, f("thr"))
-            mm(f("pC", 256), f("C1"), f("ones"), True, False)
-            mm(f("pC", 256), f("C1"), f("fs"), False, True)
-            mm(f("pd", 256, 256), f("C2f"), f("fs"))
-            act(f("pd", 256), f("pd", 256, 256), AF.Relu, f("bY"))
-        elif k == "nn":
-            mm(f("pd", 256, 256), f("C4"), f("fs"))
-            act(f("pd", 256, 256), f("pd", 256, 256), AF.Relu, -7.0)
-        elif k == "nw":
-            tt(f("r1"), f("pX", 256, 256), f("FLf"), A.mult)
-            ts(f("r2"), f("r1"), f("c613"), A.add)
-            tt(f("pC", 256, 256), f("pC", 256), f("r2"), A.min)
-            tt(f("sn"), f("pC", 256, 256), f("FLf"), A.add)
-            ts(f("new"), f("sn"), 4095, A.bitwise_and)
-        elif k == "sl":
-            if last:
-                cp(f("ylo"), f("new"))
-                dma("y", T.yl[:, :], T.ylo[:, :], [f("ylo")], [])
-            else:
-                cp(f("Ls" + nx), f("new"))
-                send(f("Ls" + nx), f("L" + nx), topo, core, dst, "aL" + nx, "lL" + nx, "L" + nx)
-        elif k == "wv":
-            ts(f("nC"), f("new"), -2048.0, A.add)
-            tt(f("Vw"), f("pd", 256), f("nC"), A.mult)
-        elif k == "wm":
-            keys_t(pw, "pX")
-            tt(f("WTw"), f("pX", 256), f("mask"), A.mult)
-            diff(pw, "WTw", "pX")
-            mylist("WTw", "pX", 0, False)
-        elif k == "we":
-            eqs("Emw", "pX")
-        elif k == "wl":
-            lost("Emw", "pX")
-        elif k == "wo":
-            offs("ofw", "pX", float(2048 + PAD))
-        elif k == "eg":
-            act(f("gs"), f("pe", 256), AF.Sign, f("Tp"), -1.0)
-            mm(f("pS", 256, 256), f("C3"), f("fs"), True, False)
-            mm(f("pS", 256, 256), f("C2"), f("gs"), False, True)
-            act(f("mg"), f("pS", 256, 256), AF.Relu, f("bM"), 1.0, f("Aac"))
-            mm(f("pS", 256), f("C2"), f("gs"))
-            act(f("fg"), f("pS", 256), AF.Relu, f("bG"))
-        elif k == "h1":
-            tt(f("Vh"), f("pH", 256), f("mg"), A.mult)
-        elif k == "hk":
-            keys_t(ph, "pC", True)
-        elif k == "zi":
-            mm(f("pF", 16, 256), f("cI"), f("J16"), True, False)
-            for r in range(16):
-                mm(f("pF", 16, 256), sk(r, "MK"), ("fg", r, K, 16), False, r == 15)
-            mm(f("pF", 256), f("cS"), f("fg"))
+            copy(ENG["fh"][c], ent("FH", c), ("@", FW, f("Bb", CL, CL * c)))
         elif k == "zz":
-            cp(f("idx"), f("pF", 16, 256))
-            ts(f("zh"), ("@", f("E"), f("idx")), 0.5, A.mult, -0.25, A.add)
-            tt(f("pF", 256, 256), f("pF", 256), f("zh"), A.mult)
-            tt(f(zs), f("pF", 256, 256), f(z), A.add)
-            if last:
-                dma("y", T.yz[:, :], T[zs][:, :], [f(zs)], [])
+            for i in range(LV):
+                copy(ENG["zz"][c][i % len(ENG["zz"][c])], st("z16", LV * a + i, LV * (a + 128)), ln(z))
+        elif k == "ce":
+            b = 16 * c
+            wrap(each(ps("cu", a, 16), 0, 2), "SKc", z, a, 128)
+            wrap(each(ps("cu", a, 16), 1, 2), "SKu", z, a, 128)
+            ts(f("i1", 16, b), ps("cu", a, 16), 255.0, A.add)
+            ts(f("i2", 16, b), f("i1", 16, b), 1023, A.bitwise_and)
+            cp(f("bl", 8, 8 * c), st("i2", b, b + 16, 2))
+            ts(ln("Bb"), ("@", f("Bt", C, PAD), f("bl", 8, 8 * c)), 0.25 - lift, A.add)
+            ts(f("bu", 16, b), f("i2", 16, b), 32.0, A.add)
+            mms([(each(ps("ub", a, 128), r), sk(r, "SEL"), st("bu", b + 1, b + 16, 2), True, True) for r in range(LV)])
+        elif k == "cb":
+            keys = st("bu", 0, 32, 2)
+            dif, lst = ps("difB", 128, K), ps("lstB", 128, 16)
+            mms([(each(dif, r), sk(r, "DF"), keys, True, True) for r in range(LV)])
+            act(f("sgb"), dif, AF.Sign, 0.25)
+            mms([(lst, f("I"), keys, True, False)] + [(lst, sk(r, "LOST"), st("sgb", r, K), False, r == LV - 1) for r in range(LV)])
+            offs("B", lst, 0, K, float(PAD - 32))
+        elif k == "xl":
+            turn(ps("FL", CL * c, CL), ["FG"], c)
+            ts(f("FLu", CL, CL * c), ps("FL", CL * c, CL), 2048.0, A.add)
+            tt(ent("D", c), ("@", XW, f("FLu", CL, CL * c)), ent("z16", c), A.subtract)
+        elif k == "fl":
+            act(ln("FLf"), pl("FL"), AF.Identity, 2048.0)
+            ts(ln("FLc"), ln("FLu"), -2048.0, A.add)
+        elif k == "yy":
+            tt(ln("y1"), pl("ub"), ln("FLf"), A.mult)
+            if ENG["y2"][c] == "s":
+                act(ln("y2"), ln("y1"), AF.Identity, f("c613"))
             else:
-                send(f(zs), f("z" + nx), topo, core, dst, "aZ" + nx, "lZ" + nx, "Z" + nx)
-        elif k == "h2":
-            tt(f("WTh"), f("pC", 256), f("mask"), A.mult)
-            diff(ph, "WTh", "pC")
-            mylist("WTh", "pC", 0, False)
-        elif k == "h3":
-            eqs("Emh", "pC", -4096.0)
-            lost("Emh", "pC")
-        elif k == "h4":
-            offs("ofh", "pC", float(PAD + 2048))
-        elif k == "l1":
-            tt(f("Vl"), f("pH", 256, 256), f("mg"), A.mult)
-        elif k == "lm":
-            mm(f("pF", 256, 768), f("c01"), f("Vl"))
-            if last:
-                ts(f("lof"), f("pF", 256, 768), 2048.0, A.add)
-            else:
-                act(f("hm"), f("pF", 256, 768), AF.Identity, 0.0, f("m0"))
-        elif k == "l2":
-            tt(f("lod"), f("pF", 256, 768), f("hm"), A.subtract)
-        elif k == "ff":
-            for b in (2 * c, 2 * c + 1):
-                bank = ("pd", "pX")[b % 2]
-                mm(f(bank), f("cS"), f("Fw", 512, PAD + 512 * b))
-                act(f("Ff", 512, PAD + 512 * b), f(bank), AF.Identity, 2048.0)
+                ts(ln("y2"), ln("y1"), f("c613"), A.add)
+        elif k == "da":
+            turn(ps("d", CL * c, CL), sizes(ENG["da"][c], "D", "DA", c), c)
+        elif k == "xg":
+            turn(ps("G", CL * c, CL), ["FH"], c)
+            ts(f("Gu", CL, CL * c), ps("G", CL * c, CL), 2048.0, A.add)
+            tt(ent("E", c), ("@", XW, f("Gu", CL, CL * c)), ent("z16", c), A.subtract)
+        elif k == "hl":
+            tt(ln("hiC"), pl("G"), ln("FLc"), A.max)
+            tt(ln("loC"), pl("G"), ln("FLc"), A.min)
+            mms([(pl("dl"), f("I"), ln("hiC"), True, False), (pl("dl"), f("In"), ln("loC"), False, True)])
+            act(ln("nq"), pl("dl"), AF.Sign, -0.5)
         elif k == "fs":
+            act(ln("fs"), pl("d"), AF.Sign, f("thr"))
+        elif k == "nw":
+            mms([(pl("M"), f("I32"), ln("FLc"), True, False), (pl("M"), f("Cc"), ln("ones"), False, False), (pl("M"), f("C1"), ln("fs"), False, True)])
+            tt(ln("rr"), pl("M"), ln("y2"), A.min)
+            ts(ln("new"), ln("rr"), 5, A.arith_shift_right, 4095, A.bitwise_and)
+            ts(ln("nC"), ln("new"), -2048.0, A.add)
             if last:
-                scatter("Ff", "ofh", "lof")
-                dma("y", T.yf[:, :], T.Ff[0:128:16, PAD:PAD + W], [f("Ff")], [])
+                ts(ln("ylo"), ln("nC"), 2048.0, A.add)
+                dma("y", T.yl[:, a:a + 128], T.ylo[:, a:a + 128], [ln("ylo")], [])
             else:
-                scatter("Fw", "ofh", "lod")
+                ts(ln("Ls" + nx), ln("nC"), 2048.0, A.add)
+                send(ln("Ls" + nx), ln("L" + nx), topo, core, dst, "L%d_%s" % (c, nx))
+        elif k == "cw":
+            mms([(pl("Pw"), f("I"), ln("nC"), True, False), (pl("Pw"), f("C2f"), ln("fs"), False, True)])
+            ts(ln("Vw"), pl("Pw"), f("bW"), A.add, NULL, A.max)
+            contest("X", ln("Vw"), a, 128)
+        elif k == "vq":
+            mms([(pl("Q"), f("I"), ln(z), True, False), (pl("Q"), f("Ih"), st("D", LV * a + 15, LV * (a + 128)), False, False),
+                 (pl("Q"), f("cV"), ln("ones"), False, False), (pl("Q"), f("c256"), ln("fs"), False, True)])
+            tt(ln("vq"), pl("Q"), ln(z), A.max)
+            ts(ln("val"), ln("vq"), 255, A.bitwise_and)
         elif k == "bs":
-            scatter("Bt", "ofb", "new")
-            if last:
-                cp(f("ybo"), f("Bt", C, PAD))
-                dma("y", T.yb[:, :], T.ybo[:, :], [f("ybo")], [], False, 4.5)
-        elif k == "hv":
-            ts(f("hd"), ("D", 15, W, LV), 0.5, A.mult, -0.25, A.add)
-        elif k == "vv":
-            tt(f("pd", 256, 256), f("pd", 256, 256), f("hd"), A.mult)
-            tt(f("val"), f("pd", 256, 256), f(z), A.add)
+            if lift:
+                ts(ln("newf"), ln("new"), lift, A.add)
+            scatter("Bt", "B", "newf" if lift else "new", a, 128, ENG["bs"])
+            if last and c == 0:
+                if lift:
+                    ts(f("ybo"), f("Bt", C, PAD), ROUND - lift, A.add, -ROUND, A.add)
+                    dma("y", T.yb[:, :], T.ybo[:, :], [f("ybo")], [], False, 4.5)
+                else:
+                    dma("y", T.yb[:, :], T.Bt[:, PAD:PAD + C], [f("Bt")], [], False, 4.5)
         elif k == "xs":
-            scatter("X", "ofw", "val")
-            if last:
-                dma("s", T.yx[:, :], T.X[:, PAD:PAD + W], [f("X", W, PAD)], [], False, 7.0)
+            scatter("X2" if last else "X", "X", "val", a, 128)
+            if last and c == 0:
+                dma("s", T.yx[:, :], T.X2[:, PAD:PAD + W], [f("X2")], [], False, 7.0)
+        elif k == "ea":
+            turn(ps("e", CL * c, CL), sizes(ENG["ea"][c], "E", "EA", c), c, False)
+            mm(ps("e", CL * c, CL), f("Iq"), f("nq", CL, CL * c), False, True)
+        elif k == "gs":
+            act(f("gs", PARTS[c][1], PARTS[c][0]), ps("e", *PARTS[c]), AF.Sign, f("Tp"), -1.0)
+        elif k == "mg":
+            merge(c, PARTS[c][0], PARTS[c][1], last)
+        elif k == "zp":
+            point(c, PARTS[c][0], PARTS[c][1], z, nx, last, dst)
         elif k == "aa":
-            mm(f("pS", 1, 256), f("cSf"), f("Aac"))
-            cp(f("a1"), f("pS", 1, 256))
+            mms([(ps("aa", 128, 1), f("sgc", 128, 128 * p, n), f("ones", 1, 0, n), p == 0, p == len(PARTS) - 1) for p, (a, n) in enumerate(PARTS)])
+            ts(f("a1"), ps("aa", 128, 1), 0.5, A.mult, K / 2.0, A.add)
             ts(f("a2"), f("a1"), 15, A.bitwise_and)
             tt(f("thr"), f("Tn"), f("a2"), A.subtract)
 
+    def merge(p, a, n, last):
+        def ln(name, b=0):
+            return f(name, n, a + b)
+        hi, lo = ps("Ph", a, n), ps("Pl", a, n)
+        mms([(hi, f("I"), ln("hiC"), True, False), (hi, f("C3B"), ln("fs"), False, False)])
+        mm(hi, f("C2B"), ln("gs"), False, True)
+        mms([(lo, f("I"), ln("loC"), True, False), (lo, f("C3B"), ln("fs"), False, False), (lo, f("C2B"), ln("gs"), False, True)])
+        ts(ln("Vh"), hi, f("bH"), A.add, NULL, A.max)
+        contest("F", ln("Vh"), a, n)
+        ts(ln("Vl"), lo, f("bH"), A.add, NULL, A.max)
+        mm(lo, sk(0), ln("Vl"))
+        if last:
+            act(ln("lof"), lo, AF.Identity, 2048 - 15 * NULL)
+            scatter("Ff", "F", "lof", a, n)
+            if a == 0:
+                dma("y", T.yf[:, :], T.Ff[0:128:16, PAD:PAD + W], [f("Ff")], [])
+        else:
+            act(ln("hm"), lo, AF.Identity, f("bhm"))
+            mms([(lo, sk(1), ln("Vl"), True, False), (lo, f("HM"), ln("hm"), False, True)])
+            act(ln("lod"), lo, AF.Identity, f("blo"))
+            scatter("Fw", "F", "lod", a, n)
+            DBG["tag"] = (DBG["tag"][0], "aa")
+            act(f("sgc", 128, 128 * p, n), ps("keyF", a, 128, 0, n), AF.Sign, 3000.0)
+
+    def point(p, a, n, z, nx, last, dst):
+        def ln(name, b=0):
+            return f(name, n, a + b)
+        zs, s0, ns = "zs" + nx, a // 16, n // 16
+        ix, pz = ps("ix", a, ns, s0 % 8), ps("Pz", a, n)
+        mm(ps("np", a, n), f("C3"), ln("gs"))
+        act(ln("npb"), ps("np", a, n), AF.Relu, f("bN"), f("wN"))
+        mms([(ix, f("I"), f("J", ns, s0), True, False)] + [(ix, sk(r), st("npb", a + r, a + n), False, r == LV - 1) for r in range(LV)])
+        ts(f("idx", ns, s0), ix, float(ES * (n // CL) - 1), A.min)
+        copy(ENG["eg"], ln("Eg"), ("@", f("E", ES * (n // CL), ES * (a // CL)), f("idx", ns, s0)))
+        mms([(pz, f("I"), ln(z), True, False), (pz, f("cQ"), ln("ones"), False, False), (pz, f("Ih"), ln("Eg"), False, True)])
+        ts(ln(zs), pz, ROUND, A.add, -ROUND, A.add)
+        if last:
+            dma("s", T.yz[:, a:a + n], T[zs][:, a:a + n], [ln(zs)], [])
+        else:
+            send(ln(zs), ln("z" + nx), topo, core, dst, "Z%d_%s" % (p, nx))
+
     for v in range(VIS):
-        L, z = "L%d" % v, "z%d" % v
-        last = v == VIS - 1
-        dst = T.cores[(rank + 1 + v % (ranks - 1)) % ranks]
         if v > 0:
             src = T.cores[(rank - 1 - (v - 1) % (ranks - 1)) % ranks]
-            n = len(topo.engines(src, core))
-            arrive(f(L), "aL%d" % v, n, "L%d" % v)
-            arrive(f(z), "aZ%d" % v, n, "Z%d" % v)
-        for s in (ORDER_LAST if last else ORDER).split():
-            step(s, v, L, z, last, dst)
+            e = len(topo.engines(src, core))
+            for h in range(2):
+                arrive(f("L%d" % v, 128, 128 * h), "L%d_%d" % (h, v), e)
+            for p, (a, n) in enumerate(PARTS):
+                arrive(f("z%d" % v, n, a), "Z%d_%d" % (p, v), e)
+        for s in (ORDER_LAST if v == VIS - 1 else ORDER_NEXT).split():
+            DBG["tag"] = (v, s)
+            step(s, v)
     issue()

@@ -8,11 +8,12 @@ CE = CL * LV
 ES = CE + 16
 PARTS = ((128, 128), (0, 128))
 NULL, BIG, ROUND, LIFT = -4096.0, 8192.0, 12582912.0, 64.0
+CUT = {}
 BLOCK = {"X": 16, "F": 32}
-WAKE, CYC, PEC, GAT, SCA, SEND, FLY, ROUNDS = 160.0, 0.9, 0.5, 1.56, 3.8, 1200.0, 4500.0, 3
-ENG = {"fg": "ssss", "fh": "ssss", "da": "ssss", "ea": "vsss", "zz": ("v", "gv"), "y2": "ss", "eg": "s", "bs": "s"}
-ORDER = ("fg3 fg2 ce1 zz1 xl3 xl2 fh3 fh2 fl1 yy1 xg3 xg2 hl1 ce0 zz0 cb fg1 fg0 xl1 xl0 fl0 yy0 fh1 fh0 da3 da2 fs1 nw1 cw1 vq1 ea3 ea2 "
-         "gs0 zp0 mg0 xg1 xg0 hl0 da1 da0 fs0 nw0 cw0 vq0 ea1 ea0 gs1 mg1 zp1 bs1 bs0 xs1 xs0 ")
+WAKE, CYC, PEC, GAT, SCA, SEND, FLY, ROUNDS = 160.0, 0.9, 0.55, 1.56, 3.8, 1600.0, 4000.0, 3
+ENG = {"fg": "ssss", "fh": "ssss", "da": "ssss", "ea": "ssvv", "zz": ("gv", "gv"), "z0": ("g", "g"), "nf": "v", "y2": "vs", "eg": "v", "bs": "s", "fs": "v"}
+ORDER = ("fg3 fg2 ce1 zz1 xl3 xl2 fh3 fh2 fl1 xg3 xg2 hl1 ea3 ea2 gs0 zp0 yy1 ce0 zz0 cb fg1 fg0 xl1 xl0 fl0 yy0 da3 da2 fs1 nw1 cw1 vq1 "
+         "fh1 fh0 mg0 xg1 xg0 hl0 da1 da0 fs0 ea1 ea0 gs1 mg1 zp1 nw0 cw0 vq0 bs1 bs0 xs1 xs0 ")
 ORDER_NEXT, ORDER_LAST = ORDER + "aa", "cp " + ORDER
 RANK_NEXT = ("ea2 zp0 fs0 zp1 fg3 ea0 mg0 nw1 hl1 xl2 nw0 fl1 da2 xg2 ea3 xl3 ea1 gs0 gs1 aa hl0 da3 xg0 zz0 ce0 +zz1 k4 xg3 yy0 fs1 fh3 cw1 fh1 "
              "mg1 fg2 xg1 yy1 fg1 fl0 +ce1 bs0 cw0 xs1 in xs0 xl0 fh2 da1 k2 fg0 vq1 xl1 k1 cb fh0 vq0 k3 da0 bs1")
@@ -27,18 +28,19 @@ for _v in range(VIS):
         else:
             FIRST.setdefault((_v, _s), 1000 * _v + _i)
 FIRST[(0, "in")] = -200
+LEAD, SLACKS = {}, (0.0, 0.2)
 
 DBG = {"rw": [], "tag": None}
 SCRATCH, LOC = {}, {}
 DT2 = ("bfloat16", "float16", "uint16")
 for _b, _d, _l in (
         ("", "bfloat16", "X 4128 X2 4128 Fw 4128 FG 4096 FH 4096 D 4096 E 4160 DA 4096 EA 4096 z16 4096 fh 256 fl 256 nq 256 "
-         "fs 256 gs 256 npb 256 sgb 256 eqF 256 eqX 256 sgc 384 hm 256 lod 256 Eg 256"),
+         "fs 256 gs 256 npb 256 sgb 256 eqF 256 eqX 256 sgc 384 hm 256 Eg 256"),
         ("kb", "bfloat16", "SK 2048 SKc 2048 SKu 2048 SEL 2048 DF 2048 LOST 2048 code 128 code2 128 cS 256 I 128 In 128 I32 128 Ih 128 "
-         "Iq 128 I8 128 tr 128 C1 128 Cc 128 C2B 128 C3B 128 C3 128 C2f 128 cV 128 cQ 128 c256 128 HM 128 c75 256 "
-         "mT16 128 mR16 128 bk16 128 dd16 16 mT32 256 mR32 256 bk32 128 dd32 16 t1 128 t2 128 J 16 ones 256"),
-        ("", "float32", "Ff 4128 Bt 1056 fc 256 FLf 256 y1 256 y2 256 lof 256 ylo 256 newf 256 ybo 1024"),
-        ("kf", "float32", "q16 128 g16 128 q32 256 g32 128 tmp 128 s16 16 j16 16 oh 16 da 16 db 16 la 16 lb 16 rp 1 p16 1 r32 1 p32 1 wc 1 wu 1 wv 1 n15 1 "
+         "Iq 128 I8 128 tr 128 C1 128 Cc 128 C2B 128 C3B 128 C3 128 C2f 128 cV 128 cQ 128 c256 128 HM 128 cK 128 c75 256 "
+         "mT16 128 mR16 128 bk16 128 dd16 16 mT32 256 mR32 256 bk32 128 dd32 16 t1 128 t2 128 J 16 ones 256 q16 128 g16 128 q32 256 g32 128 tmp 128"),
+        ("", "float32", "F32 4128 lod 256 Ff 4128 Bt 1056 fc 256 FLf 256 y1 256 y2 256 lof 256 ylo 256 newf 256 ybo 1024"),
+        ("kf", "float32", "s16 16 j16 16 oh 16 da 16 db 16 la 16 lb 16 rp 1 p16 1 r32 1 p32 1 wc 1 wu 1 wv 1 n15 1 "
          "c613 1 bW0 1 bW 1 bH 1 wN 1 bN0 1 bN 1 bhm 1 blo 1 r16 1 rp1 1 Tn 1 Tp 1 thr 1"),
         ("", "int32", "Bi 1024 tI 1 f0 256 la0 256 i1 32 i2 32 rr 256 new 256 vq 256 val 256"),
         ("ki", "int32", "pi 1 pi2 1 pi3 1 pi4 1 pi5 1 a1 1 a2 1"),
@@ -64,12 +66,12 @@ for _v in range(VIS + 1):
 PSUM = ("a0", "b0", "c0", "d0", "a1p", "b1", "c1", "d1")
 PLACE = {"FL": (0, 0), "G": (0, 128), "difF": (0, 256),
          "d": (1, 0), "M": (1, 0), "Pw": (1, 0), "keyX": (1, 0), "difX": (1, 128), "ub": (1, 256), "Q": (1, 256), "lstX": (1, 384),
-         "cu": (1, 392), "ix": (1, 408), "lstB": (1, 416),
-         "e": (2, 0), "np": (2, 0), "Pz": (2, 0), "dl": (2, 128), "Pl": (2, 128), "difB": (2, 256),
+         "cu": (1, 392), "ix": (2, 256), "lstB": (3, 416), "difB": (0, 256),
+         "e": (2, 0), "np": (2, 0), "Pz": (2, 0), "dl": (2, 128), "Pl": (2, 128),
          "Ph": (3, 0), "keyF": (3, 128), "lstF": (3, 384), "aa": (3, 400)}
 for _n in PSUM:
     SCRATCH[_n] = ("psum", [128, 512], "float32")
-NDMA = 24
+NDMA = 28
 SEMAPHORES = ["q_v", "q_s", "q_t", "q_g"] + ["d%d" % i for i in range(NDMA)]
 for _v in range(1, VIS):
     for _p in ("L0", "L1", "Z0", "Z1", "Z2"):
@@ -264,13 +266,13 @@ def make(g, T):
                             order.append(j)
             return order
 
-        def listed(rank, slack):
+        def listed(rank, slack, fwd=fwd, bwd=bwd, least=[0.0] * n):
             at, left, ready = [0.0] * n, [len(x) for x in fwd], {q: [] for q in queues}
             free, held, todo = {q: 0.0 for q in queues}, {b: {} for b in PSUM}, [i for i in range(n) if not fwd[i]]
             while True:
                 while todo:
                     i = todo.pop()
-                    at[i] = max([at[j] + lag for j, lag in fwd[i]] or [0.0])
+                    at[i] = max([at[j] + lag for j, lag in fwd[i]] + [least[i]])
                     if ops[i][0]:
                         ready[ops[i][0]].append(i)
                         continue
@@ -283,7 +285,7 @@ def make(g, T):
                     if ready[q]:
                         c = [(max([at[i], free[q]] + [held[b][r] + WAKE for b in bank[i] for r in held[b] if r != q]), i) for i in ready[q]]
                         m = min(c)[0]
-                        i = min([(rank[i], i) for s, i in c if s == m])[1]
+                        i = min([(s, rank[i], i) for s, i in c])[2]
                         s, i = min([(rank[j], s, j) for s, j in c if s <= m + slack * cost[i]])[1:]
                         if best is None or s < best[0]:
                             best = (s, q, i)
@@ -313,13 +315,24 @@ def make(g, T):
         if DBG.get("only"):
             DBG.update(place=place, rounds=rounds, ranked=ranked, listed=listed, fwd=fwd, bwd=bwd, cost=cost, tail=tail, ops=ops, bank=bank)
             return
-        back = [0.0] * n
+        chain = [0.0] * n
         for i in range(n - 1, -1, -1):
-            back[i] = cost[i] + max([back[j] + lag - cost[j] for j, lag in bwd[i]] + [tail[i]])
-        at = listed([FIRST.get(DBG["rw"][i - n][0], 0.0) - CHAIN * back[i] for i in range(n)], SLACK)
-        best = (max(at[i] + cost[i] + tail[i] for i in range(n)), at)
-        if ROUNDS:
-            best = min(best, rounds(sorted(range(n), key=lambda i: (at[i], i)), ROUNDS))
+            chain[i] = max([chain[j] + lag for j, lag in bwd[i]] + [tail[i]])
+        lead = [1000.0 * LEAD.get("FL"[t[0] // 4] + t[1] if t[0] % 4 == 0 else t[1], LEAD.get(t[1], 0)) for t, _, _ in DBG["rw"][-n:]]
+
+        def latest(t, by=[0.0] * n):
+            return [-t[i] - cost[i] - by[i] for i in range(n)]
+        best = None
+        for slack in SLACKS:
+            at = listed(latest(chain, lead), slack)
+            for _ in range(ROUNDS):
+                at = listed(latest(listed(latest(at), slack, bwd, fwd, tail), lead), slack)
+                r = latest(at)
+                r = latest(place(sorted(range(n), key=lambda i: (r[i], -i)), bwd, tail))
+                for x in (at, place(sorted(range(n), key=lambda i: (r[i], i)), fwd, [0.0] * n)):
+                    end = max(x[i] + cost[i] + tail[i] for i in range(n))
+                    if best is None or end < best[0]:
+                        best = (end, x)
         if DBG.get("at"):
             best = (0, DBG["at"])
         DBG["end"] = best[0]
@@ -392,8 +405,11 @@ def rank_program(g, core, T, topo):
     def mm(out, lhsT, rhs, start=True, stop=True):
         mms([(out, lhsT, rhs, start, stop)])
 
+    def times(out, in_, a, b=0.0):
+        act(out, in_, AF.Identity, b, a)
+
     def line(out, a, b):
-        ts(out, f("rp"), float(a), A.mult, float(b), A.add)
+        times(out, f("rp"), float(a), float(b))
 
     DBG["tag"] = (0, "in")
     dma("y", T.f0[:, :], T.fw[:, :], [], [f("f0")])
@@ -402,13 +418,13 @@ def rank_program(g, core, T, topo):
     dma("s", T.tI[:, :], T.th[:, :], [], [f("tI")])
     dma("y", T.X[:, PAD:PAD + W // 2], T.x[:, :W // 2], [], [f("X", W // 2, PAD)], False, 4.5)
     ms(f("Fw"), 0.0)
-    ts(f("fc"), f("f0"), -2048.0, A.add)
-    cp(f("fh"), f("fc"))
+    ts(f("fh"), f("f0"), float(W), A.add)
     d = dma("y", T.Fw[0:128:16, PAD:PAD + W], T.fh[:, :], [f("fh")], [f("Fw")])
+    ts(f("fc"), f("f0"), W + LIFT, A.add)
     tt(f("fl"), f("fc"), f("fh"), A.subtract)
     d = dma("y", T.Fw[1:128:16, PAD:PAD + W], T.fl[:, :], [f("fl")], [f("Fw")], True)
-    dma("y", T.X[:, PAD + W // 2:PAD + W], T.x[:, W // 2:], [], [f("X", W // 2, PAD + W // 2)], False, 4.5, False, [d])
-    dma("y", T.Bi[:, :], T.bk[:, :], [], [f("Bi")], False, 6.0, False, [d])
+    d = dma("y", T.X[:, PAD + W // 2:PAD + W], T.x[:, W // 2:], [], [f("X", W // 2, PAD + W // 2)], False, 5.0, False, [d])
+    dma("y", T.Bi[:, :], T.bk[:, :], [], [f("Bi")], False, 7.0, False, [d])
     cp(f("L0"), f("la0"))
     iota(f("pi"), [[0, 1]], 1)
     iota(f("g16"), [[1, 8], [0, 16]], 0)
@@ -431,15 +447,16 @@ def rank_program(g, core, T, topo):
     act(f("SKc"), f("SK"), AF.Identity, 0.0, f("wc"))
     ts(f("Bt", C, PAD), f("Bi"), lift, A.add)
     DBG["tag"] = (0, "k1")
-    for k in range(LV):
-        ts(sk(k, "SKu"), f("code"), float(k), A.is_equal, f("wu"), A.mult)
+    ts(f("SKu"), f("SK"), f("wu"), A.mult)
     for h in range(2):
         ts(f("cS", 128, 128 * h), f("code"), 0.0, A.is_ge)
+    ts(f("cK"), f("code"), 0.0, A.is_ge, -(W + LIFT + 2048) / LV, A.mult)
+    ms(f("ones"), 1.0)
     ts(f("I"), f("code"), f("rp"), A.is_equal)
     ts(f("tr"), f("code"), f("rp"), A.is_ge)
     ts(f("oh"), f("s16"), f("rp"), A.is_equal)
     for k in range(LV):
-        ts(sk(k, "SEL"), f("cS", 128), f("oh", 1, k), A.mult)
+        times(sk(k, "SEL"), f("cS", 128), f("oh", 1, k))
     DBG["tag"] = (0, "k2")
     tt(f("code2"), f("cS", 128), f("I"), A.add)
     ts(f("da"), f("s16"), f("rp"), A.not_equal, 1.0, A.add)
@@ -453,17 +470,16 @@ def rank_program(g, core, T, topo):
     for n, m, s in (("In", "I", -1), ("I32", "I", 32), ("Ih", "I", 0.5), ("Iq", "I", -BIG / 2), ("I8", "I", BIG),
                     ("C1", "tr", 2 ** 22), ("C3B", "tr", -BIG / 2), ("C3", "tr", -0.5), ("cQ", "cS", -1 / 64), ("c256", "cS", -256),
                     ("t1", "I", 2 ** 16)):
-        ts(f(n), f(m, 128), float(s), A.mult)
+        times(f(n), f(m, 128), float(s))
     tt(f("Cc"), f("C1"), f("t1"), A.add)
     ts(f("t2"), f("code"), f("rp"), A.is_gt, -BIG, A.mult)
     tt(f("C2B"), f("t2"), f("Iq"), A.subtract)
-    ts(f("n15"), f("rp"), 15.0, A.not_equal)
-    ts(f("C2f"), f("C2B"), f("n15"), A.mult)
-    ts(f("wv"), f("oh", 1), 255.75, A.mult, -256.0, A.add)
-    ts(f("cV"), f("cS", 128), f("wv"), A.mult)
+    times(f("n15"), f("oh", 1, 15), -1.0, 1.0)
+    times(f("C2f"), f("C2B"), f("n15"))
+    times(f("wv"), f("oh", 1), 255.75, -256.0)
+    times(f("cV"), f("cS", 128), f("wv"))
     tt(f("HM"), sk(0), sk(1), A.subtract)
     ms(f("c75"), -15 * NULL / BIG)
-    ms(f("ones"), 1.0)
     ts(f("pi4"), f("pi"), 31, A.bitwise_and)
     ts(f("pi5"), f("pi"), 5, A.arith_shift_right)
     cp(f("r32"), f("pi4"))
@@ -479,25 +495,36 @@ def rank_program(g, core, T, topo):
     ts(f("J"), f("j16"), f("r16"), A.add)
     line(f("c613"), 613 * 32, 0)
     line(f("bW0"), -BIG, -BIG / 2)
-    ts(f("bW"), f("oh", 1, 15), BIG / 2, A.mult, f("bW0"), A.add)
+    times(f("bW"), f("oh", 1, 15), BIG / 2, f("bW0"))
     line(f("bH"), -1.5 * BIG, -BIG)
-    ts(f("wN"), f("oh", 1, 15), BIG - 1, A.mult, 1.0, A.add)
+    times(f("wN"), f("oh", 1, 15), BIG - 1, 1.0)
     line(f("bN0"), -0.5, 0.5)
-    ts(f("bN"), f("bN0"), f("wN"), A.mult)
-    ts(f("bhm"), f("oh", 1), -15 * NULL, A.mult)
-    ts(f("blo"), f("oh", 1, 1), -15 * NULL, A.mult)
+    times(f("bN"), f("bN0"), f("wN"))
+    times(f("bhm"), f("oh", 1), -15 * NULL + 2048 + W)
+    times(f("blo"), f("oh", 1, 1), -15 * NULL + 2048 + W + LIFT)
     ts(f("Tn"), f("tI"), -1.0, A.mult, -0.5, A.add)
     ts(f("Tp"), f("tI"), 0.5 - BIG / 2, A.add)
     cp(f("thr"), f("Tn"))
     for c in range(NCH):
-        ms(f("E", 16, ES * c + CE), 0.0)
+        times(f("E", 16, ES * c + CE), f("s16"), 0.0)
     DBG["tag"] = (0, "k4")
-    iota(f("Ff"), [[0, PAD + W]], 0, 2048)
+    if ENG["fs"] == "s":
+        for a in range(0, PAD + W, 1032):
+            iota(f("F32", 1032, a), [[0, 1032]], 0)
+        for d in range(2):
+            dma("g", T.F32[d:128:16, PAD:PAD + W], T.Fw[d:128:16, PAD:PAD + W], [f("Fw")], [f("F32")], d == 1, 3.0)
+    DBG["tag"] = (0, "k5")
+    for a in range(0, PAD + W, 1032):
+        iota(f("Ff", 1032, a), [[0, 1032]], 0, -int(W + LIFT))
 
-    FW, XW = f("Fw", W, PAD), f("X", W, PAD)
+    XW = f("X", W, PAD)
 
-    def ent(name, c):
-        return f(name, CE, (ES if name == "E" else CE) * c)
+    def ent(name, c, a=0, n=CL):
+        return f(name, LV * n, (ES if name == "E" else CE) * c + LV * a)
+
+    def cuts(k):
+        n = CL // CUT.get(k, 1)
+        return [(b, n) for b in range(0, CL, n)]
 
     def copy(e, out, in_):
         if e == "s":
@@ -510,7 +537,9 @@ def rank_program(g, core, T, topo):
     def turn(out, srcs, c, stop=True):
         for i, src in enumerate(srcs):
             a = ent(src, c)[1]
-            mms([(out, sk(k), st(src, a + k, a + CE), i == 0 and k == 0, stop and k == LV - 1 and i == len(srcs) - 1) for k in range(LV)])
+            less = [(out, f("cK"), f("ones", CL), True, False)] * (src[0] == "F")
+            mms(less + [(out, sk(k), st(src, a + k, a + CE), i == 0 and k == 0 and not less, stop and k == LV - 1 and i == len(srcs) - 1)
+                        for k in range(LV)])
 
     def ps(name, lane, n, at=None, rows=128):
         b, a = PLACE[name]
@@ -521,7 +550,8 @@ def rank_program(g, core, T, topo):
 
     def sizes(e, src, dst, c):
         if e == "s":
-            act(ent(dst, c), ent(src, c), AF.Abs)
+            for b, n in cuts("ab"):
+                act(ent(dst, c, b, n), ent(src, c, b, n), AF.Abs)
             return [dst]
         ts(ent(dst, c), ent(src, c), 0.0, A.min, -2.0, A.mult)
         return [src, dst]
@@ -542,9 +572,11 @@ def rank_program(g, core, T, topo):
         key, dif, lst = ps("key" + tab, a, w, 0, n), ps("dif" + tab, a, w, 0, n), ps("lst" + tab, a, n // 16, a % 128 // 16)
         wt, eq = f("WT" + tab, w, 0, n), f("eq" + tab, w, 0, n)
         mms([(key, f("I8", n), f("c75", w), True, False), (key, rows, f("cS", w), False, True)])
-        mms([(dif, f("I8", n), f("mT" + s), True, False), (dif, rows, f("cS", w), False, False)])
+        both = [(dif, f("I8", n), f("mT" + s), True, False), (dif, rows, f("cS", w), False, False)]
+        if dif[0] != key[0]:
+            mms(both)
         tt(wt, key, f("mR" + s, w, 0, n), A.mult)
-        mm(dif, f("bk" + s, n, 0, n), wt, False, True)
+        mms(both * (dif[0] == key[0]) + [(dif, f("bk" + s, n, 0, n), wt, False, True)])
         ts(eq, dif, 0.0, A.is_equal, -BIG, A.mult)
         mms([(each(lst, h, m), f(x + tab, 128, 128 * h, n), f("dd" + s, n // b, 0, n), x == "WT", x == "eq")
              for h in range(m) for x in ("WT", "eq")])
@@ -565,6 +597,7 @@ def rank_program(g, core, T, topo):
         dst = T.cores[(rank + 1 + v % (ranks - 1)) % ranks]
         k, c = s[:2], int(s[2:] or 0)
         a = 128 * c
+        FW = f("F32" if v and ENG["fs"] == "s" else "Fw", W, PAD)
 
         def ln(name, b=0):
             return f(name, 128, a + b)
@@ -574,15 +607,21 @@ def rank_program(g, core, T, topo):
         if k == "cp":
             dma("y", T.X2[:, PAD:PAD + W], T.X[:, PAD:PAD + W], [XW], [f("X2", W, PAD)], False, 7.0)
             for d in range(2):
+                if ENG["fs"] == "s":
+                    dma("g", T.Fw[d:128:16, PAD:PAD + W], T.F32[d:128:16, PAD:PAD + W], [f("F32")], [f("Fw")], d == 1, 3.0)
+            for d in range(2):
                 for a in (PAD, PAD + W // 2):
                     dma("g", T.Ff[0:128:16, a:a + W // 2], T.Fw[d:128:16, a:a + W // 2], [f("Fw"), f("Ff", W // 2, a)], [f("Ff", W // 2, a)], False, 3.0, True)
         elif k == "fg":
-            copy(ENG["fg"][c], ent("FG", c), ("@", FW, f(L, CL, CL * c)))
+            for b, n in cuts(k):
+                copy(ENG["fg"][c], ent("FG", c, b, n), ("@", FW, f(L, n, CL * c + b)))
         elif k == "fh":
-            copy(ENG["fh"][c], ent("FH", c), ("@", FW, f("Bb", CL, CL * c)))
+            for b, n in cuts(k):
+                copy(ENG["fh"][c], ent("FH", c, b, n), ("@", FW, f("Bb", n, CL * c + b)))
         elif k == "zz":
             for i in range(LV):
-                copy(ENG["zz"][c][i % len(ENG["zz"][c])], st("z16", LV * a + i, LV * (a + 128)), ln(z))
+                e = ENG["zz" if v else "z0"][c]
+                copy(e[i % len(e)], st("z16", LV * a + i, LV * (a + 128)), ln(z))
         elif k == "ce":
             b = 16 * c
             wrap(each(ps("cu", a, 16), 0, 2), "SKc", z, a, 128)
@@ -603,7 +642,8 @@ def rank_program(g, core, T, topo):
         elif k == "xl":
             turn(ps("FL", CL * c, CL), ["FG"], c)
             ts(f("FLu", CL, CL * c), ps("FL", CL * c, CL), 2048.0, A.add)
-            tt(ent("D", c), ("@", XW, f("FLu", CL, CL * c)), ent("z16", c), A.subtract)
+            for b, n in cuts(k):
+                tt(ent("D", c, b, n), ("@", XW, f("FLu", n, CL * c + b)), ent("z16", c, b, n), A.subtract)
         elif k == "fl":
             act(ln("FLf"), pl("FL"), AF.Identity, 2048.0)
             ts(ln("FLc"), ln("FLu"), -2048.0, A.add)
@@ -618,7 +658,8 @@ def rank_program(g, core, T, topo):
         elif k == "xg":
             turn(ps("G", CL * c, CL), ["FH"], c)
             ts(f("Gu", CL, CL * c), ps("G", CL * c, CL), 2048.0, A.add)
-            tt(ent("E", c), ("@", XW, f("Gu", CL, CL * c)), ent("z16", c), A.subtract)
+            for b, n in cuts(k):
+                tt(ent("E", c, b, n), ("@", XW, f("Gu", n, CL * c + b)), ent("z16", c, b, n), A.subtract)
         elif k == "hl":
             tt(ln("hiC"), pl("G"), ln("FLc"), A.max)
             tt(ln("loC"), pl("G"), ln("FLc"), A.min)
@@ -647,7 +688,10 @@ def rank_program(g, core, T, topo):
             tt(ln("vq"), pl("Q"), ln(z), A.max)
             ts(ln("val"), ln("vq"), 255, A.bitwise_and)
         elif k == "bs":
-            if lift:
+            if ENG["nf"] == "s":
+                mm(pl("FL"), f("I"), ln("nC"))
+                times(ln("newf"), pl("FL"), 1.0, 2048 + lift)
+            elif lift:
                 ts(ln("newf"), ln("new"), lift, A.add)
             scatter("Bt", "B", "newf" if lift else "new", a, 128, ENG["bs"])
             if last and c == 0:
@@ -695,7 +739,7 @@ def rank_program(g, core, T, topo):
             act(ln("hm"), lo, AF.Identity, f("bhm"))
             mms([(lo, sk(1), ln("Vl"), True, False), (lo, f("HM"), ln("hm"), False, True)])
             act(ln("lod"), lo, AF.Identity, f("blo"))
-            scatter("Fw", "F", "lod", a, n)
+            scatter("F32" if ENG["fs"] == "s" else "Fw", "F", "lod", a, n, ENG["fs"])
             DBG["tag"] = (DBG["tag"][0], "aa")
             act(f("sgc", 128, 128 * p, n), ps("keyF", a, 128, 0, n), AF.Sign, 3000.0)
 

@@ -1,3 +1,4 @@
+from concourse.bass import DstId, RemoteDMATransfer
 from concourse.mybir import AluOpType as A, ActivationFunctionType as AF
 
 VIS, W, C, K, LV = 5, 4096, 1024, 256, 16
@@ -8,12 +9,15 @@ CE = CL * LV
 ES = CE + 16
 PARTS = ((128, 128), (0, 128))
 NULL, BIG, ROUND, LIFT = -4096.0, 8192.0, 12582912.0, 64.0
-CUT = {}
-BLOCK = {"X": 16, "F": 32}
-WAKE, CYC, PEC, GAT, SCA, SEND, FLY, ROUNDS = 160.0, 0.9, 0.55, 1.56, 3.8, 1600.0, 4000.0, 3
-ENG = {"fg": "ssss", "fh": "ssss", "da": "ssss", "ea": "ssvv", "zz": ("gv", "gv"), "z0": ("g", "g"), "nf": "v", "y2": "vs", "eg": "v", "bs": "s", "fs": "v"}
-ORDER = ("fg3 fg2 ce1 zz1 xl3 xl2 fh3 fh2 fl1 xg3 xg2 hl1 ea3 ea2 gs0 zp0 yy1 ce0 zz0 cb fg1 fg0 xl1 xl0 fl0 yy0 da3 da2 fs1 nw1 cw1 vq1 "
-         "fh1 fh0 mg0 xg1 xg0 hl0 da1 da0 fs0 ea1 ea0 gs1 mg1 zp1 nw0 cw0 vq0 bs1 bs0 xs1 xs0 ")
+FINE, LAST = ("xl0c", "xl1c", "xg0c", "xg1c"), {"X": 16, "F": 32, "B": 16}
+XA, BA, XOUT = 0, 1024, 7.0
+BLOCK = {"X": (16, 16), "F": (32, 16), "B": (16, 16)}
+WAKE, CYC, PEC, GAT, SCA, SEND, FLY, ROUNDS = 160.0, 0.9, 0.5, 1.56, 3.8, 1600.0, 4000.0, 3
+ENG = {"fg": "ssss", "fh": "ssss", "da": "sssv", "ea": "ssss", "zz": ("gggv", "gv"), "z0": ("g", "g"), "ix": "tv", "nf": "v", "y2": "vs", "eg": "v", "bs": "s", "fs": "s", "yb": "s"}
+ONE = True
+ORDER = ("zc1 zc0 fg3 fg2 ce1 zz1 xl3 xl2 fh3 fh2 fl1 xg3 xg2 hl1 ea3 ea2 gs0 zp0 ce0 yy1 zz0 cb fg1 fg0 xl1 xl0 fl0 yy0 da3 da2 fs1 nw1 cw1 vq1 "
+         "fh1 fh0 mg0 xg1 xg0 hl0 da1 da0 fs0 ea1 ea0 gs1 mg1 zp1 nw0 cw0 vq0 bs1 bs0 xs1 xs0 sn0 sn1 sn2 sn3 ")
+SENDS = ((("z", 128, 128), ("L", 128, 128)), (("z", 0, 128), ("L", 0, 128)))
 ORDER_NEXT, ORDER_LAST = ORDER + "aa", "cp " + ORDER
 RANK_NEXT = ("ea2 zp0 fs0 zp1 fg3 ea0 mg0 nw1 hl1 xl2 nw0 fl1 da2 xg2 ea3 xl3 ea1 gs0 gs1 aa hl0 da3 xg0 zz0 ce0 +zz1 k4 xg3 yy0 fs1 fh3 cw1 fh1 "
              "mg1 fg2 xg1 yy1 fg1 fl0 +ce1 bs0 cw0 xs1 in xs0 xl0 fh2 da1 k2 fg0 vq1 xl1 k1 cb fh0 vq0 k3 da0 bs1")
@@ -28,23 +32,26 @@ for _v in range(VIS):
         else:
             FIRST.setdefault((_v, _s), 1000 * _v + _i)
 FIRST[(0, "in")] = -200
-LEAD, SLACKS = {}, (0.0, 0.2)
+LEAD, SLACKS = {"k0": 30, "ks": 10}, (0.0, 0.075, 0.15, 0.225, 0.3, 0.4)
+LAID, CACHE, ONCE = {}, True, 3000.0
+PLANS = ((160.0, 0.0, 1.0, 1.0, 1.0, 1.0), (160.0, 15.0, 0.95, 1.06, 1.0, 1.0))
+OTHER = ((160.0, 0.0, 1.0, 1.0, 1.0, 1.0), (240.0, 20.0, 0.85, 0.85, 0.5, 0.8), (110.0, 20.0, 0.9, 0.9, 1.2, 1.3), (170.0, 0.0, 0.85, 1.15, 0.5, 1.3))
 
 DBG = {"rw": [], "tag": None}
 SCRATCH, LOC = {}, {}
 DT2 = ("bfloat16", "float16", "uint16")
 for _b, _d, _l in (
         ("", "bfloat16", "X 4128 X2 4128 Fw 4128 FG 4096 FH 4096 D 4096 E 4160 DA 4096 EA 4096 z16 4096 fh 256 fl 256 nq 256 "
-         "fs 256 gs 256 npb 256 sgb 256 eqF 256 eqX 256 sgc 384 hm 256 Eg 256"),
+         "fs 256 gs 256 qb 256 npb 256 sgb 256 eqF 256 eqX 256 sgc 384 hm 256 Eg 256"),
         ("kb", "bfloat16", "SK 2048 SKc 2048 SKu 2048 SEL 2048 DF 2048 LOST 2048 code 128 code2 128 cS 256 I 128 In 128 I32 128 Ih 128 "
          "Iq 128 I8 128 tr 128 C1 128 Cc 128 C2B 128 C3B 128 C3 128 C2f 128 cV 128 cQ 128 c256 128 HM 128 cK 128 c75 256 "
-         "mT16 128 mR16 128 bk16 128 dd16 16 mT32 256 mR32 256 bk32 128 dd32 16 t1 128 t2 128 J 16 ones 256 q16 128 g16 128 q32 256 g32 128 tmp 128"),
-        ("", "float32", "F32 4128 lod 256 Ff 4128 Bt 1056 fc 256 FLf 256 y1 256 y2 256 lof 256 ylo 256 newf 256 ybo 1024"),
+         "mF16 128 m216 128 mF32 256 m232 256 mT16 128 mR16 128 bk16 128 dd16 16 mT32 256 mR32 256 bk32 128 dd32 16 t1 128 t2 128 J 16 ones 256 q16 128 g16 128 q32 256 g32 128 tmp 128"),
+        ("", "float32", "F32 4128 lod 256 Ff 4128 Bt 1056 fc 256 FLf 256 y1 256 y2 256 lof 256 ylo 256 newf 256 ybo 1024 ybr 1024"),
         ("kf", "float32", "s16 16 j16 16 oh 16 da 16 db 16 la 16 lb 16 rp 1 p16 1 r32 1 p32 1 wc 1 wu 1 wv 1 n15 1 "
-         "c613 1 bW0 1 bW 1 bH 1 wN 1 bN0 1 bN 1 bhm 1 blo 1 r16 1 rp1 1 Tn 1 Tp 1 thr 1"),
+         "c613 1 bW0 1 bW 1 bH 1 bQ 1 wN 1 bN0 1 bN 1 bhm 1 blo 1 r16 1 rp1 1 Tn 1 Tp 1 thr 1"),
         ("", "int32", "Bi 1024 tI 1 f0 256 la0 256 i1 32 i2 32 rr 256 new 256 vq 256 val 256"),
         ("ki", "int32", "pi 1 pi2 1 pi3 1 pi4 1 pi5 1 a1 1 a2 1"),
-        ("", "float16", "bu 32 FLc 256 hiC 256 loC 256 nC 256 Vw 256 Vh 256 Vl 256 WTF 256 WTX 256"),
+        ("", "float16", "bu 32 FLc 256 hiC 256 loC 256 nC 256 Vw 256 Vh 256 Vl 256 WTF 256 WTX 256 WTz 128 Iz 128 Izh 128"),
         ("", "uint16", "bl 16 Bb 256 FLu 256 Gu 256 ofB 32 ofX 32 ofF 32 idx 16")):
     _l, _c = _l.split(), 0
     for _i in range(0, len(_l), 2):
@@ -63,9 +70,11 @@ for _v in range(VIS + 1):
         SCRATCH["zs%d" % _v] = ("sbuf", [128, K], "bfloat16")
     if 0 < _v < VIS:
         SCRATCH["Ls%d" % _v] = ("sbuf", [128, K], "uint16")
+        SCRATCH["go%d" % _v] = ("sbuf", [128, 2 * K], "uint16")
+        SCRATCH["in%d" % _v] = ("sbuf", [128, 2 * K], "uint16")
 PSUM = ("a0", "b0", "c0", "d0", "a1p", "b1", "c1", "d1")
 PLACE = {"FL": (0, 0), "G": (0, 128), "difF": (0, 256),
-         "d": (1, 0), "M": (1, 0), "Pw": (1, 0), "keyX": (1, 0), "difX": (1, 128), "ub": (1, 256), "Q": (1, 256), "lstX": (1, 384),
+         "d": (1, 0), "M": (1, 0), "Pw": (1, 0), "keyX": (1, 0), "difX": (1, 128), "ub": (0, 256), "Q": (1, 256), "lstX": (1, 384),
          "cu": (1, 392), "ix": (2, 256), "lstB": (3, 416), "difB": (0, 256),
          "e": (2, 0), "np": (2, 0), "Pz": (2, 0), "dl": (2, 128), "Pl": (2, 128),
          "Ph": (3, 0), "keyF": (3, 128), "lstF": (3, 384), "aa": (3, 400)}
@@ -74,14 +83,14 @@ for _n in PSUM:
 NDMA = 28
 SEMAPHORES = ["q_v", "q_s", "q_t", "q_g"] + ["d%d" % i for i in range(NDMA)]
 for _v in range(1, VIS):
-    for _p in ("L0", "L1", "Z0", "Z1", "Z2"):
+    for _p in range(4):
         SEMAPHORES += ["a%s_%d" % (_p, _v), "l%s_%d" % (_p, _v)]
 
 
 def make(g, T):
     queues = {"v": g.vector, "s": g.scalar, "t": g.tensor, "g": g, "y": g.sync}
     ops, hw, hr, bank, marks = [], {}, {}, [], {}
-    nd, fence = [0], {}
+    nd, fence = [0, False], {}
 
     def ap(o):
         if o[0] == "@":
@@ -122,7 +131,7 @@ def make(g, T):
                     if meet(h, o):
                         dep(h[2], not (own and ops[h[2]][0] == q and ops[h[2]][5] is None))
         bank.append(sorted(set(o[0] for o in reads + writes if o[0] in PSUM)))
-        for j, w in extra:
+        for j, w in list(extra) + (list(ops[hw[writes[0][0]][-1][2]][2].items()) if beside else []):
             dep(j, w)
         ops.append((q, call, deps, cost, tail, tok))
         DBG["rw"].append((DBG["tag"], reads, writes))
@@ -182,7 +191,9 @@ def make(g, T):
             kw["bias"] = val(bias)
         if not (isinstance(scale, float) and scale == 1.0):
             kw["scale"] = val(scale)
-        work("s", out, [in_, bias, scale], lambda e: e.activation(ap(out), ap(in_), func, **kw), 1.0)
+        first = func == AF.Silu and not nd[1]
+        nd[1] = nd[1] or first
+        work("s", out, [in_, bias, scale], lambda e: e.activation(ap(out), ap(in_), func, **kw), 100.0 if first else 1.0)
 
     def mms(l):
         since = fence.setdefault(l[0][0][0], [])
@@ -194,8 +205,8 @@ def make(g, T):
             del since[:]
         since.append(i)
 
-    def iota(out, pattern, mult, base=0):
-        rec("g", [], regs(out), lambda e: e.iota(ap(out), pattern, base, mult, allow_small_or_imprecise_dtypes=True), 130.0 + 2 * CYC * num(out))
+    def iota(out, pattern, mult, base=0, after=()):
+        rec("g", list(after), regs(out), lambda e: e.iota(ap(out), pattern, base, mult, allow_small_or_imprecise_dtypes=True), 130.0 + 2 * CYC * num(out))
 
     def keep(out, in_):
         rec("g", regs(in_), regs(out), lambda e: e.affine_select(ap(out), ap(in_), [[0, num(out)]], A.is_equal, 0.0, 0, 0), 170.0 + 2 * CYC * num(out))
@@ -207,22 +218,48 @@ def make(g, T):
         return rec(q, reads, writes, lambda e: e.dma_start(out, in_, **kw), 70.0, 1000.0 * us, (s, 16), False, [(j, False) for j in after], beside)
 
     def arrive(o, mark, v):
-        rec(None, [], [o], None, 0.0, 0.0, ("a" + mark, v), False, [(marks[mark], True)])
+        rec(None, [], o, None, 0.0, 0.0, ("a" + mark, v), False, [(marks[mark], True)])
 
-    def send(o, out, topo, core, dst, mark):
+    def send(srcs, outs, topo, core, dst, mark):
         rid, pid = topo.addr(dst)[0:2]
-        marks[mark] = rec("g", regs(o), [], lambda e: e.remote_dma(ap(out), ap(o), T.sem["a" + mark], T.sem["l" + mark], pid, rid, topo.mask(core, dst)),
-                          SEND, FLY, ("l" + mark, len(topo.engines(core, dst))), False)
+        eng = topo.engines(core, dst)
+        m = len(eng) // len(srcs)
+
+        def call(e):
+            if len(srcs) == 1:
+                return e.remote_dma(ap(outs[0]), ap(srcs[0]), T.sem["a" + mark], T.sem["l" + mark], pid, rid, topo.mask(core, dst))
+            return e.remote_dma_fused([RemoteDMATransfer(dst_ids=[DstId(rid=rid, pnc=pid)], dma_engine_mask=sum(1 << x for x in eng[m * i:m * i + m]),
+                                                         remote_sem=T.sem["a" + mark], src=ap(srcs[i]), dst=ap(outs[i])) for i in range(len(srcs))],
+                                      local_sem=T.sem["l" + mark])
+        marks[mark] = rec("g", srcs, [], call, SEND, FLY + ONCE * (not marks), ("l" + mark, len(eng)), False)
 
     def issue():
         n = len(ops)
-        cost, tail = [op[3] for op in ops], [op[4] for op in ops]
+        cost, tail, wake = [0.0] * n, [0.0] * n, [0.0]
         fwd, bwd = [[] for _ in ops], [[] for _ in ops]
-        for i, op in enumerate(ops):
-            for j in op[2]:
-                lag = cost[j] + ((tail[j] + (WAKE if op[0] else 0.0)) if op[2][j] else 0.0)
-                fwd[i].append((j, lag))
-                bwd[j].append((i, lag + cost[i] - cost[j]))
+
+        def priced(more, long, pe, send, fly):
+            r = []
+            for q, _, _, c, e, _ in ops:
+                if q == "t":
+                    c *= pe
+                elif c == SEND:
+                    c, e = c * send, e * fly
+                elif q in ("v", "s") and not e:
+                    c = c * long if c > 700 else c + more
+                r.append((c, e))
+            return r
+
+        def assume(costs):
+            wake[0] = costs[0]
+            for i, (c, e) in enumerate(priced(*costs[1:])):
+                cost[i], tail[i], fwd[i][:], bwd[i][:] = c, e, [], []
+            for i, op in enumerate(ops):
+                for j in op[2]:
+                    lag = cost[j] + ((tail[j] + (wake[0] if op[0] else 0.0)) if op[2][j] else 0.0)
+                    fwd[i].append((j, lag))
+                    bwd[j].append((i, lag + cost[i] - cost[j]))
+        assume(PLANS[0])
 
         def place(order, first, least):
             at, busy = [0.0] * n, {q: [] for q in list(queues) + list(PSUM)}
@@ -232,7 +269,7 @@ def make(g, T):
                     t0 = -1.0
                     while t0 < t:
                         t0 = t
-                        for r, gap in [(q, 0.0)] + [(b, WAKE) for b in bank[i]]:
+                        for r, gap in [(q, 0.0)] + [(b, wake[0]) for b in bank[i]]:
                             b = busy[r]
                             k = len(b)
                             while k and b[k - 1][1] + gap > t:
@@ -283,7 +320,7 @@ def make(g, T):
                 best = None
                 for q in queues:
                     if ready[q]:
-                        c = [(max([at[i], free[q]] + [held[b][r] + WAKE for b in bank[i] for r in held[b] if r != q]), i) for i in ready[q]]
+                        c = [(max([at[i], free[q]] + [held[b][r] + wake[0] for b in bank[i] for r in held[b] if r != q]), i) for i in ready[q]]
                         m = min(c)[0]
                         i = min([(s, rank[i], i) for s, i in c])[2]
                         s, i = min([(rank[j], s, j) for s, j in c if s <= m + slack * cost[i]])[1:]
@@ -315,24 +352,39 @@ def make(g, T):
         if DBG.get("only"):
             DBG.update(place=place, rounds=rounds, ranked=ranked, listed=listed, fwd=fwd, bwd=bwd, cost=cost, tail=tail, ops=ops, bank=bank)
             return
-        chain = [0.0] * n
-        for i in range(n - 1, -1, -1):
-            chain[i] = max([chain[j] + lag for j, lag in bwd[i]] + [tail[i]])
         lead = [1000.0 * LEAD.get("FL"[t[0] // 4] + t[1] if t[0] % 4 == 0 else t[1], LEAD.get(t[1], 0)) for t, _, _ in DBG["rw"][-n:]]
 
         def latest(t, by=[0.0] * n):
             return [-t[i] - cost[i] - by[i] for i in range(n)]
-        best = None
-        for slack in SLACKS:
-            at = listed(latest(chain, lead), slack)
-            for _ in range(ROUNDS):
-                at = listed(latest(listed(latest(at), slack, bwd, fwd, tail), lead), slack)
-                r = latest(at)
-                r = latest(place(sorted(range(n), key=lambda i: (r[i], -i)), bwd, tail))
-                for x in (at, place(sorted(range(n), key=lambda i: (r[i], i)), fwd, [0.0] * n)):
-                    end = max(x[i] + cost[i] + tail[i] for i in range(n))
+
+        def replay(x, w, times):
+            done, free, held = [0.0] * n, {q: 0.0 for q in queues}, {b: {} for b in PSUM}
+            for i in x:
+                q, (c, e) = ops[i][0], times[i]
+                t = max([done[j] + (w if q else 0.0) for j in ops[i][2] if ops[i][2][j]] + [held[b][r] + w for b in bank[i] for r in held[b] if r != q]
+                        + [free.get(q, 0.0)])
+                free[q], done[i] = (t + c if q else 0.0), t + c + e
+                for b in bank[i]:
+                    held[b][q] = t + c
+            return max(done)
+        best, other = LAID.get(n), [(o[0], priced(*o[1:])) for o in OTHER]
+        for costs in PLANS * (best is None):
+            assume(costs)
+            chain = [0.0] * n
+            for i in range(n - 1, -1, -1):
+                chain[i] = max([chain[j] + lag for j, lag in bwd[i]] + [tail[i]])
+            for slack in SLACKS:
+                at = listed(latest(chain, lead), slack)
+                for _ in range(ROUNDS):
+                    at = listed(latest(listed(latest(at), slack, bwd, fwd, tail), lead), slack)
+                    r = latest(at)
+                    r = latest(place(sorted(range(n), key=lambda i: (r[i], -i)), bwd, tail))
+                    x = place(sorted(range(n), key=lambda i: (r[i], i)), fwd, [0.0] * n)
+                    end = sum(replay(sorted(range(n), key=lambda i: (x[i], i)), *o) for o in other)
                     if best is None or end < best[0]:
                         best = (end, x)
+        if CACHE:
+            LAID[n] = best
         if DBG.get("at"):
             best = (0, DBG["at"])
         DBG["end"] = best[0]
@@ -391,6 +443,7 @@ def rank_program(g, core, T, topo):
     cp, ms, tt, ts, act, mms, iota, keep, dma, arrive, send, issue = make(g, T)
     ranks = len(T.cores)
     lift = LIFT if ENG["bs"] == "s" else 0.0
+    up = (float(W), W + LIFT) if ENG["fs"] == "s" else (-2048.0, -2048.0)
 
     def f(name, w=None, a=0, rows=128):
         full = LOC[name][2] if name in LOC else SCRATCH[name][1][1]
@@ -416,15 +469,19 @@ def rank_program(g, core, T, topo):
     dma("s", T.la0[:, :], T.la[:, :], [], [f("la0")])
     dma("s", T.z0[:, :], T.zz[:, :], [], [f("z0")])
     dma("s", T.tI[:, :], T.th[:, :], [], [f("tI")])
-    dma("y", T.X[:, PAD:PAD + W // 2], T.x[:, :W // 2], [], [f("X", W // 2, PAD)], False, 4.5)
+    if XA:
+        dma("y", T.X[:, PAD:PAD + XA], T.x[:, :XA], [], [f("X", XA, PAD)], False, 4.5)
+    if BA:
+        dma("y", T.Bi[:, :BA], T.bk[:, :BA], [], [f("Bi", BA)], False, 4.5)
     ms(f("Fw"), 0.0)
-    ts(f("fh"), f("f0"), float(W), A.add)
+    ts(f("fh"), f("f0"), up[0], A.add)
     d = dma("y", T.Fw[0:128:16, PAD:PAD + W], T.fh[:, :], [f("fh")], [f("Fw")])
-    ts(f("fc"), f("f0"), W + LIFT, A.add)
+    ts(f("fc"), f("f0"), up[1], A.add)
     tt(f("fl"), f("fc"), f("fh"), A.subtract)
     d = dma("y", T.Fw[1:128:16, PAD:PAD + W], T.fl[:, :], [f("fl")], [f("Fw")], True)
-    d = dma("y", T.X[:, PAD + W // 2:PAD + W], T.x[:, W // 2:], [], [f("X", W // 2, PAD + W // 2)], False, 5.0, False, [d])
-    dma("y", T.Bi[:, :], T.bk[:, :], [], [f("Bi")], False, 7.0, False, [d])
+    d = dma("y", T.X[:, PAD + XA:PAD + W], T.x[:, XA:], [], [f("X", W - XA, PAD + XA)], False, 2.5 + (W - XA) / 900.0, False, [d])
+    if BA < C:
+        dma("y", T.Bi[:, BA:], T.bk[:, BA:], [], [f("Bi", C - BA, BA)], False, 2.5 + (W - XA + 2 * (C - BA)) / 900.0, False, [d])
     cp(f("L0"), f("la0"))
     iota(f("pi"), [[0, 1]], 1)
     iota(f("g16"), [[1, 8], [0, 16]], 0)
@@ -448,13 +505,16 @@ def rank_program(g, core, T, topo):
     ts(f("Bt", C, PAD), f("Bi"), lift, A.add)
     DBG["tag"] = (0, "k1")
     ts(f("SKu"), f("SK"), f("wu"), A.mult)
+    DBG["tag"] = (0, "k0")
     for h in range(2):
         ts(f("cS", 128, 128 * h), f("code"), 0.0, A.is_ge)
-    ts(f("cK"), f("code"), 0.0, A.is_ge, -(W + LIFT + 2048) / LV, A.mult)
+    if ENG["fs"] == "s":
+        ts(f("cK"), f("code"), 0.0, A.is_ge, -(W + LIFT + 2048) / LV, A.mult)
     ms(f("ones"), 1.0)
     ts(f("I"), f("code"), f("rp"), A.is_equal)
     ts(f("tr"), f("code"), f("rp"), A.is_ge)
     ts(f("oh"), f("s16"), f("rp"), A.is_equal)
+    DBG["tag"] = (0, "ks")
     for k in range(LV):
         times(sk(k, "SEL"), f("cS", 128), f("oh", 1, k))
     DBG["tag"] = (0, "k2")
@@ -468,9 +528,11 @@ def rank_program(g, core, T, topo):
         ts(sk(k, "LOST"), f("code"), f("la", 1, k), A.is_equal, f("lb", 1, k), A.mult)
     DBG["tag"] = (0, "k3")
     for n, m, s in (("In", "I", -1), ("I32", "I", 32), ("Ih", "I", 0.5), ("Iq", "I", -BIG / 2), ("I8", "I", BIG),
-                    ("C1", "tr", 2 ** 22), ("C3B", "tr", -BIG / 2), ("C3", "tr", -0.5), ("cQ", "cS", -1 / 64), ("c256", "cS", -256),
+                    ("C1", "tr", 2 ** 22), ("C3", "tr", -0.5), ("c256", "cS", -256),
                     ("t1", "I", 2 ** 16)):
         times(f(n), f(m, 128), float(s))
+    ts(f("Iz"), f("I"), 1023 / 1024, A.mult)
+    ts(f("Izh"), f("I"), 1023 / 2048, A.mult)
     tt(f("Cc"), f("C1"), f("t1"), A.add)
     ts(f("t2"), f("code"), f("rp"), A.is_gt, -BIG, A.mult)
     tt(f("C2B"), f("t2"), f("Iq"), A.subtract)
@@ -484,10 +546,13 @@ def rank_program(g, core, T, topo):
     ts(f("pi5"), f("pi"), 5, A.arith_shift_right)
     cp(f("r32"), f("pi4"))
     cp(f("p32"), f("pi5"))
-    for b in sorted(set(BLOCK.values())):
+    for b in (16, 32):
         r, s = f("rp" if b == 16 else "r32"), "%d" % b
         ts(f("mT" + s), f("q" + s), r, A.is_le, -15 * NULL / BIG, A.add)
         ts(f("mR" + s), f("q" + s), r, A.is_equal)
+        if b in BLOCK["F"] + (LAST["F"],):
+            times(f("m2" + s), f("mR" + s), 2.0)
+            tt(f("mF" + s), f("mT" + s), f("m2" + s), A.subtract)
         ts(f("bk" + s), f("g" + s), f("p" + s), A.is_equal, -1.0, A.mult)
         ts(f("dd" + s), f("s16"), f("p" + s), A.is_equal)
     line(f("rp1"), 1, 16)
@@ -496,35 +561,32 @@ def rank_program(g, core, T, topo):
     line(f("c613"), 613 * 32, 0)
     line(f("bW0"), -BIG, -BIG / 2)
     times(f("bW"), f("oh", 1, 15), BIG / 2, f("bW0"))
-    line(f("bH"), -1.5 * BIG, -BIG)
+    line(f("bH"), -BIG, -BIG / 2)
+    line(f("bQ"), -2 * BIG, BIG / 2)
     times(f("wN"), f("oh", 1, 15), BIG - 1, 1.0)
     line(f("bN0"), -0.5, 0.5)
     times(f("bN"), f("bN0"), f("wN"))
-    times(f("bhm"), f("oh", 1), -15 * NULL + 2048 + W)
-    times(f("blo"), f("oh", 1, 1), -15 * NULL + 2048 + W + LIFT)
+    times(f("bhm"), f("oh", 1), -15 * NULL + 2048 + up[0])
+    times(f("blo"), f("oh", 1, 1), -15 * NULL + 2048 + up[1])
     ts(f("Tn"), f("tI"), -1.0, A.mult, -0.5, A.add)
     ts(f("Tp"), f("tI"), 0.5 - BIG / 2, A.add)
     cp(f("thr"), f("Tn"))
     for c in range(NCH):
-        times(f("E", 16, ES * c + CE), f("s16"), 0.0)
+        act(f("E", 16, ES * c + CE), f("s16"), AF.Silu, 0.0, 0.0)
     DBG["tag"] = (0, "k4")
     if ENG["fs"] == "s":
         for a in range(0, PAD + W, 1032):
             iota(f("F32", 1032, a), [[0, 1032]], 0)
         for d in range(2):
             dma("g", T.F32[d:128:16, PAD:PAD + W], T.Fw[d:128:16, PAD:PAD + W], [f("Fw")], [f("F32")], d == 1, 3.0)
-    DBG["tag"] = (0, "k5")
-    for a in range(0, PAD + W, 1032):
-        iota(f("Ff", 1032, a), [[0, 1032]], 0, -int(W + LIFT))
 
     XW = f("X", W, PAD)
 
     def ent(name, c, a=0, n=CL):
         return f(name, LV * n, (ES if name == "E" else CE) * c + LV * a)
 
-    def cuts(k):
-        n = CL // CUT.get(k, 1)
-        return [(b, n) for b in range(0, CL, n)]
+    def cuts(s):
+        return ((CL // 2, CL // 2), (0, CL // 2)) if s in FINE else ((0, CL),)
 
     def copy(e, out, in_):
         if e == "s":
@@ -534,11 +596,12 @@ def rank_program(g, core, T, topo):
         else:
             keep(out, in_)
 
-    def turn(out, srcs, c, stop=True):
+    def turn(out, srcs, c, b, n, stop=True):
+        out = ps(out, CL * c + b, n)
         for i, src in enumerate(srcs):
-            a = ent(src, c)[1]
-            less = [(out, f("cK"), f("ones", CL), True, False)] * (src[0] == "F")
-            mms(less + [(out, sk(k), st(src, a + k, a + CE), i == 0 and k == 0 and not less, stop and k == LV - 1 and i == len(srcs) - 1)
+            a = ent(src, c, b, n)[1]
+            less = [(out, f("cK"), f("ones", n), True, False)] * (src[0] == "F" and ENG["fs"] == "s")
+            mms(less + [(out, sk(k), st(src, a + k, a + LV * n), i == 0 and k == 0 and not less, stop and k == LV - 1 and i == len(srcs) - 1)
                         for k in range(LV)])
 
     def ps(name, lane, n, at=None, rows=128):
@@ -548,42 +611,47 @@ def rank_program(g, core, T, topo):
     def each(o, r, by=LV):
         return (o[0], o[1] + r, o[2], by, o[4])
 
-    def sizes(e, src, dst, c):
+    def sizes(e, src, dst, c, b, n):
         if e == "s":
-            for b, n in cuts("ab"):
-                act(ent(dst, c, b, n), ent(src, c, b, n), AF.Abs)
+            act(ent(dst, c, b, n), ent(src, c, b, n), AF.Abs)
             return [dst]
-        ts(ent(dst, c), ent(src, c), 0.0, A.min, -2.0, A.mult)
+        ts(ent(dst, c, b, n), ent(src, c, b, n), 0.0, A.min, -2.0, A.mult)
         return [src, dst]
 
     def wrap(out, fam, src, a, n, start=True):
         mms([(out, sk(r, fam), st(src, a + r, a + n), start and r == 0, r == LV - 1) for r in range(LV)])
 
+    def block(tab, a):
+        return LAST[tab] if DBG["tag"][0] == VIS - 1 else BLOCK[tab][a // 128]
+
     def offs(tab, p, a, n, c):
-        if BLOCK.get(tab) == 32:
+        if block(tab, a) == 32:
             for h in range(2):
                 ts(st("of" + tab, a // 16 + h, (a + n) // 16, 2), st(p[0], p[1] + h, p[2], 2), c, A.add, f(("rp", "rp1")[h]), A.max)
         else:
             ts(st("of" + tab, a // 8, (a + n) // 8 - 1, 2), p, c, A.add, f("rp"), A.max)
 
-    def contest(tab, rows, a, n):
-        b = BLOCK[tab]
+    def contest(tab, rows, a, n, back=None):
+        b = block(tab, a)
         s, w, m = "%d" % b, 8 * b, b // 16
-        key, dif, lst = ps("key" + tab, a, w, 0, n), ps("dif" + tab, a, w, 0, n), ps("lst" + tab, a, n // 16, a % 128 // 16)
+        room = "F" if b > BLOCK[tab][a // 128] else tab
+        key, dif, lst = ps("key" + room, a, w, 0, n), ps("dif" + room, a, w, 0, n), ps("lst" + tab, a, n // 16, a % 128 // 16)
         wt, eq = f("WT" + tab, w, 0, n), f("eq" + tab, w, 0, n)
         mms([(key, f("I8", n), f("c75", w), True, False), (key, rows, f("cS", w), False, True)])
-        both = [(dif, f("I8", n), f("mT" + s), True, False), (dif, rows, f("cS", w), False, False)]
+        both = [(dif, f("I8", n), f(("mF" if back else "mT") + s), True, False), (dif, rows, f("cS", w), False, False)]
         if dif[0] != key[0]:
             mms(both)
         tt(wt, key, f("mR" + s, w, 0, n), A.mult)
-        mms(both * (dif[0] == key[0]) + [(dif, f("bk" + s, n, 0, n), wt, False, True)])
+        mms(both * (dif[0] == key[0]) + [(dif, f("bk" + s, n, 0, n), wt, False, not back)])
+        if back:
+            mm(dif, back(), f("cS", w), False, True)
         ts(eq, dif, 0.0, A.is_equal, -BIG, A.mult)
         mms([(each(lst, h, m), f(x + tab, 128, 128 * h, n), f("dd" + s, n // b, 0, n), x == "WT", x == "eq")
              for h in range(m) for x in ("WT", "eq")])
         offs(tab, lst, a, n, float(2048 + PAD))
 
     def scatter(tab, of, data, a, n, e="v"):
-        b = BLOCK.get(of, 16)
+        b = block(of, a)
         for s in range((a + n) // b - 1, a // b - 1, -1):
             out = ("@", f(tab), f("of" + of, b // 16, 2 * s))
             if e == "s":
@@ -613,52 +681,64 @@ def rank_program(g, core, T, topo):
                 for a in (PAD, PAD + W // 2):
                     dma("g", T.Ff[0:128:16, a:a + W // 2], T.Fw[d:128:16, a:a + W // 2], [f("Fw"), f("Ff", W // 2, a)], [f("Ff", W // 2, a)], False, 3.0, True)
         elif k == "fg":
-            for b, n in cuts(k):
-                copy(ENG["fg"][c], ent("FG", c, b, n), ("@", FW, f(L, n, CL * c + b)))
+            for b, n in cuts(s):
+                copy(ENG["fg"][c], ent("FG", c, b, n), ("@", FW, f("in%d" % v, n, CL * c + b + 128 * (c // 2)) if v and ONE else f(L, n, CL * c + b)))
+        elif k == "zc":
+            if v and ONE:
+                cp(ln(z), f("in%d" % v, 128, 2 * a + 128))
         elif k == "fh":
-            for b, n in cuts(k):
+            for b, n in cuts(s):
                 copy(ENG["fh"][c], ent("FH", c, b, n), ("@", FW, f("Bb", n, CL * c + b)))
         elif k == "zz":
             for i in range(LV):
                 e = ENG["zz" if v else "z0"][c]
                 copy(e[i % len(e)], st("z16", LV * a + i, LV * (a + 128)), ln(z))
+            if v == 2 and c == 0:
+                DBG["tag"] = (v, "k5")
+                for b in range(0, PAD + W, 1032):
+                    iota(f("Ff", 1032, b), [[0, 1032]], 0, -int(up[1]), [f("z16", CE)])
         elif k == "ce":
-            b = 16 * c
-            wrap(each(ps("cu", a, 16), 0, 2), "SKc", z, a, 128)
-            wrap(each(ps("cu", a, 16), 1, 2), "SKu", z, a, 128)
-            ts(f("i1", 16, b), ps("cu", a, 16), 255.0, A.add)
-            ts(f("i2", 16, b), f("i1", 16, b), 1023, A.bitwise_and)
-            cp(f("bl", 8, 8 * c), st("i2", b, b + 16, 2))
+            b, n = (24, 8) if c else (0, 24)
+            wrap(ps("cu", a, 8, n - 8), "SKc", z, a, 128)
+            if c == 0:
+                wrap(ps("cu", a, 16), "SKu", z, 0, K)
+            ts(f("i1", n, b), ps("cu", a, n), 255.0, A.add)
+            ts(f("i2", n, b), f("i1", n, b), 1023, A.bitwise_and)
+            cp(f("bl", 8, 8 * c), f("i2", 8, 16 + 8 * c))
             ts(ln("Bb"), ("@", f("Bt", C, PAD), f("bl", 8, 8 * c)), 0.25 - lift, A.add)
-            ts(f("bu", 16, b), f("i2", 16, b), 32.0, A.add)
-            mms([(each(ps("ub", a, 128), r), sk(r, "SEL"), st("bu", b + 1, b + 16, 2), True, True) for r in range(LV)])
+            if c == 0:
+                ts(f("bu"), f("i2"), 32.0, A.add)
+                mms([(each(ps("ub", 0, K), r), sk(r, "SEL"), f("bu", 16), True, True) for r in range(LV)])
         elif k == "cb":
-            keys = st("bu", 0, 32, 2)
+            keys = f("bu", 16, 16)
             dif, lst = ps("difB", 128, K), ps("lstB", 128, 16)
             mms([(each(dif, r), sk(r, "DF"), keys, True, True) for r in range(LV)])
             act(f("sgb"), dif, AF.Sign, 0.25)
             mms([(lst, f("I"), keys, True, False)] + [(lst, sk(r, "LOST"), st("sgb", r, K), False, r == LV - 1) for r in range(LV)])
             offs("B", lst, 0, K, float(PAD - 32))
         elif k == "xl":
-            turn(ps("FL", CL * c, CL), ["FG"], c)
-            ts(f("FLu", CL, CL * c), ps("FL", CL * c, CL), 2048.0, A.add)
-            for b, n in cuts(k):
+            for b, n in cuts(s):
+                turn("FL", ["FG"], c, b, n)
+                ts(f("FLu", n, CL * c + b), ps("FL", CL * c + b, n), 2048.0, A.add)
+            for b, n in cuts(s if s in FINE else s + "c"):
                 tt(ent("D", c, b, n), ("@", XW, f("FLu", n, CL * c + b)), ent("z16", c, b, n), A.subtract)
         elif k == "fl":
             act(ln("FLf"), pl("FL"), AF.Identity, 2048.0)
             ts(ln("FLc"), ln("FLu"), -2048.0, A.add)
         elif k == "yy":
-            tt(ln("y1"), pl("ub"), ln("FLf"), A.mult)
+            tt(ln("y1"), ps("ub", 0, 128, a), ln("FLf"), A.mult)
             if ENG["y2"][c] == "s":
                 act(ln("y2"), ln("y1"), AF.Identity, f("c613"))
             else:
                 ts(ln("y2"), ln("y1"), f("c613"), A.add)
         elif k == "da":
-            turn(ps("d", CL * c, CL), sizes(ENG["da"][c], "D", "DA", c), c)
+            for b, n in cuts(s):
+                turn("d", sizes(ENG["da"][c], "D", "DA", c, b, n), c, b, n)
         elif k == "xg":
-            turn(ps("G", CL * c, CL), ["FH"], c)
-            ts(f("Gu", CL, CL * c), ps("G", CL * c, CL), 2048.0, A.add)
-            for b, n in cuts(k):
+            for b, n in cuts(s):
+                turn("G", ["FH"], c, b, n)
+                ts(f("Gu", n, CL * c + b), ps("G", CL * c + b, n), 2048.0, A.add)
+            for b, n in cuts(s if s in FINE else s + "c"):
                 tt(ent("E", c, b, n), ("@", XW, f("Gu", n, CL * c + b)), ent("z16", c, b, n), A.subtract)
         elif k == "hl":
             tt(ln("hiC"), pl("G"), ln("FLc"), A.max)
@@ -676,8 +756,13 @@ def rank_program(g, core, T, topo):
                 ts(ln("ylo"), ln("nC"), 2048.0, A.add)
                 dma("y", T.yl[:, a:a + 128], T.ylo[:, a:a + 128], [ln("ylo")], [])
             else:
-                ts(ln("Ls" + nx), ln("nC"), 2048.0, A.add)
-                send(ln("Ls" + nx), ln("L" + nx), topo, core, dst, "L%d_%s" % (c, nx))
+                ts(f("go" + nx, 128, 2 * a) if ONE else ln("Ls" + nx), ln("nC"), 2048.0, A.add)
+        elif k == "sn":
+            if ONE:
+                if not last and c < 2:
+                    send([f("go" + nx, K, K * (1 - c))], [f("in" + nx, K, K * (1 - c))], topo, core, dst, "%d_%s" % (c, nx))
+            elif not last and c < len(SENDS):
+                send([f(x + "s" + nx, n, b) for x, b, n in SENDS[c]], [f(x + nx, n, b) for x, b, n in SENDS[c]], topo, core, dst, "%d_%s" % (c, nx))
         elif k == "cw":
             mms([(pl("Pw"), f("I"), ln("nC"), True, False), (pl("Pw"), f("C2f"), ln("fs"), False, True)])
             ts(ln("Vw"), pl("Pw"), f("bW"), A.add, NULL, A.max)
@@ -696,17 +781,22 @@ def rank_program(g, core, T, topo):
             scatter("Bt", "B", "newf" if lift else "new", a, 128, ENG["bs"])
             if last and c == 0:
                 if lift:
-                    ts(f("ybo"), f("Bt", C, PAD), ROUND - lift, A.add, -ROUND, A.add)
+                    if ENG["yb"] == "s":
+                        times(f("ybr"), f("Bt", C, PAD), 1.0, ROUND - lift)
+                        times(f("ybo"), f("ybr"), 1.0, -ROUND)
+                    else:
+                        ts(f("ybo"), f("Bt", C, PAD), ROUND - lift, A.add, -ROUND, A.add)
                     dma("y", T.yb[:, :], T.ybo[:, :], [f("ybo")], [], False, 4.5)
                 else:
                     dma("y", T.yb[:, :], T.Bt[:, PAD:PAD + C], [f("Bt")], [], False, 4.5)
         elif k == "xs":
             scatter("X2" if last else "X", "X", "val", a, 128)
             if last and c == 0:
-                dma("s", T.yx[:, :], T.X2[:, PAD:PAD + W], [f("X2")], [], False, 7.0)
+                dma("s", T.yx[:, :], T.X2[:, PAD:PAD + W], [f("X2")], [], False, XOUT)
         elif k == "ea":
-            turn(ps("e", CL * c, CL), sizes(ENG["ea"][c], "E", "EA", c), c, False)
-            mm(ps("e", CL * c, CL), f("Iq"), f("nq", CL, CL * c), False, True)
+            for b, n in cuts(s):
+                turn("e", sizes(ENG["ea"][c], "E", "EA", c, b, n), c, b, n, False)
+                mm(ps("e", CL * c + b, n), f("Iq"), f("nq", n, CL * c + b), False, True)
         elif k == "gs":
             act(f("gs", PARTS[c][1], PARTS[c][0]), ps("e", *PARTS[c]), AF.Sign, f("Tp"), -1.0)
         elif k == "mg":
@@ -723,11 +813,16 @@ def rank_program(g, core, T, topo):
         def ln(name, b=0):
             return f(name, n, a + b)
         hi, lo = ps("Ph", a, n), ps("Pl", a, n)
-        mms([(hi, f("I"), ln("hiC"), True, False), (hi, f("C3B"), ln("fs"), False, False)])
-        mm(hi, f("C2B"), ln("gs"), False, True)
-        mms([(lo, f("I"), ln("loC"), True, False), (lo, f("C3B"), ln("fs"), False, False), (lo, f("C2B"), ln("gs"), False, True)])
+        mms([(hi, f("I"), ln("hiC"), True, False), (hi, f("C2B"), ln("gs"), False, True)])
+        mms([(lo, f("I"), ln("loC"), True, False), (lo, f("C2B"), ln("gs"), False, True)])
         ts(ln("Vh"), hi, f("bH"), A.add, NULL, A.max)
-        contest("F", ln("Vh"), a, n)
+
+        def back():
+            mm(hi, f("t2"), ln("gs"), True, False)
+            mm(hi, f("C2B"), ln("fs"), False, True)
+            act(ln("qb"), hi, AF.Relu, f("bQ"))
+            return ln("qb")
+        contest("F", ln("Vh"), a, n, back)
         ts(ln("Vl"), lo, f("bH"), A.add, NULL, A.max)
         mm(lo, sk(0), ln("Vl"))
         if last:
@@ -741,7 +836,9 @@ def rank_program(g, core, T, topo):
             act(ln("lod"), lo, AF.Identity, f("blo"))
             scatter("F32" if ENG["fs"] == "s" else "Fw", "F", "lod", a, n, ENG["fs"])
             DBG["tag"] = (DBG["tag"][0], "aa")
-            act(f("sgc", 128, 128 * p, n), ps("keyF", a, 128, 0, n), AF.Sign, 3000.0)
+            key = ps("keyF", a, 128, 0, n)
+            mms([(key, ln("Vh"), f("cS", 128), True, False), (key, ln("qb"), f("bk16"), False, True)])
+            act(f("sgc", 128, 128 * p, n), key, AF.Sign, 3000.0 - 15 * NULL)
 
     def point(p, a, n, z, nx, last, dst):
         def ln(name, b=0):
@@ -750,24 +847,26 @@ def rank_program(g, core, T, topo):
         ix, pz = ps("ix", a, ns, s0 % 8), ps("Pz", a, n)
         mm(ps("np", a, n), f("C3"), ln("gs"))
         act(ln("npb"), ps("np", a, n), AF.Relu, f("bN"), f("wN"))
-        mms([(ix, f("I"), f("J", ns, s0), True, False)] + [(ix, sk(r), st("npb", a + r, a + n), False, r == LV - 1) for r in range(LV)])
+        if ENG["ix"][p] == "t":
+            mms([(ix, f("I"), f("J", ns, s0), True, False)] + [(ix, sk(r), st("npb", a + r, a + n), False, r == LV - 1) for r in range(LV)])
+        else:
+            mt = ps("np", a, 128, 0, n)
+            mm(mt, ln("npb"), f("cS", 128))
+            tt(f("WTz", 128, 0, n), mt, f("mR16", 128, 0, n), A.mult)
+            mms([(ix, f("I"), f("J", ns, s0), True, False), (ix, f("WTz", 128, 0, n), f("dd16", ns, 0, n), False, True)])
         ts(f("idx", ns, s0), ix, float(ES * (n // CL) - 1), A.min)
         copy(ENG["eg"], ln("Eg"), ("@", f("E", ES * (n // CL), ES * (a // CL)), f("idx", ns, s0)))
-        mms([(pz, f("I"), ln(z), True, False), (pz, f("cQ"), ln("ones"), False, False), (pz, f("Ih"), ln("Eg"), False, True)])
-        ts(ln(zs), pz, ROUND, A.add, -ROUND, A.add)
+        mms([(pz, f("Iz"), ln(z), True, False), (pz, f("Izh"), ln("Eg"), False, True)])
+        ts(f("go" + nx, n, 2 * a + 128) if ONE and not last else ln(zs), pz, ROUND, A.add, -ROUND, A.add)
         if last:
             dma("s", T.yz[:, a:a + n], T[zs][:, a:a + n], [ln(zs)], [])
-        else:
-            send(ln(zs), ln("z" + nx), topo, core, dst, "Z%d_%s" % (p, nx))
 
     for v in range(VIS):
         if v > 0:
             src = T.cores[(rank - 1 - (v - 1) % (ranks - 1)) % ranks]
             e = len(topo.engines(src, core))
-            for h in range(2):
-                arrive(f("L%d" % v, 128, 128 * h), "L%d_%d" % (h, v), e)
-            for p, (a, n) in enumerate(PARTS):
-                arrive(f("z%d" % v, n, a), "Z%d_%d" % (p, v), e)
+            for c, l in enumerate(SENDS):
+                arrive([f("in%d" % v, K, K * (1 - c))] if ONE else [f("%s%d" % (x, v), n, b) for x, b, n in l], "%d_%d" % (c, v), e)
         for s in (ORDER_LAST if v == VIS - 1 else ORDER_NEXT).split():
             DBG["tag"] = (v, s)
             step(s, v)

from concourse.bass import DstId, RemoteDMATransfer
from concourse.mybir import AluOpType as A, ActivationFunctionType as AF

VIS, W, C, K, LV = 5, 4096, 1024, 256, 16
PAD = 32
NCH = 4
CL = K // NCH
CE = CL * LV
ES = CE + 16
PARTS = ((128, 128), (0, 128))
NULL, BIG, ROUND, LIFT = -4096.0, 8192.0, 12582912.0, 64.0
FINE, LAST = ("xl0c", "xl1c", "xg0c", "xg1c"), {"X": 16, "F": 32, "B": 16}
XA, BA, XOUT = 0, 1024, 7.0
BLOCK = {"X": (16, 16), "F": (32, 16), "B": (16, 16)}
WAKE, CYC, PEC, GAT, SCA, SEND, FLY, ROUNDS = 160.0, 0.9, 0.5, 1.56, 3.8, 1600.0, 4000.0, 3
ENG = {"fg": "ssss", "fh": "ssss", "da": "sssv", "ea": "ssss", "zz": ("gggv", "gv"), "z0": ("g", "g"), "ix": "tv", "nf": "v", "y2": "vs", "eg": "v", "bs": "s", "fs": "s", "yb": "s"}
ONE = True
ORDER = ("zc1 zc0 fg3 fg2 ce1 zz1 xl3 xl2 fh3 fh2 fl1 xg3 xg2 hl1 ea3 ea2 gs0 zp0 ce0 yy1 zz0 cb fg1 fg0 xl1 xl0 fl0 yy0 da3 da2 fs1 nw1 cw1 vq1 "
         "fh1 fh0 mg0 xg1 xg0 hl0 da1 da0 fs0 ea1 ea0 gs1 mg1 zp1 nw0 cw0 vq0 bs1 bs0 xs1 xs0 sn0 sn1 sn2 sn3 ")
SENDS = ((("z", 128, 128), ("L", 128, 128)), (("z", 0, 128), ("L", 0, 128)))
ORDER_NEXT, ORDER_LAST = ORDER + "aa", "cp " + ORDER
RANK_NEXT = ("ea2 zp0 fs0 zp1 fg3 ea0 mg0 nw1 hl1 xl2 nw0 fl1 da2 xg2 ea3 xl3 ea1 gs0 gs1 aa hl0 da3 xg0 zz0 ce0 +zz1 k4 xg3 yy0 fs1 fh3 cw1 fh1 "
             "mg1 fg2 xg1 yy1 fg1 fl0 +ce1 bs0 cw0 xs1 in xs0 xl0 fh2 da1 k2 fg0 vq1 xl1 k1 cb fh0 vq0 k3 da0 bs1")
RANK_LAST = ("zp0 ea2 gs1 gs0 cp fs0 ea3 cw0 xg2 fg3 zp1 zz1 fl1 fl0 fh2 hl1 fg0 fh1 mg1 fg2 fh3 zz0 fs1 ea1 yy0 xg3 da1 hl0 yy1 ce0 ce1 ea0 xs1 "
             "nw0 cw1 xl3 xg0 nw1 vq1 xl0 bs1 xg1 cb fh0 vq0 da3 xl2 da2 da0 xs0 xl1 bs0 mg0 fg1")
FIRST, SLACK, CHAIN = {}, 0.0, 1e-6
for _v in range(VIS):
    for _i, _s in enumerate((RANK_LAST if _v == VIS - 1 else RANK_NEXT).split()):
        if _s[0] == "+":
            FIRST[(_v + 1, _s[1:])] = 1000 * _v + _i
            FIRST[(0, _s[1:])] = _i - 100
        else:
            FIRST.setdefault((_v, _s), 1000 * _v + _i)
FIRST[(0, "in")] = -200
LEAD, SLACKS = {"k0": 30, "ks": 10}, (0.0, 0.075, 0.15, 0.225, 0.3, 0.4)
LAID, CACHE, ONCE = {}, True, 3000.0
PLANS = ((160.0, 0.0, 1.0, 1.0, 1.0, 1.0), (160.0, 15.0, 0.95, 1.06, 1.0, 1.0))
OTHER = ((160.0, 0.0, 1.0, 1.0, 1.0, 1.0), (240.0, 20.0, 0.85, 0.85, 0.5, 0.8), (110.0, 20.0, 0.9, 0.9, 1.2, 1.3), (170.0, 0.0, 0.85, 1.15, 0.5, 1.3))

DBG = {"rw": [], "tag": None}
SCRATCH, LOC = {}, {}
DT2 = ("bfloat16", "float16", "uint16")
for _b, _d, _l in (
        ("", "bfloat16", "X 4128 X2 4128 Fw 4128 FG 4096 FH 4096 D 4096 E 4160 DA 4096 EA 4096 z16 4096 fh 256 fl 256 nq 256 "
         "fs 256 gs 256 qb 256 npb 256 sgb 256 eqF 256 eqX 256 sgc 384 hm 256 Eg 256"),
        ("kb", "bfloat16", "SK 2048 SKc 2048 SKu 2048 SEL 2048 DF 2048 LOST 2048 code 128 code2 128 cS 256 I 128 In 128 I32 128 Ih 128 "
         "Iq 128 I8 128 tr 128 C1 128 Cc 128 C2B 128 C3B 128 C3 128 C2f 128 cV 128 cQ 128 c256 128 HM 128 cK 128 c75 256 "
         "mF16 128 m216 128 mF32 256 m232 256 mT16 128 mR16 128 bk16 128 dd16 16 mT32 256 mR32 256 bk32 128 dd32 16 t1 128 t2 128 J 16 ones 256 q16 128 g16 128 q32 256 g32 128 tmp 128"),
        ("", "float32", "F32 4128 lod 256 Ff 4128 Bt 1056 fc 256 FLf 256 y1 256 y2 256 lof 256 ylo 256 newf 256 ybo 1024 ybr 1024"),
        ("kf", "float32", "s16 16 j16 16 oh 16 da 16 db 16 la 16 lb 16 rp 1 p16 1 r32 1 p32 1 wc 1 wu 1 wv 1 n15 1 "
         "c613 1 bW0 1 bW 1 bH 1 bQ 1 wN 1 bN0 1 bN 1 bhm 1 blo 1 r16 1 rp1 1 Tn 1 Tp 1 thr 1"),
        ("", "int32", "Bi 1024 tI 1 f0 256 la0 256 i1 32 i2 32 rr 256 new 256 vq 256 val 256"),
        ("ki", "int32", "pi 1 pi2 1 pi3 1 pi4 1 pi5 1 a1 1 a2 1"),
        ("", "float16", "bu 32 FLc 256 hiC 256 loC 256 nC 256 Vw 256 Vh 256 Vl 256 WTF 256 WTX 256 WTz 128 Iz 128 Izh 128"),
        ("", "uint16", "bl 16 Bb 256 FLu 256 Gu 256 ofB 32 ofX 32 ofF 32 idx 16")):
    _l, _c = _l.split(), 0
    for _i in range(0, len(_l), 2):
        _n, _w = _l[_i], int(_l[_i + 1])
        if _b:
            LOC[_n] = (_b, _c, _w)
            _c += (_w + 15) // 16 * 16
            SCRATCH[_b] = ("sbuf", [128, _c], _d)
        else:
            SCRATCH[_n] = ("sbuf", [128, _w], _d)
for _v in range(VIS + 1):
    if _v < VIS:
        SCRATCH["L%d" % _v] = ("sbuf", [128, K], "uint16")
        SCRATCH["z%d" % _v] = ("sbuf", [128, K], "bfloat16")
    if _v > 0:
        SCRATCH["zs%d" % _v] = ("sbuf", [128, K], "bfloat16")
    if 0 < _v < VIS:
        SCRATCH["Ls%d" % _v] = ("sbuf", [128, K], "uint16")
        SCRATCH["go%d" % _v] = ("sbuf", [128, 2 * K], "uint16")
        SCRATCH["in%d" % _v] = ("sbuf", [128, 2 * K], "uint16")
PSUM = ("a0", "b0", "c0", "d0", "a1p", "b1", "c1", "d1")
PLACE = {"FL": (0, 0), "G": (0, 128), "difF": (0, 256),
         "d": (1, 0), "M": (1, 0), "Pw": (1, 0), "keyX": (1, 0), "difX": (1, 128), "ub": (0, 256), "Q": (1, 256), "lstX": (1, 384),
         "cu": (1, 392), "ix": (2, 256), "lstB": (3, 416), "difB": (0, 256),
         "e": (2, 0), "np": (2, 0), "Pz": (2, 0), "dl": (2, 128), "Pl": (2, 128),
         "Ph": (3, 0), "keyF": (3, 128), "lstF": (3, 384), "aa": (3, 400)}
for _n in PSUM:
    SCRATCH[_n] = ("psum", [128, 512], "float32")
NDMA = 28
SEMAPHORES = ["q_v", "q_s", "q_t", "q_g"] + ["d%d" % i for i in range(NDMA)]
for _v in range(1, VIS):
    for _p in range(4):
        SEMAPHORES += ["a%s_%d" % (_p, _v), "l%s_%d" % (_p, _v)]


def make(g, T):
    queues = {"v": g.vector, "s": g.scalar, "t": g.tensor, "g": g, "y": g.sync}
    ops, hw, hr, bank, marks = [], {}, {}, [], {}
    nd, fence = [0, False], {}

    def ap(o):
        if o[0] == "@":
            return ap(o[1]).indirect(ap(o[2]))
        b, a = (LOC[o[0]][0], LOC[o[0]][1]) if o[0] in LOC else (o[0], 0)
        rows = slice(None) if o[4] == 128 else slice(0, o[4])
        if o[3] != 1:
            return T[b][rows, a + o[1]:a + o[2]:o[3]]
        return T[b][rows, a + o[1]:a + o[2]]

    def regs(o):
        if o is None or isinstance(o, (int, float)):
            return []
        if o[0] == "@":
            return regs(o[1]) + regs(o[2])
        return [o]

    def val(o):
        return o if o is None or isinstance(o, (int, float)) else ap(o)

    def meet(h, o):
        return h[0] < o[2] and o[1] < h[1] and not (h[3] == o[3] and (h[0] - o[1]) % o[3])

    def rec(q, reads, writes, call, cost, tail=0.0, tok=None, own=True, extra=(), beside=False):
        i = len(ops)
        deps = {}

        def dep(j, w):
            deps[j] = deps.get(j, False) or w
        for o, w in [(r, False) for r in reads] + [(r, True) for r in writes]:
            if w and beside:
                continue
            for h in hw.get(o[0], []):
                if meet(h, o):
                    dep(h[2], not (own and ops[h[2]][0] == q and w and q == "t"))
            if w:
                for h in hr.get(o[0], []):
                    if meet(h, o):
                        dep(h[2], not (own and ops[h[2]][0] == q and ops[h[2]][5] is None))
        bank.append(sorted(set(o[0] for o in reads + writes if o[0] in PSUM)))
        for j, w in list(extra) + (list(ops[hw[writes[0][0]][-1][2]][2].items()) if beside else []):
            dep(j, w)
        ops.append((q, call, deps, cost, tail, tok))
        DBG["rw"].append((DBG["tag"], reads, writes))
        for o in reads:
            hr.setdefault(o[0], []).append((o[1], o[2], i, o[3]))
        for o in writes:
            if o[3] == 1 and o[4] == 128 and not beside:
                for h in (hw, hr):
                    h[o[0]] = [e for e in h.get(o[0], []) if not (o[1] <= e[0] and e[1] <= o[2])]
            hw.setdefault(o[0], []).append((o[1], o[2], i, o[3]))
        return i

    def num(o):
        if o[0] == "@":
            return LV * num(o[2])
        return -(-(o[2] - o[1]) // o[3])

    def two(*l):
        for o in l:
            o = o[1] if o[0] == "@" else o
            if SCRATCH[LOC[o[0]][0] if o[0] in LOC else o[0]][2] not in DT2:
                return 1.0
        return 0.5

    def work(q, out, ins, call, rate):
        n, fixed = num(out), 50.0 if q == "v" else 65.0
        cost = max(64.0, rate * n) * CYC
        for o in ins:
            if not isinstance(o, (int, float)) and o[0] == "@":
                cost = fixed + GAT * n * CYC
        if out[0] == "@":
            cost = fixed + SCA * n * CYC
        reads, writes = sum([regs(o) for o in ins], []), regs(out)
        if out[0] == "@":
            reads, writes = reads + regs(out[2]), regs(out[1])
        rec(q, reads, writes, call, cost)

    def cp(out, in_):
        work("v", out, [in_], lambda e: e.tensor_copy(ap(out), ap(in_)), two(out, in_))

    def ms(out, c):
        work("v", out, [], lambda e: e.memset(ap(out), c), two(out))

    def tt(out, a, b, op):
        work("v", out, [a, b], lambda e: e.tensor_tensor(ap(out), ap(a), ap(b), op), 1.0 if a[0] in PSUM or b[0] in PSUM else 2.0)

    def ts(out, a, s1, op0, s2=None, op1=None):
        ins = [o for o in (a, s1, s2) if o is not None]
        if op1 is None:
            work("v", out, ins, lambda e: e.tensor_scalar(ap(out), ap(a), val(s1), None, op0), two(out, a))
        else:
            work("v", out, ins, lambda e: e.tensor_scalar(ap(out), ap(a), val(s1), val(s2), op0, op1), two(out, a))

    def act(out, in_, func, bias=0.0, scale=1.0):
        kw = {}
        if not (isinstance(bias, float) and bias == 0.0):
            kw["bias"] = val(bias)
        if not (isinstance(scale, float) and scale == 1.0):
            kw["scale"] = val(scale)
        first = func == AF.Silu and not nd[1]
        nd[1] = nd[1] or first
        work("s", out, [in_, bias, scale], lambda e: e.activation(ap(out), ap(in_), func, **kw), 100.0 if first else 1.0)

    def mms(l):
        since = fence.setdefault(l[0][0][0], [])
        opens = l[0][3] and not l[-1][4]
        i = rec("t", [o for m in l for o in m[1:3]], [m[0] for m in l],
                [lambda e, m=m: e.matmul(ap(m[0]), ap(m[1]), ap(m[2]), m[3], m[4]) for m in l], sum(max(64.0, num(m[0])) * PEC for m in l),
                extra=[(j, False) for j in (since if opens else since[:1])])
        if l[-1][4] and not l[0][3]:
            del since[:]
        since.append(i)

    def iota(out, pattern, mult, base=0, after=()):
        rec("g", list(after), regs(out), lambda e: e.iota(ap(out), pattern, base, mult, allow_small_or_imprecise_dtypes=True), 130.0 + 2 * CYC * num(out))

    def keep(out, in_):
        rec("g", regs(in_), regs(out), lambda e: e.affine_select(ap(out), ap(in_), [[0, num(out)]], A.is_equal, 0.0, 0, 0), 170.0 + 2 * CYC * num(out))

    def dma(q, out, in_, reads, writes, beside=False, us=2.5, add=False, after=()):
        s = "d%d" % nd[0]
        nd[0] += 1
        kw = {"accum_op": A.add} if add else {}
        return rec(q, reads, writes, lambda e: e.dma_start(out, in_, **kw), 70.0, 1000.0 * us, (s, 16), False, [(j, False) for j in after], beside)

    def arrive(o, mark, v):
        rec(None, [], o, None, 0.0, 0.0, ("a" + mark, v), False, [(marks[mark], True)])

    def send(srcs, outs, topo, core, dst, mark):
        rid, pid = topo.addr(dst)[0:2]
        eng = topo.engines(core, dst)
        m = len(eng) // len(srcs)

        def call(e):
            if len(srcs) == 1:
                return e.remote_dma(ap(outs[0]), ap(srcs[0]), T.sem["a" + mark], T.sem["l" + mark], pid, rid, topo.mask(core, dst))
            return e.remote_dma_fused([RemoteDMATransfer(dst_ids=[DstId(rid=rid, pnc=pid)], dma_engine_mask=sum(1 << x for x in eng[m * i:m * i + m]),
                                                         remote_sem=T.sem["a" + mark], src=ap(srcs[i]), dst=ap(outs[i])) for i in range(len(srcs))],
                                      local_sem=T.sem["l" + mark])
        marks[mark] = rec("g", srcs, [], call, SEND, FLY + ONCE * (not marks), ("l" + mark, len(eng)), False)

    def issue():
        n = len(ops)
        cost, tail, wake = [0.0] * n, [0.0] * n, [0.0]
        fwd, bwd = [[] for _ in ops], [[] for _ in ops]

        def priced(more, long, pe, send, fly):
            r = []
            for q, _, _, c, e, _ in ops:
                if q == "t":
                    c *= pe
                elif c == SEND:
                    c, e = c * send, e * fly
                elif q in ("v", "s") and not e:
                    c = c * long if c > 700 else c + more
                r.append((c, e))
            return r

        def assume(costs):
            wake[0] = costs[0]
            for i, (c, e) in enumerate(priced(*costs[1:])):
                cost[i], tail[i], fwd[i][:], bwd[i][:] = c, e, [], []
            for i, op in enumerate(ops):
                for j in op[2]:
                    lag = cost[j] + ((tail[j] + (wake[0] if op[0] else 0.0)) if op[2][j] else 0.0)
                    fwd[i].append((j, lag))
                    bwd[j].append((i, lag + cost[i] - cost[j]))
        assume(PLANS[0])

        def place(order, first, least):
            at, busy = [0.0] * n, {q: [] for q in list(queues) + list(PSUM)}
            for i in order:
                t, q, c = max([at[j] + lag for j, lag in first[i]] + [least[i]]), ops[i][0], cost[i]
                if q:
                    t0 = -1.0
                    while t0 < t:
                        t0 = t
                        for r, gap in [(q, 0.0)] + [(b, wake[0]) for b in bank[i]]:
                            b = busy[r]
                            k = len(b)
                            while k and b[k - 1][1] + gap > t:
                                k -= 1
                            while k < len(b) and b[k][0] < t + c + gap:
                                if b[k][2] != q or not gap:
                                    t = max(t, b[k][1] + gap)
                                k += 1
                    for r in [q] + bank[i]:
                        b = busy[r]
                        k = len(b)
                        while k and b[k - 1][0] > t:
                            k -= 1
                        b.insert(k, (t, t + c, q))
                at[i] = t
            return at

        def ranked(rank):
            order, seen = [], [False] * n
            for i in sorted(range(n), key=lambda i: (rank[i], i)):
                todo = [i]
                while todo:
                    j = todo[-1]
                    miss = [k for k, _ in fwd[j] if not seen[k]]
                    if miss:
                        todo.append(min(miss))
                    else:
                        todo.pop()
                        if not seen[j]:
                            seen[j] = True
                            order.append(j)
            return order

        def listed(rank, slack, fwd=fwd, bwd=bwd, least=[0.0] * n):
            at, left, ready = [0.0] * n, [len(x) for x in fwd], {q: [] for q in queues}
            free, held, todo = {q: 0.0 for q in queues}, {b: {} for b in PSUM}, [i for i in range(n) if not fwd[i]]
            while True:
                while todo:
                    i = todo.pop()
                    at[i] = max([at[j] + lag for j, lag in fwd[i]] + [least[i]])
                    if ops[i][0]:
                        ready[ops[i][0]].append(i)
                        continue
                    for j, _ in bwd[i]:
                        left[j] -= 1
                        if not left[j]:
                            todo.append(j)
                best = None
                for q in queues:
                    if ready[q]:
                        c = [(max([at[i], free[q]] + [held[b][r] + wake[0] for b in bank[i] for r in held[b] if r != q]), i) for i in ready[q]]
                        m = min(c)[0]
                        i = min([(s, rank[i], i) for s, i in c])[2]
                        s, i = min([(rank[j], s, j) for s, j in c if s <= m + slack * cost[i]])[1:]
                        if best is None or s < best[0]:
                            best = (s, q, i)
                if best is None:
                    return at
                s, q, i = best
                ready[q].remove(i)
                at[i], free[q] = s, s + cost[i]
                for b in bank[i]:
                    held[b][q] = s + cost[i]
                for j, _ in bwd[i]:
                    left[j] -= 1
                    if not left[j]:
                        todo.append(j)

        def rounds(order, m):
            best = None
            for r in range(m):
                at = place(order, fwd, [0.0] * n)
                end = max(at[i] + cost[i] + tail[i] for i in range(n))
                if best is None or end < best[0]:
                    best = (end, at)
                if r < m - 1:
                    back = place(sorted(range(n), key=lambda i: (-at[i] - cost[i], -i)), bwd, tail)
                    order = sorted(range(n), key=lambda i: (-back[i] - cost[i], i))
            return best
        if DBG.get("only"):
            DBG.update(place=place, rounds=rounds, ranked=ranked, listed=listed, fwd=fwd, bwd=bwd, cost=cost, tail=tail, ops=ops, bank=bank)
            return
        lead = [1000.0 * LEAD.get("FL"[t[0] // 4] + t[1] if t[0] % 4 == 0 else t[1], LEAD.get(t[1], 0)) for t, _, _ in DBG["rw"][-n:]]

        def latest(t, by=[0.0] * n):
            return [-t[i] - cost[i] - by[i] for i in range(n)]

        def replay(x, w, times):
            done, free, held = [0.0] * n, {q: 0.0 for q in queues}, {b: {} for b in PSUM}
            for i in x:
                q, (c, e) = ops[i][0], times[i]
                t = max([done[j] + (w if q else 0.0) for j in ops[i][2] if ops[i][2][j]] + [held[b][r] + w for b in bank[i] for r in held[b] if r != q]
                        + [free.get(q, 0.0)])
                free[q], done[i] = (t + c if q else 0.0), t + c + e
                for b in bank[i]:
                    held[b][q] = t + c
            return max(done)
        best, other = LAID.get(n), [(o[0], priced(*o[1:])) for o in OTHER]
        for costs in PLANS * (best is None):
            assume(costs)
            chain = [0.0] * n
            for i in range(n - 1, -1, -1):
                chain[i] = max([chain[j] + lag for j, lag in bwd[i]] + [tail[i]])
            for slack in SLACKS:
                at = listed(latest(chain, lead), slack)
                for _ in range(ROUNDS):
                    at = listed(latest(listed(latest(at), slack, bwd, fwd, tail), lead), slack)
                    r = latest(at)
                    r = latest(place(sorted(range(n), key=lambda i: (r[i], -i)), bwd, tail))
                    x = place(sorted(range(n), key=lambda i: (r[i], i)), fwd, [0.0] * n)
                    end = sum(replay(sorted(range(n), key=lambda i: (x[i], i)), *o) for o in other)
                    if best is None or end < best[0]:
                        best = (end, x)
        if CACHE:
            LAID[n] = best
        if DBG.get("at"):
            best = (0, DBG["at"])
        DBG["end"] = best[0]
        seq = sorted(range(n), key=lambda i: (best[1][i], i))
        holder = {b: {} for b in PSUM}
        for i in seq:
            for b in bank[i]:
                for q in holder[b]:
                    if q != ops[i][0]:
                        ops[i][2][holder[b][q]] = True
                holder[b][ops[i][0]] = i
        clk, snap, final = {q: {} for q in queues}, {}, {}
        cnt, token = {"v": 0, "s": 0, "t": 0, "g": 0}, {}

        def wait(q, tok):
            s, v = tok
            if clk[q].get(s, 0) >= v:
                return
            queues[q].wait_ge(T.sem[s], v)
            for a in snap[tok]:
                if clk[q].get(a, 0) < snap[tok][a]:
                    clk[q][a] = snap[tok][a]
            clk[q][s] = v
        for i in seq:
            q, call, deps, _, _, tok = ops[i]
            need = {}
            for j in deps:
                if deps[j] and q is not None:
                    need[token[j][0]] = max(need.get(token[j][0], 0), token[j][1])
            for s in need:
                wait(q, (s, need[s]))
            if q is None:
                snap[tok] = {}
            else:
                own = tok is None
                for one in (call if isinstance(call, list) else [call]):
                    ins = one(queues[q])
                    if own:
                        cnt[q] += 1
                        tok = ("q_" + q, cnt[q])
                        ins.then_inc(T.sem[tok[0]], 1)
                    elif tok[0][0] == "d":
                        ins.then_inc(T.sem[tok[0]], 16)
                snap[tok] = dict(clk[q])
            token[i] = tok
            final[tok[0]] = max(final.get(tok[0], 0), tok[1])
        for s in final:
            wait("g", (s, final[s]))
    return cp, ms, tt, ts, act, mms, iota, keep, dma, arrive, send, issue


def rank_program(g, core, T, topo):
    rank = T.rank_of(core)
    if rank is None:
        return
    cp, ms, tt, ts, act, mms, iota, keep, dma, arrive, send, issue = make(g, T)
    ranks = len(T.cores)
    lift = LIFT if ENG["bs"] == "s" else 0.0
    up = (float(W), W + LIFT) if ENG["fs"] == "s" else (-2048.0, -2048.0)

    def f(name, w=None, a=0, rows=128):
        full = LOC[name][2] if name in LOC else SCRATCH[name][1][1]
        return (name, a, full if w is None else a + w, 1, rows)

    def st(name, a, end, by=LV):
        return (name, a, end, by, 128)

    def sk(k, name="SK"):
        return f(name, 128, 128 * k)

    def mm(out, lhsT, rhs, start=True, stop=True):
        mms([(out, lhsT, rhs, start, stop)])

    def times(out, in_, a, b=0.0):
        act(out, in_, AF.Identity, b, a)

    def line(out, a, b):
        times(out, f("rp"), float(a), float(b))

    DBG["tag"] = (0, "in")
    dma("y", T.f0[:, :], T.fw[:, :], [], [f("f0")])
    dma("s", T.la0[:, :], T.la[:, :], [], [f("la0")])
    dma("s", T.z0[:, :], T.zz[:, :], [], [f("z0")])
    dma("s", T.tI[:, :], T.th[:, :], [], [f("tI")])
    if XA:
        dma("y", T.X[:, PAD:PAD + XA], T.x[:, :XA], [], [f("X", XA, PAD)], False, 4.5)
    if BA:
        dma("y", T.Bi[:, :BA], T.bk[:, :BA], [], [f("Bi", BA)], False, 4.5)
    ms(f("Fw"), 0.0)
    ts(f("fh"), f("f0"), up[0], A.add)
    d = dma("y", T.Fw[0:128:16, PAD:PAD + W], T.fh[:, :], [f("fh")], [f("Fw")])
    ts(f("fc"), f("f0"), up[1], A.add)
    tt(f("fl"), f("fc"), f("fh"), A.subtract)
    d = dma("y", T.Fw[1:128:16, PAD:PAD + W], T.fl[:, :], [f("fl")], [f("Fw")], True)
    d = dma("y", T.X[:, PAD + XA:PAD + W], T.x[:, XA:], [], [f("X", W - XA, PAD + XA)], False, 2.5 + (W - XA) / 900.0, False, [d])
    if BA < C:
        dma("y", T.Bi[:, BA:], T.bk[:, BA:], [], [f("Bi", C - BA, BA)], False, 2.5 + (W - XA + 2 * (C - BA)) / 900.0, False, [d])
    cp(f("L0"), f("la0"))
    iota(f("pi"), [[0, 1]], 1)
    iota(f("g16"), [[1, 8], [0, 16]], 0)
    iota(f("q16"), [[0, 8], [1, 16]], 0)
    iota(f("s16"), [[1, 16]], 0)
    iota(f("g32"), [[1, 4], [0, 32]], 0)
    iota(f("q32"), [[16, 2], [0, 8], [1, 16]], 0)
    for a, n in PARTS:
        iota(f("j16", n // 16, a // 16), [[ES, n // CL], [256, CL // 16]], 0)
    ts(f("pi2"), f("pi"), 15, A.bitwise_and)
    ts(f("pi3"), f("pi"), 4, A.arith_shift_right)
    cp(f("rp"), f("pi2"))
    cp(f("p16"), f("pi3"))
    ts(f("tmp"), f("g16"), f("p16"), A.not_equal, -100.0, A.mult)
    tt(f("code"), f("tmp"), f("q16"), A.add)
    line(f("wc"), 14, 39)
    line(f("wu"), 10, 5)
    for k in range(LV):
        ts(sk(k), f("code"), float(k), A.is_equal)
    act(f("SKc"), f("SK"), AF.Identity, 0.0, f("wc"))
    ts(f("Bt", C, PAD), f("Bi"), lift, A.add)
    DBG["tag"] = (0, "k1")
    ts(f("SKu"), f("SK"), f("wu"), A.mult)
    DBG["tag"] = (0, "k0")
    for h in range(2):
        ts(f("cS", 128, 128 * h), f("code"), 0.0, A.is_ge)
    if ENG["fs"] == "s":
        ts(f("cK"), f("code"), 0.0, A.is_ge, -(W + LIFT + 2048) / LV, A.mult)
    ms(f("ones"), 1.0)
    ts(f("I"), f("code"), f("rp"), A.is_equal)
    ts(f("tr"), f("code"), f("rp"), A.is_ge)
    ts(f("oh"), f("s16"), f("rp"), A.is_equal)
    DBG["tag"] = (0, "ks")
    for k in range(LV):
        times(sk(k, "SEL"), f("cS", 128), f("oh", 1, k))
    DBG["tag"] = (0, "k2")
    tt(f("code2"), f("cS", 128), f("I"), A.add)
    ts(f("da"), f("s16"), f("rp"), A.not_equal, 1.0, A.add)
    ts(f("db"), f("s16"), f("rp"), A.not_equal, -0.5, A.add)
    ts(f("la"), f("s16"), f("rp"), A.max)
    ts(f("lb"), f("s16"), f("rp"), A.not_equal, -BIG / 2, A.mult)
    for k in range(LV):
        ts(sk(k, "DF"), f("code2"), f("da", 1, k), A.is_equal, f("db", 1, k), A.mult)
        ts(sk(k, "LOST"), f("code"), f("la", 1, k), A.is_equal, f("lb", 1, k), A.mult)
    DBG["tag"] = (0, "k3")
    for n, m, s in (("In", "I", -1), ("I32", "I", 32), ("Ih", "I", 0.5), ("Iq", "I", -BIG / 2), ("I8", "I", BIG),
                    ("C1", "tr", 2 ** 22), ("C3", "tr", -0.5), ("c256", "cS", -256),
                    ("t1", "I", 2 ** 16)):
        times(f(n), f(m, 128), float(s))
    ts(f("Iz"), f("I"), 1023 / 1024, A.mult)
    ts(f("Izh"), f("I"), 1023 / 2048, A.mult)
    tt(f("Cc"), f("C1"), f("t1"), A.add)
    ts(f("t2"), f("code"), f("rp"), A.is_gt, -BIG, A.mult)
    tt(f("C2B"), f("t2"), f("Iq"), A.subtract)
    times(f("n15"), f("oh", 1, 15), -1.0, 1.0)
    times(f("C2f"), f("C2B"), f("n15"))
    times(f("wv"), f("oh", 1), 255.75, -256.0)
    times(f("cV"), f("cS", 128), f("wv"))
    tt(f("HM"), sk(0), sk(1), A.subtract)
    ms(f("c75"), -15 * NULL / BIG)
    ts(f("pi4"), f("pi"), 31, A.bitwise_and)
    ts(f("pi5"), f("pi"), 5, A.arith_shift_right)
    cp(f("r32"), f("pi4"))
    cp(f("p32"), f("pi5"))
    for b in (16, 32):
        r, s = f("rp" if b == 16 else "r32"), "%d" % b
        ts(f("mT" + s), f("q" + s), r, A.is_le, -15 * NULL / BIG, A.add)
        ts(f("mR" + s), f("q" + s), r, A.is_equal)
        if b in BLOCK["F"] + (LAST["F"],):
            times(f("m2" + s), f("mR" + s), 2.0)
            tt(f("mF" + s), f("mT" + s), f("m2" + s), A.subtract)
        ts(f("bk" + s), f("g" + s), f("p" + s), A.is_equal, -1.0, A.mult)
        ts(f("dd" + s), f("s16"), f("p" + s), A.is_equal)
    line(f("rp1"), 1, 16)
    line(f("r16"), 16, 0)
    ts(f("J"), f("j16"), f("r16"), A.add)
    line(f("c613"), 613 * 32, 0)
    line(f("bW0"), -BIG, -BIG / 2)
    times(f("bW"), f("oh", 1, 15), BIG / 2, f("bW0"))
    line(f("bH"), -BIG, -BIG / 2)
    line(f("bQ"), -2 * BIG, BIG / 2)
    times(f("wN"), f("oh", 1, 15), BIG - 1, 1.0)
    line(f("bN0"), -0.5, 0.5)
    times(f("bN"), f("bN0"), f("wN"))
    times(f("bhm"), f("oh", 1), -15 * NULL + 2048 + up[0])
    times(f("blo"), f("oh", 1, 1), -15 * NULL + 2048 + up[1])
    ts(f("Tn"), f("tI"), -1.0, A.mult, -0.5, A.add)
    ts(f("Tp"), f("tI"), 0.5 - BIG / 2, A.add)
    cp(f("thr"), f("Tn"))
    for c in range(NCH):
        act(f("E", 16, ES * c + CE), f("s16"), AF.Silu, 0.0, 0.0)
    DBG["tag"] = (0, "k4")
    if ENG["fs"] == "s":
        for a in range(0, PAD + W, 1032):
            iota(f("F32", 1032, a), [[0, 1032]], 0)
        for d in range(2):
            dma("g", T.F32[d:128:16, PAD:PAD + W], T.Fw[d:128:16, PAD:PAD + W], [f("Fw")], [f("F32")], d == 1, 3.0)

    XW = f("X", W, PAD)

    def ent(name, c, a=0, n=CL):
        return f(name, LV * n, (ES if name == "E" else CE) * c + LV * a)

    def cuts(s):
        return ((CL // 2, CL // 2), (0, CL // 2)) if s in FINE else ((0, CL),)

    def copy(e, out, in_):
        if e == "s":
            act(out, in_, AF.Copy)
        elif e == "v":
            cp(out, in_)
        else:
            keep(out, in_)

    def turn(out, srcs, c, b, n, stop=True):
        out = ps(out, CL * c + b, n)
        for i, src in enumerate(srcs):
            a = ent(src, c, b, n)[1]
            less = [(out, f("cK"), f("ones", n), True, False)] * (src[0] == "F" and ENG["fs"] == "s")
            mms(less + [(out, sk(k), st(src, a + k, a + LV * n), i == 0 and k == 0 and not less, stop and k == LV - 1 and i == len(srcs) - 1)
                        for k in range(LV)])

    def ps(name, lane, n, at=None, rows=128):
        b, a = PLACE[name]
        return f(PSUM[4 * (lane // 128) + b], n, a + (lane % 128 if at is None else at), rows)

    def each(o, r, by=LV):
        return (o[0], o[1] + r, o[2], by, o[4])

    def sizes(e, src, dst, c, b, n):
        if e == "s":
            act(ent(dst, c, b, n), ent(src, c, b, n), AF.Abs)
            return [dst]
        ts(ent(dst, c, b, n), ent(src, c, b, n), 0.0, A.min, -2.0, A.mult)
        return [src, dst]

    def wrap(out, fam, src, a, n, start=True):
        mms([(out, sk(r, fam), st(src, a + r, a + n), start and r == 0, r == LV - 1) for r in range(LV)])

    def block(tab, a):
        return LAST[tab] if DBG["tag"][0] == VIS - 1 else BLOCK[tab][a // 128]

    def offs(tab, p, a, n, c):
        if block(tab, a) == 32:
            for h in range(2):
                ts(st("of" + tab, a // 16 + h, (a + n) // 16, 2), st(p[0], p[1] + h, p[2], 2), c, A.add, f(("rp", "rp1")[h]), A.max)
        else:
            ts(st("of" + tab, a // 8, (a + n) // 8 - 1, 2), p, c, A.add, f("rp"), A.max)

    def contest(tab, rows, a, n, back=None):
        b = block(tab, a)
        s, w, m = "%d" % b, 8 * b, b // 16
        room = "F" if b > BLOCK[tab][a // 128] else tab
        key, dif, lst = ps("key" + room, a, w, 0, n), ps("dif" + room, a, w, 0, n), ps("lst" + tab, a, n // 16, a % 128 // 16)
        wt, eq = f("WT" + tab, w, 0, n), f("eq" + tab, w, 0, n)
        mms([(key, f("I8", n), f("c75", w), True, False), (key, rows, f("cS", w), False, True)])
        both = [(dif, f("I8", n), f(("mF" if back else "mT") + s), True, False), (dif, rows, f("cS", w), False, False)]
        if dif[0] != key[0]:
            mms(both)
        tt(wt, key, f("mR" + s, w, 0, n), A.mult)
        mms(both * (dif[0] == key[0]) + [(dif, f("bk" + s, n, 0, n), wt, False, not back)])
        if back:
            mm(dif, back(), f("cS", w), False, True)
        ts(eq, dif, 0.0, A.is_equal, -BIG, A.mult)
        mms([(each(lst, h, m), f(x + tab, 128, 128 * h, n), f("dd" + s, n // b, 0, n), x == "WT", x == "eq")
             for h in range(m) for x in ("WT", "eq")])
        offs(tab, lst, a, n, float(2048 + PAD))

    def scatter(tab, of, data, a, n, e="v"):
        b = block(of, a)
        for s in range((a + n) // b - 1, a // b - 1, -1):
            out = ("@", f(tab), f("of" + of, b // 16, 2 * s))
            if e == "s":
                act(out, f(data, b, b * s), AF.Silu)
            else:
                cp(out, f(data, b, b * s))

    def step(s, v):
        L, z, nx = "L%d" % v, "z%d" % v, "%d" % (v + 1)
        last = v == VIS - 1
        dst = T.cores[(rank + 1 + v % (ranks - 1)) % ranks]
        k, c = s[:2], int(s[2:] or 0)
        a = 128 * c
        FW = f("F32" if v and ENG["fs"] == "s" else "Fw", W, PAD)

        def ln(name, b=0):
            return f(name, 128, a + b)

        def pl(name):
            return ps(name, a, 128)
        if k == "cp":
            dma("y", T.X2[:, PAD:PAD + W], T.X[:, PAD:PAD + W], [XW], [f("X2", W, PAD)], False, 7.0)
            for d in range(2):
                if ENG["fs"] == "s":
                    dma("g", T.Fw[d:128:16, PAD:PAD + W], T.F32[d:128:16, PAD:PAD + W], [f("F32")], [f("Fw")], d == 1, 3.0)
            for d in range(2):
                for a in (PAD, PAD + W // 2):
                    dma("g", T.Ff[0:128:16, a:a + W // 2], T.Fw[d:128:16, a:a + W // 2], [f("Fw"), f("Ff", W // 2, a)], [f("Ff", W // 2, a)], False, 3.0, True)
        elif k == "fg":
            for b, n in cuts(s):
                copy(ENG["fg"][c], ent("FG", c, b, n), ("@", FW, f("in%d" % v, n, CL * c + b + 128 * (c // 2)) if v and ONE else f(L, n, CL * c + b)))
        elif k == "zc":
            if v and ONE:
                cp(ln(z), f("in%d" % v, 128, 2 * a + 128))
        elif k == "fh":
            for b, n in cuts(s):
                copy(ENG["fh"][c], ent("FH", c, b, n), ("@", FW, f("Bb", n, CL * c + b)))
        elif k == "zz":
            for i in range(LV):
                e = ENG["zz" if v else "z0"][c]
                copy(e[i % len(e)], st("z16", LV * a + i, LV * (a + 128)), ln(z))
            if v == 2 and c == 0:
                DBG["tag"] = (v, "k5")
                for b in range(0, PAD + W, 1032):
                    iota(f("Ff", 1032, b), [[0, 1032]], 0, -int(up[1]), [f("z16", CE)])
        elif k == "ce":
            b, n = (24, 8) if c else (0, 24)
            wrap(ps("cu", a, 8, n - 8), "SKc", z, a, 128)
            if c == 0:
                wrap(ps("cu", a, 16), "SKu", z, 0, K)
            ts(f("i1", n, b), ps("cu", a, n), 255.0, A.add)
            ts(f("i2", n, b), f("i1", n, b), 1023, A.bitwise_and)
            cp(f("bl", 8, 8 * c), f("i2", 8, 16 + 8 * c))
            ts(ln("Bb"), ("@", f("Bt", C, PAD), f("bl", 8, 8 * c)), 0.25 - lift, A.add)
            if c == 0:
                ts(f("bu"), f("i2"), 32.0, A.add)
                mms([(each(ps("ub", 0, K), r), sk(r, "SEL"), f("bu", 16), True, True) for r in range(LV)])
        elif k == "cb":
            keys = f("bu", 16, 16)
            dif, lst = ps("difB", 128, K), ps("lstB", 128, 16)
            mms([(each(dif, r), sk(r, "DF"), keys, True, True) for r in range(LV)])
            act(f("sgb"), dif, AF.Sign, 0.25)
            mms([(lst, f("I"), keys, True, False)] + [(lst, sk(r, "LOST"), st("sgb", r, K), False, r == LV - 1) for r in range(LV)])
            offs("B", lst, 0, K, float(PAD - 32))
        elif k == "xl":
            for b, n in cuts(s):
                turn("FL", ["FG"], c, b, n)
                ts(f("FLu", n, CL * c + b), ps("FL", CL * c + b, n), 2048.0, A.add)
            for b, n in cuts(s if s in FINE else s + "c"):
                tt(ent("D", c, b, n), ("@", XW, f("FLu", n, CL * c + b)), ent("z16", c, b, n), A.subtract)
        elif k == "fl":
            act(ln("FLf"), pl("FL"), AF.Identity, 2048.0)
            ts(ln("FLc"), ln("FLu"), -2048.0, A.add)
        elif k == "yy":
            tt(ln("y1"), ps("ub", 0, 128, a), ln("FLf"), A.mult)
            if ENG["y2"][c] == "s":
                act(ln("y2"), ln("y1"), AF.Identity, f("c613"))
            else:
                ts(ln("y2"), ln("y1"), f("c613"), A.add)
        elif k == "da":
            for b, n in cuts(s):
                turn("d", sizes(ENG["da"][c], "D", "DA", c, b, n), c, b, n)
        elif k == "xg":
            for b, n in cuts(s):
                turn("G", ["FH"], c, b, n)
                ts(f("Gu", n, CL * c + b), ps("G", CL * c + b, n), 2048.0, A.add)
            for b, n in cuts(s if s in FINE else s + "c"):
                tt(ent("E", c, b, n), ("@", XW, f("Gu", n, CL * c + b)), ent("z16", c, b, n), A.subtract)
        elif k == "hl":
            tt(ln("hiC"), pl("G"), ln("FLc"), A.max)
            tt(ln("loC"), pl("G"), ln("FLc"), A.min)
            mms([(pl("dl"), f("I"), ln("hiC"), True, False), (pl("dl"), f("In"), ln("loC"), False, True)])
            act(ln("nq"), pl("dl"), AF.Sign, -0.5)
        elif k == "fs":
            act(ln("fs"), pl("d"), AF.Sign, f("thr"))
        elif k == "nw":
            mms([(pl("M"), f("I32"), ln("FLc"), True, False), (pl("M"), f("Cc"), ln("ones"), False, False), (pl("M"), f("C1"), ln("fs"), False, True)])
            tt(ln("rr"), pl("M"), ln("y2"), A.min)
            ts(ln("new"), ln("rr"), 5, A.arith_shift_right, 4095, A.bitwise_and)
            ts(ln("nC"), ln("new"), -2048.0, A.add)
            if last:
                ts(ln("ylo"), ln("nC"), 2048.0, A.add)
                dma("y", T.yl[:, a:a + 128], T.ylo[:, a:a + 128], [ln("ylo")], [])
            else:
                ts(f("go" + nx, 128, 2 * a) if ONE else ln("Ls" + nx), ln("nC"), 2048.0, A.add)
        elif k == "sn":
            if ONE:
                if not last and c < 2:
                    send([f("go" + nx, K, K * (1 - c))], [f("in" + nx, K, K * (1 - c))], topo, core, dst, "%d_%s" % (c, nx))
            elif not last and c < len(SENDS):
                send([f(x + "s" + nx, n, b) for x, b, n in SENDS[c]], [f(x + nx, n, b) for x, b, n in SENDS[c]], topo, core, dst, "%d_%s" % (c, nx))
        elif k == "cw":
            mms([(pl("Pw"), f("I"), ln("nC"), True, False), (pl("Pw"), f("C2f"), ln("fs"), False, True)])
            ts(ln("Vw"), pl("Pw"), f("bW"), A.add, NULL, A.max)
            contest("X", ln("Vw"), a, 128)
        elif k == "vq":
            mms([(pl("Q"), f("I"), ln(z), True, False), (pl("Q"), f("Ih"), st("D", LV * a + 15, LV * (a + 128)), False, False),
                 (pl("Q"), f("cV"), ln("ones"), False, False), (pl("Q"), f("c256"), ln("fs"), False, True)])
            tt(ln("vq"), pl("Q"), ln(z), A.max)
            ts(ln("val"), ln("vq"), 255, A.bitwise_and)
        elif k == "bs":
            if ENG["nf"] == "s":
                mm(pl("FL"), f("I"), ln("nC"))
                times(ln("newf"), pl("FL"), 1.0, 2048 + lift)
            elif lift:
                ts(ln("newf"), ln("new"), lift, A.add)
            scatter("Bt", "B", "newf" if lift else "new", a, 128, ENG["bs"])
            if last and c == 0:
                if lift:
                    if ENG["yb"] == "s":
                        times(f("ybr"), f("Bt", C, PAD), 1.0, ROUND - lift)
                        times(f("ybo"), f("ybr"), 1.0, -ROUND)
                    else:
                        ts(f("ybo"), f("Bt", C, PAD), ROUND - lift, A.add, -ROUND, A.add)
                    dma("y", T.yb[:, :], T.ybo[:, :], [f("ybo")], [], False, 4.5)
                else:
                    dma("y", T.yb[:, :], T.Bt[:, PAD:PAD + C], [f("Bt")], [], False, 4.5)
        elif k == "xs":
            scatter("X2" if last else "X", "X", "val", a, 128)
            if last and c == 0:
                dma("s", T.yx[:, :], T.X2[:, PAD:PAD + W], [f("X2")], [], False, XOUT)
        elif k == "ea":
            for b, n in cuts(s):
                turn("e", sizes(ENG["ea"][c], "E", "EA", c, b, n), c, b, n, False)
                mm(ps("e", CL * c + b, n), f("Iq"), f("nq", n, CL * c + b), False, True)
        elif k == "gs":
            act(f("gs", PARTS[c][1], PARTS[c][0]), ps("e", *PARTS[c]), AF.Sign, f("Tp"), -1.0)
        elif k == "mg":
            merge(c, PARTS[c][0], PARTS[c][1], last)
        elif k == "zp":
            point(c, PARTS[c][0], PARTS[c][1], z, nx, last, dst)
        elif k == "aa":
            mms([(ps("aa", 128, 1), f("sgc", 128, 128 * p, n), f("ones", 1, 0, n), p == 0, p == len(PARTS) - 1) for p, (a, n) in enumerate(PARTS)])
            ts(f("a1"), ps("aa", 128, 1), 0.5, A.mult, K / 2.0, A.add)
            ts(f("a2"), f("a1"), 15, A.bitwise_and)
            tt(f("thr"), f("Tn"), f("a2"), A.subtract)

    def merge(p, a, n, last):
        def ln(name, b=0):
            return f(name, n, a + b)
        hi, lo = ps("Ph", a, n), ps("Pl", a, n)
        mms([(hi, f("I"), ln("hiC"), True, False), (hi, f("C2B"), ln("gs"), False, True)])
        mms([(lo, f("I"), ln("loC"), True, False), (lo, f("C2B"), ln("gs"), False, True)])
        ts(ln("Vh"), hi, f("bH"), A.add, NULL, A.max)

        def back():
            mm(hi, f("t2"), ln("gs"), True, False)
            mm(hi, f("C2B"), ln("fs"), False, True)
            act(ln("qb"), hi, AF.Relu, f("bQ"))
            return ln("qb")
        contest("F", ln("Vh"), a, n, back)
        ts(ln("Vl"), lo, f("bH"), A.add, NULL, A.max)
        mm(lo, sk(0), ln("Vl"))
        if last:
            act(ln("lof"), lo, AF.Identity, 2048 - 15 * NULL)
            scatter("Ff", "F", "lof", a, n)
            if a == 0:
                dma("y", T.yf[:, :], T.Ff[0:128:16, PAD:PAD + W], [f("Ff")], [])
        else:
            act(ln("hm"), lo, AF.Identity, f("bhm"))
            mms([(lo, sk(1), ln("Vl"), True, False), (lo, f("HM"), ln("hm"), False, True)])
            act(ln("lod"), lo, AF.Identity, f("blo"))
            scatter("F32" if ENG["fs"] == "s" else "Fw", "F", "lod", a, n, ENG["fs"])
            DBG["tag"] = (DBG["tag"][0], "aa")
            key = ps("keyF", a, 128, 0, n)
            mms([(key, ln("Vh"), f("cS", 128), True, False), (key, ln("qb"), f("bk16"), False, True)])
            act(f("sgc", 128, 128 * p, n), key, AF.Sign, 3000.0 - 15 * NULL)

    def point(p, a, n, z, nx, last, dst):
        def ln(name, b=0):
            return f(name, n, a + b)
        zs, s0, ns = "zs" + nx, a // 16, n // 16
        ix, pz = ps("ix", a, ns, s0 % 8), ps("Pz", a, n)
        mm(ps("np", a, n), f("C3"), ln("gs"))
        act(ln("npb"), ps("np", a, n), AF.Relu, f("bN"), f("wN"))
        if ENG["ix"][p] == "t":
            mms([(ix, f("I"), f("J", ns, s0), True, False)] + [(ix, sk(r), st("npb", a + r, a + n), False, r == LV - 1) for r in range(LV)])
        else:
            mt = ps("np", a, 128, 0, n)
            mm(mt, ln("npb"), f("cS", 128))
            tt(f("WTz", 128, 0, n), mt, f("mR16", 128, 0, n), A.mult)
            mms([(ix, f("I"), f("J", ns, s0), True, False), (ix, f("WTz", 128, 0, n), f("dd16", ns, 0, n), False, True)])
        ts(f("idx", ns, s0), ix, float(ES * (n // CL) - 1), A.min)
        copy(ENG["eg"], ln("Eg"), ("@", f("E", ES * (n // CL), ES * (a // CL)), f("idx", ns, s0)))
        mms([(pz, f("Iz"), ln(z), True, False), (pz, f("Izh"), ln("Eg"), False, True)])
        ts(f("go" + nx, n, 2 * a + 128) if ONE and not last else ln(zs), pz, ROUND, A.add, -ROUND, A.add)
        if last:
            dma("s", T.yz[:, a:a + n], T[zs][:, a:a + n], [ln(zs)], [])

    for v in range(VIS):
        if v > 0:
            src = T.cores[(rank - 1 - (v - 1) % (ranks - 1)) % ranks]
            e = len(topo.engines(src, core))
            for c, l in enumerate(SENDS):
                arrive([f("in%d" % v, K, K * (1 - c))] if ONE else [f("%s%d" % (x, v), n, b) for x, b, n in l], "%d_%d" % (c, v), e)
        for s in (ORDER_LAST if v == VIS - 1 else ORDER_NEXT).split():
            DBG["tag"] = (v, s)
            step(s, v)
    issue()
